import numpy as np
import ml_dtypes


def mxq(x, axis, fmt="e4m3"):
    dtype, down = {"e4m3": (ml_dtypes.float8_e4m3fn, 7), "e5m2": (ml_dtypes.float8_e5m2, 14)}[fmt]
    v = np.moveaxis(np.asarray(x, np.float32).astype(ml_dtypes.bfloat16).astype(np.float64), axis, -1)
    blocks = v.reshape(v.shape[:-1] + (-1, 32))
    amax = np.abs(blocks).max(-1, keepdims=True)
    byte = np.maximum(np.where(amax > 0, np.frexp(amax)[1] - 1 + 127, 0) - down, 1)
    scale = np.exp2(byte - 127.0)
    codes = (blocks / scale).astype(np.float32).astype(dtype).astype(np.float64)
    return np.moveaxis((codes * scale).reshape(v.shape), -1, axis)


WIDE = False


def mx_kscale(k):
    if not WIDE:
        return np.ones(k)
    levels = np.array([10, -10, 5, -5, 0])
    if k % 512:
        return np.exp2(np.random.permutation(np.resize(levels, k // 32))).repeat(32)
    a = np.empty((k // 512, 16))
    for p in range(k // 512):
        a[p, :8] = np.random.permutation(np.resize(levels, 8))
        for g in range(8):
            far = levels[np.abs(levels - a[p, g]) >= 10]
            a[p, g + 8] = far[np.random.randint(len(far))]
    return np.exp2(a.ravel()).repeat(32)


def f64(x):
    return np.asarray(x).astype(np.float64)


def striped(idx):
    return np.tile(idx.reshape(-1, 16).T, (8, 1)).astype(np.uint16)


def unstriped(offs):
    return offs[:16].T.reshape(-1).astype(np.int64)


E2M1 = np.array([0.0, 0.5, 1.0, 1.5, 2.0, 3.0, 4.0, 6.0, -0.0, -0.5, -1.0, -1.5, -2.0, -3.0, -4.0, -6.0])


def pack_weight(w, fmt):
    k, n = w.shape
    w = f64(np.asarray(w, np.float32).astype(ml_dtypes.bfloat16)).reshape(k // 32, 32, n)
    amax = np.abs(w).max(1)
    if fmt == "e4m3":
        byte = np.frexp(amax)[1] - 1 + 127 - 7
    else:
        mant, ex = np.frexp(amax / 6.0)
        byte = np.where(mant > 0.5, ex, ex - 1) + 127
    byte = np.clip(np.where(amax > 0, byte, 1), 1, 254)
    scaled = (w * np.exp2(127.0 - byte)[:, None, :]).reshape(k, n).astype(np.float32)
    by_word = np.ascontiguousarray(scaled.reshape(k // 512, 128, 4, n).transpose(0, 1, 3, 2))
    if fmt == "e4m3":
        words = by_word.astype(ml_dtypes.float8_e4m3fn).view(np.uint8)
    else:
        c = by_word.astype(ml_dtypes.float4_e2m1fn).view(np.uint8) & 0xF
        words = (c[..., 0::2] | (c[..., 1::2] << 4)).reshape(k // 512, 128, 2 * n)
    return np.ascontiguousarray(words), np.ascontiguousarray(byte.astype(np.uint8).reshape(k // 512, 16, n))


def unpack_weight(words, scales, fmt):
    g, _, n = scales.shape
    words = np.ascontiguousarray(words).reshape(g, 128, n, -1)
    if fmt == "e4m3":
        vals = words.view(ml_dtypes.float8_e4m3fn).astype(np.float64)
    else:
        nib = np.empty((g, 128, n, 4), np.uint8)
        nib[..., 0::2] = words & 0xF
        nib[..., 1::2] = words >> 4
        vals = E2M1[nib]
    vals = vals * np.repeat(np.exp2(scales.astype(np.float64) - 127.0), 8, axis=1)[..., None]
    return vals.transpose(0, 1, 3, 2).reshape(g * 512, n)


def gelu(v):
    return 0.5 * v * (1.0 + np.tanh(np.sqrt(2.0 / np.pi) * (v + 0.044715 * v**3)))


def bf(x):
    return np.asarray(x, np.float32).astype(ml_dtypes.bfloat16)

def planes(Y):
    n, m = Y.shape
    b = f64(bf(Y)).reshape(n // 32, 32, m)
    amax = np.abs(b).max(1)
    byte = np.clip(np.where(amax > 0, np.frexp(amax)[1] - 1 + 127 - 7, 1), 1, 254)
    codes = (b * np.exp2(127.0 - byte)[:, None, :]).reshape(n, m).astype(np.float32).astype(ml_dtypes.float8_e4m3fn).view(np.uint8)
    words = codes.reshape(n // 512, 128, 4, m).transpose(0, 1, 3, 2)
    return np.ascontiguousarray(words), np.ascontiguousarray(byte.astype(np.uint8).reshape(n // 512, 16, m))


K, T, S, H, N = 512, 4096, 1024, 1024, 512

def setup_inputs():
    n = np.random.standard_normal
    s = mx_kscale(K)[:, None]
    u = mx_kscale(H)[:, None]
    g = np.exp(0.8 * n(N))
    tab_words, tab_scales = pack_weight(n((K, T)) * s, "e4m3")
    wc_words, wc_scales = pack_weight(0.6 * n((K, H)) / np.sqrt(K) / s, "e2m1")
    we_words, we_scales = pack_weight(n((K, H)) / np.sqrt(K) / s * u.T, "e4m3")
    return {
        "tab_words": tab_words, "tab_scales": tab_scales,
        "offs": striped(np.random.permutation(T)[:S]),
        "offs2": striped(np.random.permutation(T)[:S]),
        "offs3": striped(np.random.permutation(T)[:S]),
        "wa": (0.6 * n((K, H)) / np.sqrt(K) / s).astype(np.float32),
        "wc_words": wc_words, "wc_scales": wc_scales,
        "we_words": we_words, "we_scales": we_scales,
        "wt": (n((H, N)) / np.sqrt(H) / u * g).astype(np.float32),
        "src": (0.5 * n(N) * g).astype(np.float32),
    }

def reference(tab_words, tab_scales, offs, offs2, offs3, wa, wc_words, wc_scales, we_words, we_scales, wt, src):
    va = unpack_weight(tab_words, tab_scales, "e4m3")[:, unstriped(offs)]
    vc = unpack_weight(tab_words, tab_scales, "e4m3")[:, unstriped(offs2)]
    ve = unpack_weight(tab_words, tab_scales, "e4m3")[:, unstriped(offs3)]
    wc = unpack_weight(wc_words, wc_scales, "e2m1")
    we = unpack_weight(we_words, we_scales, "e4m3")
    a = mxq(f64(wa), 0, "e4m3").T @ va
    c = wc.T @ vc
    e = we.T @ ve
    h = (np.exp(a) - np.exp(c)) * e
    y = (mxq(f64(wt), 0, "e4m3").T @ mxq(h, 0, "e4m3")) + f64(src)[:, None]
    words, scales = planes(y)
    return y, words, scales

@@ -1,0 +1,272 @@
+from contextlib import ExitStack
+
+import concourse.mybir as mybir
+
+K, T, S, H, N = 512, 4096, 1024, 1024, 512
+FLOPS = 2 * (3 * K * H * S + H * N * S)
+
+F32 = mybir.dt.float32
+BF16 = mybir.dt.bfloat16
+I32 = mybir.dt.int32
+U32 = mybir.dt.uint32
+U16 = mybir.dt.uint16
+U8 = mybir.dt.uint8
+E4M3 = mybir.dt.float8_e4m3fn_x4
+E2M1 = mybir.dt.float4_e2m1fn_x4
+ACT = mybir.ActivationFunctionType
+ALU = mybir.AluOpType
+
+P = 128
+PACK = 4
+JC = 128
+CHUNKS = S // JC
+HALF = S // 2
+SLICES = H // P
+PASSES = H // (P * PACK)
+SUB_ON_GPSIMD = tuple(range(16))
+WT_CAST = "ss"
+YBF = "vvvvvvvv"
+STORE_GROUPS = ((0, 2), (2, 2), (4, 2), (6, 1), (7, 1))
+
+
+def tile_list_electrode_kinetics_transport_kernel(
+    tc, tab_words, tab_scales, offs, offs2, offs3, wa, wc_words, wc_scales, we_words, we_scales, wt, src,
+    out_0, out_1, out_2,
+):
+    nc = tc.nc
+    with ExitStack() as ctx:
+        keep = ctx.enter_context(tc.tile_pool(name="keep", bufs=1))
+        ring = ctx.enter_context(tc.tile_pool(name="ring", bufs=1))
+        psum = ctx.enter_context(tc.psum_pool(name="psum", bufs=2))
+
+        def held(name, shape, dtype):
+            return keep.tile(shape, dtype, name=name, align_bytes=64)
+
+        lists = {n: held("list_" + n, [P, S // 16], U16) for n in "ace"}
+        tab_w = held("tab_w", [P, T], U32)
+        tab_s = held("tab_s", [P, T], U8)
+        wc_s_raw = held("wc_s_raw", [P, H], U8)
+        we_s_raw = held("we_s_raw", [P, H], U8)
+        wc_raw = held("wc_raw", [P, H // 2], I32)
+        we_raw = held("we_raw", [P, H], I32)
+        wa_raw = [held("wa_raw%d" % u, [P, PACK, H // 2], F32) for u in range(2)]
+        wt_raw = held("wt_raw", [P, SLICES, N], F32)
+        src_sb = held("src_sb", [P, PACK], F32)
+
+        def load_scale_rows(plane, rows):
+            for quad in range(4):
+                nc.sync.dma_start(
+                    out=plane[32 * quad : 32 * quad + 4, :].bitcast(I32),
+                    in_=rows[0, 4 * quad : 4 * quad + 4, :].bitcast(I32),
+                )
+
+        for plane in (tab_s, wc_s_raw, we_s_raw):
+            nc.vector.memset(plane[:].bitcast(I32), 0)
+        for n, lst in (("a", offs), ("c", offs2), ("e", offs3)):
+            nc.sync.dma_start(lists[n][:], lst)
+        load_scale_rows(tab_s, tab_scales)
+        wa_rows = wa.rearrange("(p j) r -> p j r", j=PACK)
+        nc.scalar.dma_start(out=wa_raw[0][:], in_=wa_rows[:, :, : H // 2])
+        load_scale_rows(wc_s_raw, wc_scales)
+        nc.sync.dma_start(out=wc_raw[:], in_=wc_words[0].bitcast(I32))
+        nc.sync.dma_start(out=wa_raw[1][:], in_=wa_rows[:, :, H // 2 :])
+        nc.sync.dma_start(
+            out=tab_w[:].bitcast(I32), in_=tab_words[0].rearrange("p t i -> p (t i)").bitcast(I32)
+        )
+        nc.sync.dma_start(out=we_raw[:], in_=we_words[0].rearrange("p y i -> p (y i)").bitcast(I32))
+        load_scale_rows(we_s_raw, we_scales)
+        nc.sync.dma_start(out=src_sb[:], in_=src.rearrange("(p t) -> p t", t=PACK))
+        wt_rows = wt.rearrange("(q s i) n -> i q s n", s=SLICES, i=8)
+        for i in (0, 4, 1, 5, 2, 6, 3, 7):
+            nc.sync.dma_start(out=wt_raw[i:P:8, :, :], in_=wt_rows[i])
+
+        v_s = {n: held("v_s_" + n, [P, S], U8) for n in "ace"}
+        for n in "ace":
+            nc.vector.tensor_copy(v_s[n][:], tab_s[:].indirect(lists[n][:]))
+
+        wa_bf = held("wa_bf", [P, PACK * H], BF16)
+        wa_dst = wa_bf[:].rearrange("p (s u q h i j) -> p u h q s j i", s=SLICES, u=2, q=8, h=2, i=4, j=PACK)
+        for u in range(2):
+            wa_src = wa_raw[u][:].rearrange("p j (q s h i) -> p h q s j i", s=SLICES, h=2, i=4)
+            for h in range(2):
+                nc.scalar.copy(out=wa_dst[:, u, h], in_=wa_src[:, h])
+        wa_w = held("wa_w", [P, H], U32)
+        wa_s = held("wa_s", [P, H], U8)
+        for g in range(PASSES):
+            nc.vector.quantize_mx(
+                out=wa_w[:, 512 * g : 512 * (g + 1)].bitcast(E4M3),
+                scales=wa_s[:, 512 * g : 512 * (g + 1)],
+                in_=wa_bf[:, 2048 * g : 2048 * (g + 1)],
+            )
+
+        v_w = {(n, u): held("v_w_%s%d" % (n, u), [P, HALF], U32) for n in "ace" for u in range(2)}
+
+        def gather_words(n, u):
+            cols = HALF // 16
+            nc.vector.tensor_copy(v_w[n, u][:], tab_w[:].indirect(lists[n][:, cols * u : cols * (u + 1)]))
+
+        def deal(name, raw):
+            width = raw.shape[1]
+            dealt = held(name, [P, width], I32)
+            nc.vector.tensor_copy(
+                out=dealt[:].rearrange("p (s q w) -> p s q w", s=SLICES, q=16),
+                in_=raw.rearrange("p (q s w) -> p s q w", s=SLICES, q=16),
+            )
+            return dealt
+
+        wc_w = deal("wc_w", wc_raw[:])
+        wc_s = deal("wc_s", wc_s_raw[:].bitcast(I32))
+        gather_words("a", 0)
+        gather_words("c", 0)
+        gather_words("e", 0)
+        we_w = deal("we_w", we_raw[:])
+        we_s = deal("we_s", we_s_raw[:].bitcast(I32))
+
+        def weights(n, s):
+            cols = slice(P * s, P * (s + 1))
+            if n == "a":
+                return wa_w[:, cols].bitcast(E4M3), wa_s[:, cols]
+            if n == "c":
+                return (
+                    wc_w[:].bitcast(U8)[:, 2 * P * s : 2 * P * (s + 1)].bitcast(E2M1),
+                    wc_s[:].bitcast(U8)[:, cols],
+                )
+            return we_w[:, cols].bitcast(E4M3), we_s[:].bitcast(U8)[:, cols]
+
+        def first_product(n, jc, g):
+            bank = psum.tile([P, PACK, JC], F32, name="bank_" + n)
+            u, j0 = divmod(jc * JC, HALF)
+            for t in range(PACK):
+                codes, scales = weights(n, PACK * g + t)
+                nc.tensor.matmul_mx(
+                    out=bank[:, t, :], lhsT=codes, lhsT_scale=scales,
+                    rhs=v_w[n, u][:, j0 : j0 + JC].bitcast(E4M3),
+                    rhs_scale=v_s[n][:, jc * JC : (jc + 1) * JC],
+                    start=True, stop=True,
+                )
+            return bank[:].rearrange("p t j -> p j t")
+
+        diffs, h_bf, h_q, y_sb, y_bf = {}, {}, {}, {}, {}
+
+        def exponentials(unit):
+            jc, g = divmod(unit, PASSES)
+            ex = {}
+            for n in "ac":
+                ex[n] = ring.tile([P, JC * PACK], F32, name="exp_" + n, bufs=4)
+                nc.scalar.activation(
+                    out=ex[n][:].rearrange("p (j t) -> p j t", t=PACK), in_=first_product(n, jc, g), func=ACT.Exp
+                )
+            diffs[unit] = ring.tile([P, JC * PACK], F32, name="diff", bufs=8)
+            eng = nc.gpsimd if unit in SUB_ON_GPSIMD else nc.vector
+            eng.tensor_tensor(out=diffs[unit][:], in0=ex["a"][:], in1=ex["c"][:], op=ALU.subtract)
+
+        def rates(unit):
+            jc, g = divmod(unit, PASSES)
+            if g == 0:
+                h_bf[jc] = ring.tile([P, PASSES * JC * PACK], BF16, name="h_bf", bufs=3, align_bytes=64)
+            nc.vector.tensor_tensor(
+                out=h_bf[jc][:, JC * PACK * g : JC * PACK * (g + 1)].rearrange("p (j t) -> p j t", t=PACK),
+                in0=diffs[unit][:].rearrange("p (j t) -> p j t", t=PACK),
+                in1=first_product("e", jc, g),
+                op=ALU.mult,
+            )
+
+        def quantise_rates(jc):
+            words = ring.tile([P, PASSES * JC], U32, name="h_w", bufs=4, align_bytes=64)
+            scales = ring.tile([P, PASSES * JC], U8, name="h_s", bufs=4, align_bytes=64)
+            nc.vector.quantize_mx(out=words[:].bitcast(E4M3), scales=scales[:], in_=h_bf[jc][:])
+            h_q[jc] = (words, scales)
+
+        wt_bf = held("wt_bf", [P, SLICES * N], BF16)
+        wt_w = held("wt_w", [P, PASSES * N], U32)
+        wt_s = held("wt_s", [P, PASSES * N], U8)
+
+        def prepare_wt(g):
+            dst = wt_bf[:, 2048 * g : 2048 * (g + 1)].rearrange("p (t m j) -> p m j t", t=PACK, j=PACK)
+            source = wt_raw[:, PACK * g : PACK * (g + 1), :].rearrange("p j (m t) -> p m j t", t=PACK)
+            if WT_CAST[g] == "v":
+                nc.vector.tensor_copy(out=dst, in_=source)
+            else:
+                nc.scalar.copy(out=dst, in_=source)
+
+        def quantise_wt(g):
+            nc.vector.quantize_mx(
+                out=wt_w[:, N * g : N * (g + 1)].bitcast(E4M3),
+                scales=wt_s[:, N * g : N * (g + 1)],
+                in_=wt_bf[:, 2048 * g : 2048 * (g + 1)],
+            )
+
+        y_s = held("y_s", [P, S], U8)
+        group_of = {}
+        for first, count in STORE_GROUPS:
+            y_tile = held("y_sb%d" % first, [P, PACK, count * JC], F32)
+            w_tile = held("y_w%d" % first, [P, count * JC], U32)
+            for jc in range(first, first + count):
+                group_of[jc] = (first, count, y_tile, w_tile)
+        out_rows = out_0.rearrange("(p t) j -> p t j", t=PACK)
+        out_words = out_1[0].rearrange("p m t -> p (m t)").bitcast(I32)
+
+        def transport(jc):
+            first, count, y_tile, w_tile = group_of[jc]
+            words, scales = h_q[jc]
+            bank = psum.tile([P, PACK, JC], F32, name="bank_y")
+            for t in range(PACK):
+                for g in range(PASSES):
+                    cols = slice(N * g + P * t, N * g + P * (t + 1))
+                    nc.tensor.matmul_mx(
+                        out=bank[:, t, :], lhsT=wt_w[:, cols].bitcast(E4M3), lhsT_scale=wt_s[:, cols],
+                        rhs=words[:, JC * g : JC * (g + 1)].bitcast(E4M3),
+                        rhs_scale=scales[:, JC * g : JC * (g + 1)],
+                        start=(g == 0), stop=(g == PASSES - 1),
+                    )
+            j0 = (jc - first) * JC
+            for t in range(PACK):
+                nc.scalar.activation(
+                    out=y_tile[:, t, j0 : j0 + JC], in_=bank[:, t, :], func=ACT.Identity, bias=src_sb[:, t : t + 1]
+                )
+            if jc == first + count - 1:
+                nc.sync.dma_start(out=out_rows[:, :, first * JC : (first + count) * JC], in_=y_tile[:])
+
+        def round_y(jc):
+            first, count, y_tile, w_tile = group_of[jc]
+            j0 = (jc - first) * JC
+            y_bf[jc] = ring.tile([P, JC * PACK], BF16, name="y_bf", bufs=3, align_bytes=64)
+            dst = y_bf[jc][:].rearrange("p (c i t) -> p c t i", i=4, t=PACK)
+            source = y_tile[:, :, j0 : j0 + JC].rearrange("p t (c i) -> p c t i", i=4)
+            if YBF[jc] == "v":
+                nc.vector.tensor_copy(out=dst, in_=source)
+            else:
+                nc.scalar.copy(out=dst, in_=source)
+
+        def quantise_y(jc):
+            first, count, y_tile, w_tile = group_of[jc]
+            j0 = (jc - first) * JC
+            nc.vector.quantize_mx(
+                out=w_tile[:, j0 : j0 + JC].bitcast(E4M3), scales=y_s[:, jc * JC : (jc + 1) * JC], in_=y_bf[jc][:]
+            )
+            if jc == first + count - 1:
+                nc.sync.dma_start(out=out_words[:, first * JC : (first + count) * JC], in_=w_tile[:].bitcast(I32))
+
+        units = CHUNKS * PASSES
+        for step in range(units + 8):
+            if step < units:
+                exponentials(step)
+            if 0 <= step - 1 < units:
+                rates(step - 1)
+            if 1 <= step <= 3:
+                gather_words("ace"[step - 1], 1)
+            if step in (3, 4):
+                prepare_wt(step - 3)
+            if step in (4, 5):
+                quantise_wt(step - 4)
+            for lag, stage in (((3, quantise_rates), (6, transport), (7, round_y), (8, quantise_y))):
+                jc, odd = divmod(step - lag, PASSES)
+                if odd == 0 and 0 <= jc < CHUNKS:
+                    stage(jc)
+
+        for quad in range(4):
+            queue = nc.sync if quad % 2 == 0 else nc.scalar
+            queue.dma_start(
+                out=out_2[0, 4 * quad : 4 * quad + 4, :].bitcast(I32),
+                in_=y_s[32 * quad : 32 * quad + 4, :].bitcast(I32),
+            )

@@ -23,9 +23,12 @@ CHUNKS = S // JC
 HALF = S // 2
 SLICES = H // P
 PASSES = H // (P * PACK)
-SUB_ON_GPSIMD = tuple(range(16))
+SUB_ON_GPSIMD = ()
 WT_CAST = "ss"
-YBF = "vvvvvvvv"
+YBF = "ssssssvv"
+HOLD = 2
+SPLIT_SUB = (0, 7)
+GATHER_STEPS = (2, 3, 5)
 STORE_GROUPS = ((0, 2), (2, 2), (4, 2), (6, 1), (7, 1))
 
 
@@ -45,17 +48,17 @@ def tile_list_electrode_kinetics_transport_kernel(
         lists = {n: held("list_" + n, [P, S // 16], U16) for n in "ace"}
         tab_w = held("tab_w", [P, T], U32)
         tab_s = held("tab_s", [P, T], U8)
-        wc_s_raw = held("wc_s_raw", [P, H], U8)
+        wc_s_raw = ring.tile([P, H], U8, name="wc_s_raw", tag="then_c0", align_bytes=64)
         we_s_raw = held("we_s_raw", [P, H], U8)
         wc_raw = held("wc_raw", [P, H // 2], I32)
-        we_raw = held("we_raw", [P, H], I32)
+        we_raw = ring.tile([P, H], I32, name="we_raw", tag="then_e0", align_bytes=64)
         wa_raw = [held("wa_raw%d" % u, [P, PACK, H // 2], F32) for u in range(2)]
-        wt_raw = held("wt_raw", [P, SLICES, N], F32)
+        wt_raw = ring.tile([P, SLICES * N], F32, name="wt_raw", tag="then_exp")
         src_sb = held("src_sb", [P, PACK], F32)
 
-        def load_scale_rows(plane, rows):
+        def load_scale_rows(queue, plane, rows):
             for quad in range(4):
-                nc.sync.dma_start(
+                queue.dma_start(
                     out=plane[32 * quad : 32 * quad + 4, :].bitcast(I32),
                     in_=rows[0, 4 * quad : 4 * quad + 4, :].bitcast(I32),
                 )
@@ -64,32 +67,38 @@ def tile_list_electrode_kinetics_transport_kernel(
             nc.vector.memset(plane[:].bitcast(I32), 0)
         for n, lst in (("a", offs), ("c", offs2), ("e", offs3)):
             nc.sync.dma_start(lists[n][:], lst)
-        load_scale_rows(tab_s, tab_scales)
+        load_scale_rows(nc.scalar, tab_s, tab_scales)
         wa_rows = wa.rearrange("(p j) r -> p j r", j=PACK)
-        nc.scalar.dma_start(out=wa_raw[0][:], in_=wa_rows[:, :, : H // 2])
-        load_scale_rows(wc_s_raw, wc_scales)
+        nc.sync.dma_start(out=wa_raw[0][:], in_=wa_rows[:, :, :512])
+        load_scale_rows(nc.sync, wc_s_raw, wc_scales)
         nc.sync.dma_start(out=wc_raw[:], in_=wc_words[0].bitcast(I32))
-        nc.sync.dma_start(out=wa_raw[1][:], in_=wa_rows[:, :, H // 2 :])
+        nc.sync.dma_start(out=wa_raw[1][:], in_=wa_rows[:, :, 512:])
         nc.sync.dma_start(
             out=tab_w[:].bitcast(I32), in_=tab_words[0].rearrange("p t i -> p (t i)").bitcast(I32)
         )
+        load_scale_rows(nc.sync, we_s_raw, we_scales)
         nc.sync.dma_start(out=we_raw[:], in_=we_words[0].rearrange("p y i -> p (y i)").bitcast(I32))
-        load_scale_rows(we_s_raw, we_scales)
         nc.sync.dma_start(out=src_sb[:], in_=src.rearrange("(p t) -> p t", t=PACK))
-        wt_rows = wt.rearrange("(q s i) n -> i q s n", s=SLICES, i=8)
-        for i in (0, 4, 1, 5, 2, 6, 3, 7):
-            nc.sync.dma_start(out=wt_raw[i:P:8, :, :], in_=wt_rows[i])
+        wt_rows = wt.rearrange("(g k t i) n -> g i k t n", g=PASSES, t=PACK, i=4)
+        for g in range(PASSES):
+            for i in range(4):
+                nc.sync.dma_start(out=wt_raw[i:P:4, 2048 * g : 2048 * (g + 1)].rearrange("k (t n) -> k t n", t=PACK), in_=wt_rows[g, i])
 
         v_s = {n: held("v_s_" + n, [P, S], U8) for n in "ace"}
-        for n in "ace":
+
+        def gather_scales(n):
             nc.vector.tensor_copy(v_s[n][:], tab_s[:].indirect(lists[n][:]))
 
+        gather_scales("a")
+        gather_scales("c")
+        gather_scales("e")
+
         wa_bf = held("wa_bf", [P, PACK * H], BF16)
-        wa_dst = wa_bf[:].rearrange("p (s u q h i j) -> p u h q s j i", s=SLICES, u=2, q=8, h=2, i=4, j=PACK)
-        for u in range(2):
-            wa_src = wa_raw[u][:].rearrange("p j (q s h i) -> p h q s j i", s=SLICES, h=2, i=4)
-            for h in range(2):
-                nc.scalar.copy(out=wa_dst[:, u, h], in_=wa_src[:, h])
+        for g in range(PASSES):
+            nc.scalar.copy(
+                out=wa_bf[:, 2048 * g : 2048 * (g + 1)].rearrange("p (t k i j) -> p t k j i", t=PACK, i=4, j=PACK),
+                in_=wa_raw[g][:].rearrange("p j (k t i) -> p t k j i", t=PACK, i=4),
+            )
         wa_w = held("wa_w", [P, H], U32)
         wa_s = held("wa_s", [P, H], U8)
         for g in range(PASSES):
@@ -99,18 +108,19 @@ def tile_list_electrode_kinetics_transport_kernel(
                 in_=wa_bf[:, 2048 * g : 2048 * (g + 1)],
             )
 
-        v_w = {(n, u): held("v_w_%s%d" % (n, u), [P, HALF], U32) for n in "ace" for u in range(2)}
+        v_w = {}
 
         def gather_words(n, u):
             cols = HALF // 16
+            v_w[n, u] = ring.tile([P, HALF], U32, name="v_w_%s%d" % (n, u), tag="then_%s%d" % (n, u), align_bytes=64)
             nc.vector.tensor_copy(v_w[n, u][:], tab_w[:].indirect(lists[n][:, cols * u : cols * (u + 1)]))
 
         def deal(name, raw):
             width = raw.shape[1]
             dealt = held(name, [P, width], I32)
             nc.vector.tensor_copy(
-                out=dealt[:].rearrange("p (s q w) -> p s q w", s=SLICES, q=16),
-                in_=raw.rearrange("p (q s w) -> p s q w", s=SLICES, q=16),
+                out=dealt[:].rearrange("p (g t k w) -> p g t k w", g=PASSES, t=PACK, k=32),
+                in_=raw.rearrange("p (g k t w) -> p g t k w", g=PASSES, t=PACK, k=32),
             )
             return dealt
 
@@ -118,9 +128,9 @@ def tile_list_electrode_kinetics_transport_kernel(
         wc_s = deal("wc_s", wc_s_raw[:].bitcast(I32))
         gather_words("a", 0)
         gather_words("c", 0)
-        gather_words("e", 0)
-        we_w = deal("we_w", we_raw[:])
         we_s = deal("we_s", we_s_raw[:].bitcast(I32))
+        we_w = deal("we_w", we_raw[:])
+        gather_words("e", 0)
 
         def weights(n, s):
             cols = slice(P * s, P * (s + 1))
@@ -146,36 +156,51 @@ def tile_list_electrode_kinetics_transport_kernel(
                 )
             return bank[:].rearrange("p t j -> p j t")
 
-        diffs, h_bf, h_q, y_sb, y_bf = {}, {}, {}, {}, {}
+        late, ex, diffs, h_bf, h_q, y_sb, y_bf = {}, {}, {}, {}, {}, {}, {}
+        group_of = {jc: (first, count) for first, count in STORE_GROUPS for jc in range(first, first + count)}
+        UNIT = JC * PACK
 
         def exponentials(unit):
             jc, g = divmod(unit, PASSES)
-            ex = {}
+            if unit == PASSES * HOLD:
+                both = ring.tile([P, SLICES * N], F32, name="late", tag="then_exp")
+                late["a"], late["c"] = both[:, :2048], both[:, 2048:]
             for n in "ac":
-                ex[n] = ring.tile([P, JC * PACK], F32, name="exp_" + n, bufs=4)
+                if g == 0 and jc >= HOLD:
+                    ex[n] = late[n][:, PASSES * UNIT * (jc % 2) : PASSES * UNIT * (jc % 2 + 1)]
+                elif g == 0:
+                    tag = {"a0": "then_a1", "c0": "then_c1", "a1": "then_e1", "c1": "early_c1"}[n + str(jc)]
+                    ex[n] = ring.tile([P, PASSES * UNIT], F32, name="exp_" + n, tag=tag, align_bytes=64)[:]
                 nc.scalar.activation(
-                    out=ex[n][:].rearrange("p (j t) -> p j t", t=PACK), in_=first_product(n, jc, g), func=ACT.Exp
+                    out=ex[n][:, UNIT * g : UNIT * (g + 1)].rearrange("p (j t) -> p j t", t=PACK),
+                    in_=first_product(n, jc, g),
+                    func=ACT.Exp,
                 )
-            diffs[unit] = ring.tile([P, JC * PACK], F32, name="diff", bufs=8)
-            eng = nc.gpsimd if unit in SUB_ON_GPSIMD else nc.vector
-            eng.tensor_tensor(out=diffs[unit][:], in0=ex["a"][:], in1=ex["c"][:], op=ALU.subtract)
+            if g == 0:
+                diffs[jc] = ring.tile([P, PASSES * UNIT], F32, name="diff", bufs=3)
+            if jc in SPLIT_SUB or g == PASSES - 1:
+                cols = slice(UNIT * g, UNIT * (g + 1)) if jc in SPLIT_SUB else slice(0, PASSES * UNIT)
+                eng = nc.gpsimd if unit in SUB_ON_GPSIMD else nc.vector
+                eng.tensor_tensor(out=diffs[jc][:, cols], in0=ex["a"][:, cols], in1=ex["c"][:, cols], op=ALU.subtract)
 
         def rates(unit):
             jc, g = divmod(unit, PASSES)
-            if g == 0:
-                h_bf[jc] = ring.tile([P, PASSES * JC * PACK], BF16, name="h_bf", bufs=3, align_bytes=64)
+            first, count = group_of[jc]
+            if g == 0 and jc == first:
+                h_bf[first] = ring.tile([P, PASSES * count * UNIT], BF16, name="h_bf", bufs=2, align_bytes=64)
+            at = UNIT * (g * count + jc - first)
             nc.vector.tensor_tensor(
-                out=h_bf[jc][:, JC * PACK * g : JC * PACK * (g + 1)].rearrange("p (j t) -> p j t", t=PACK),
-                in0=diffs[unit][:].rearrange("p (j t) -> p j t", t=PACK),
+                out=h_bf[first][:, at : at + UNIT].rearrange("p (j t) -> p j t", t=PACK),
+                in0=diffs[jc][:, UNIT * g : UNIT * (g + 1)].rearrange("p (j t) -> p j t", t=PACK),
                 in1=first_product("e", jc, g),
                 op=ALU.mult,
             )
 
-        def quantise_rates(jc):
-            words = ring.tile([P, PASSES * JC], U32, name="h_w", bufs=4, align_bytes=64)
-            scales = ring.tile([P, PASSES * JC], U8, name="h_s", bufs=4, align_bytes=64)
-            nc.vector.quantize_mx(out=words[:].bitcast(E4M3), scales=scales[:], in_=h_bf[jc][:])
-            h_q[jc] = (words, scales)
+        def quantise_rates(first, count):
+            words = ring.tile([P, PASSES * count * JC], U32, name="h_w", bufs=2, align_bytes=64)
+            scales = ring.tile([P, PASSES * count * JC], U8, name="h_s", bufs=2, align_bytes=64)
+            nc.vector.quantize_mx(out=words[:].bitcast(E4M3), scales=scales[:], in_=h_bf[first][:])
+            h_q[first] = (words, scales)
 
         wt_bf = held("wt_bf", [P, SLICES * N], BF16)
         wt_w = held("wt_w", [P, PASSES * N], U32)
@@ -183,7 +208,7 @@ def tile_list_electrode_kinetics_transport_kernel(
 
         def prepare_wt(g):
             dst = wt_bf[:, 2048 * g : 2048 * (g + 1)].rearrange("p (t m j) -> p m j t", t=PACK, j=PACK)
-            source = wt_raw[:, PACK * g : PACK * (g + 1), :].rearrange("p j (m t) -> p m j t", t=PACK)
+            source = wt_raw[:, 2048 * g : 2048 * (g + 1)].rearrange("p (j m t) -> p m j t", j=PACK, t=PACK)
             if WT_CAST[g] == "v":
                 nc.vector.tensor_copy(out=dst, in_=source)
             else:
@@ -197,72 +222,67 @@ def tile_list_electrode_kinetics_transport_kernel(
             )
 
         y_s = held("y_s", [P, S], U8)
-        group_of = {}
-        for first, count in STORE_GROUPS:
-            y_tile = held("y_sb%d" % first, [P, PACK, count * JC], F32)
-            w_tile = held("y_w%d" % first, [P, count * JC], U32)
-            for jc in range(first, first + count):
-                group_of[jc] = (first, count, y_tile, w_tile)
         out_rows = out_0.rearrange("(p t) j -> p t j", t=PACK)
         out_words = out_1[0].rearrange("p m t -> p (m t)").bitcast(I32)
 
-        def transport(jc):
-            first, count, y_tile, w_tile = group_of[jc]
-            words, scales = h_q[jc]
-            bank = psum.tile([P, PACK, JC], F32, name="bank_y")
+        def transport(first, count):
+            words, scales = h_q[first]
+            width = count * JC
+            y_sb[first] = held("y_sb%d" % first, [P, PACK, width], F32)
             for t in range(PACK):
+                at = (t * width) % 512
+                if at == 0:
+                    bank = psum.tile([P, 512], F32, name="bank_y")
                 for g in range(PASSES):
                     cols = slice(N * g + P * t, N * g + P * (t + 1))
                     nc.tensor.matmul_mx(
-                        out=bank[:, t, :], lhsT=wt_w[:, cols].bitcast(E4M3), lhsT_scale=wt_s[:, cols],
-                        rhs=words[:, JC * g : JC * (g + 1)].bitcast(E4M3),
-                        rhs_scale=scales[:, JC * g : JC * (g + 1)],
+                        out=bank[:, at : at + width], lhsT=wt_w[:, cols].bitcast(E4M3), lhsT_scale=wt_s[:, cols],
+                        rhs=words[:, width * g : width * (g + 1)].bitcast(E4M3),
+                        rhs_scale=scales[:, width * g : width * (g + 1)],
                         start=(g == 0), stop=(g == PASSES - 1),
                     )
-            j0 = (jc - first) * JC
-            for t in range(PACK):
-                nc.scalar.activation(
-                    out=y_tile[:, t, j0 : j0 + JC], in_=bank[:, t, :], func=ACT.Identity, bias=src_sb[:, t : t + 1]
-                )
-            if jc == first + count - 1:
-                nc.sync.dma_start(out=out_rows[:, :, first * JC : (first + count) * JC], in_=y_tile[:])
+                if at + width == 512:
+                    for done in range(t + 1 - 512 // width, t + 1):
+                        at = (done * width) % 512
+                        nc.scalar.activation(
+                            out=y_sb[first][:, done, :], in_=bank[:, at : at + width], func=ACT.Identity,
+                            bias=src_sb[:, done : done + 1],
+                        )
+            nc.sync.dma_start(out=out_rows[:, :, first * JC : first * JC + width], in_=y_sb[first][:])
 
-        def round_y(jc):
-            first, count, y_tile, w_tile = group_of[jc]
-            j0 = (jc - first) * JC
-            y_bf[jc] = ring.tile([P, JC * PACK], BF16, name="y_bf", bufs=3, align_bytes=64)
-            dst = y_bf[jc][:].rearrange("p (c i t) -> p c t i", i=4, t=PACK)
-            source = y_tile[:, :, j0 : j0 + JC].rearrange("p t (c i) -> p c t i", i=4)
-            if YBF[jc] == "v":
+        def round_y(first, count):
+            y_bf[first] = ring.tile([P, count * UNIT], BF16, name="y_bf", bufs=2, align_bytes=64)
+            dst = y_bf[first][:].rearrange("p (c i t) -> p c t i", i=4, t=PACK)
+            source = y_sb[first][:].rearrange("p t (c i) -> p c t i", i=4)
+            if YBF[first] == "v":
                 nc.vector.tensor_copy(out=dst, in_=source)
             else:
                 nc.scalar.copy(out=dst, in_=source)
 
-        def quantise_y(jc):
-            first, count, y_tile, w_tile = group_of[jc]
-            j0 = (jc - first) * JC
-            nc.vector.quantize_mx(
-                out=w_tile[:, j0 : j0 + JC].bitcast(E4M3), scales=y_s[:, jc * JC : (jc + 1) * JC], in_=y_bf[jc][:]
-            )
-            if jc == first + count - 1:
-                nc.sync.dma_start(out=out_words[:, first * JC : (first + count) * JC], in_=w_tile[:].bitcast(I32))
+        def quantise_y(first, count):
+            cols = slice(first * JC, (first + count) * JC)
+            y_w = held("y_w%d" % first, [P, count * JC], U32)
+            nc.vector.quantize_mx(out=y_w[:].bitcast(E4M3), scales=y_s[:, cols], in_=y_bf[first][:])
+            nc.sync.dma_start(out=out_words[:, cols], in_=y_w[:].bitcast(I32))
 
         units = CHUNKS * PASSES
         for step in range(units + 8):
             if step < units:
                 exponentials(step)
-            if 0 <= step - 1 < units:
-                rates(step - 1)
-            if 1 <= step <= 3:
-                gather_words("ace"[step - 1], 1)
-            if step in (3, 4):
-                prepare_wt(step - 3)
-            if step in (4, 5):
-                quantise_wt(step - 4)
-            for lag, stage in (((3, quantise_rates), (6, transport), (7, round_y), (8, quantise_y))):
-                jc, odd = divmod(step - lag, PASSES)
-                if odd == 0 and 0 <= jc < CHUNKS:
-                    stage(jc)
+            if 0 <= step - 2 < units:
+                rates(step - 2)
+            if step in GATHER_STEPS:
+                gather_words("ace"[GATHER_STEPS.index(step)], 1)
+            if step == PASSES * HOLD - 1:
+                for g in range(PASSES):
+                    prepare_wt(g)
+            if step == PASSES * HOLD:
+                for g in range(PASSES):
+                    quantise_wt(g)
+            for lag, stage in (((2, quantise_rates), (3, transport), (4, round_y), (5, quantise_y))):
+                for first, count in STORE_GROUPS:
+                    if step == PASSES * (first + count) + lag:
+                        stage(first, count)
 
         for quad in range(4):
             queue = nc.sync if quad % 2 == 0 else nc.scalar

@@ -29,6 +29,7 @@ YBF = "ssssssvv"
 HOLD = 2
 SPLIT_SUB = (0, 7)
 GATHER_STEPS = (2, 3, 5)
+RUN = 2
 STORE_GROUPS = ((0, 2), (2, 2), (4, 2), (6, 1), (7, 1))
 
 
@@ -154,7 +155,7 @@ def tile_list_electrode_kinetics_transport_kernel(
                     rhs_scale=v_s[n][:, jc * JC : (jc + 1) * JC],
                     start=True, stop=True,
                 )
-            return bank[:].rearrange("p t j -> p j t")
+            return bank[:].rearrange("p t j -> p (t j)")
 
         late, ex, diffs, h_bf, h_q, y_sb, y_bf = {}, {}, {}, {}, {}, {}, {}
         group_of = {jc: (first, count) for first, count in STORE_GROUPS for jc in range(first, first + count)}
@@ -169,10 +170,10 @@ def tile_list_electrode_kinetics_transport_kernel(
                 if g == 0 and jc >= HOLD:
                     ex[n] = late[n][:, PASSES * UNIT * (jc % 2) : PASSES * UNIT * (jc % 2 + 1)]
                 elif g == 0:
-                    tag = {"a0": "then_a1", "c0": "then_c1", "a1": "then_e1", "c1": "early_c1"}[n + str(jc)]
+                    tag = {"a0": "then_a1", "c0": "then_c1", "a1": "then_e1"}.get(n + str(jc), "early_" + n + str(jc))
                     ex[n] = ring.tile([P, PASSES * UNIT], F32, name="exp_" + n, tag=tag, align_bytes=64)[:]
                 nc.scalar.activation(
-                    out=ex[n][:, UNIT * g : UNIT * (g + 1)].rearrange("p (j t) -> p j t", t=PACK),
+                    out=ex[n][:, UNIT * g : UNIT * (g + 1)],
                     in_=first_product(n, jc, g),
                     func=ACT.Exp,
                 )
@@ -190,9 +191,9 @@ def tile_list_electrode_kinetics_transport_kernel(
                 h_bf[first] = ring.tile([P, PASSES * count * UNIT], BF16, name="h_bf", bufs=2, align_bytes=64)
             at = UNIT * (g * count + jc - first)
             nc.vector.tensor_tensor(
-                out=h_bf[first][:, at : at + UNIT].rearrange("p (j t) -> p j t", t=PACK),
-                in0=diffs[jc][:, UNIT * g : UNIT * (g + 1)].rearrange("p (j t) -> p j t", t=PACK),
-                in1=first_product("e", jc, g),
+                out=h_bf[first][:, at : at + UNIT].rearrange("p (c i t) -> p c t i", i=RUN, t=PACK),
+                in0=diffs[jc][:, UNIT * g : UNIT * (g + 1)].rearrange("p (t c i) -> p c t i", i=RUN, t=PACK),
+                in1=first_product("e", jc, g).rearrange("p (t c i) -> p c t i", i=RUN, t=PACK),
                 op=ALU.mult,
             )
 
@@ -201,6 +202,37 @@ def tile_list_electrode_kinetics_transport_kernel(
             scales = ring.tile([P, PASSES * count * JC], U8, name="h_s", bufs=2, align_bytes=64)
             nc.vector.quantize_mx(out=words[:].bitcast(E4M3), scales=scales[:], in_=h_bf[first][:])
             h_q[first] = (words, scales)
+
+        last_banks = []
+
+        def last_pass(g):
+            jc = CHUNKS - 1
+            words = held("h_w_last%d" % g, [P, JC], U32)
+            scales = held("h_s_last%d" % g, [P, JC], U8)
+            nc.vector.quantize_mx(
+                out=words[:].bitcast(E4M3), scales=scales[:], in_=h_bf[jc][:, UNIT * g : UNIT * (g + 1)]
+            )
+            if g == PASSES - 1:
+                y_sb[jc] = held("y_sb%d" % jc, [P, PACK, JC], F32)
+            for t in range(PACK):
+                if g == 0:
+                    last_banks.append(psum.tile([P, PACK, JC], F32, name="bank_" + "ac"[t % 2]))
+                cols = slice(N * g + P * t, N * g + P * (t + 1))
+                nc.tensor.matmul_mx(
+                    out=last_banks[t][:, 0, :], lhsT=wt_w[:, cols].bitcast(E4M3), lhsT_scale=wt_s[:, cols],
+                    rhs=words[:].bitcast(E4M3), rhs_scale=scales[:], start=(g == 0), stop=(g == PASSES - 1),
+                )
+                if g == PASSES - 1 and t % 2 == 0:
+                    nc.scalar.activation(
+                        out=y_sb[jc][:, t, :], in_=last_banks[t][:, 0, :], func=ACT.Identity, bias=src_sb[:, t : t + 1]
+                    )
+                elif g == PASSES - 1:
+                    nc.vector.tensor_scalar(
+                        out=y_sb[jc][:, t, :], in0=last_banks[t][:, 0, :], scalar1=src_sb[:, t : t + 1], scalar2=None,
+                        op0=ALU.add,
+                    )
+            if g == PASSES - 1:
+                nc.sync.dma_start(out=out_rows[:, :, jc * JC :], in_=y_sb[jc][:])
 
         wt_bf = held("wt_bf", [P, SLICES * N], BF16)
         wt_w = held("wt_w", [P, PASSES * N], U32)
@@ -281,8 +313,10 @@ def tile_list_electrode_kinetics_transport_kernel(
                     quantise_wt(g)
             for lag, stage in (((2, quantise_rates), (3, transport), (4, round_y), (5, quantise_y))):
                 for first, count in STORE_GROUPS:
-                    if step == PASSES * (first + count) + lag:
+                    if step == PASSES * (first + count) + lag and (first < CHUNKS - 1 or lag > 3):
                         stage(first, count)
+            if step - units - 1 in range(PASSES):
+                last_pass(step - units - 1)
 
         for quad in range(4):
             queue = nc.sync if quad % 2 == 0 else nc.scalar

@@ -23,14 +23,13 @@ CHUNKS = S // JC
 HALF = S // 2
 SLICES = H // P
 PASSES = H // (P * PACK)
-SUB_ON_GPSIMD = ()
-WT_CAST = "ss"
-YBF = "ssssssvv"
-HOLD = 2
-SPLIT_SUB = (0, 7)
-GATHER_STEPS = (2, 3, 5)
+UNIT = JC * PACK
 RUN = 2
-STORE_GROUPS = ((0, 2), (2, 2), (4, 2), (6, 1), (7, 1))
+GROUPS = ((0, 2), (2, 2), (4, 2), (6, 1), (7, 1))
+YBF = "vsssv"
+HOLDS = {4: 1}
+SUB_G = ((0, 0),)
+WT_CAST = "gs"
 
 
 def tile_list_electrode_kinetics_transport_kernel(
@@ -41,6 +40,7 @@ def tile_list_electrode_kinetics_transport_kernel(
     with ExitStack() as ctx:
         keep = ctx.enter_context(tc.tile_pool(name="keep", bufs=1))
         ring = ctx.enter_context(tc.tile_pool(name="ring", bufs=1))
+        placed = ctx.enter_context(tc.tile_pool(name="placed", bufs=1))
         psum = ctx.enter_context(tc.psum_pool(name="psum", bufs=2))
 
         def held(name, shape, dtype):
@@ -49,72 +49,73 @@ def tile_list_electrode_kinetics_transport_kernel(
         lists = {n: held("list_" + n, [P, S // 16], U16) for n in "ace"}
         tab_w = held("tab_w", [P, T], U32)
         tab_s = held("tab_s", [P, T], U8)
-        wc_s_raw = ring.tile([P, H], U8, name="wc_s_raw", tag="then_c0", align_bytes=64)
+        wc_s_raw = held("wc_s_raw", [P, H], U8)
         we_s_raw = held("we_s_raw", [P, H], U8)
-        wc_raw = held("wc_raw", [P, H // 2], I32)
-        we_raw = ring.tile([P, H], I32, name="we_raw", tag="then_e0", align_bytes=64)
+        wc_raw = placed.tile([P, H // 2], I32, name="wc_raw", offset=3072, align_bytes=64)
+        we_raw = placed.tile([P, H], I32, name="we_raw", offset=8192, align_bytes=64)
         wa_raw = [held("wa_raw%d" % u, [P, PACK, H // 2], F32) for u in range(2)]
-        wt_raw = ring.tile([P, SLICES * N], F32, name="wt_raw", tag="then_exp")
+        wt_raw = [ring.tile([P, PACK * N], F32, name="wt_raw%d" % g, tag="stage%d" % g) for g in range(PASSES)]
         src_sb = held("src_sb", [P, PACK], F32)
 
         def load_scale_rows(queue, plane, rows):
             for quad in range(4):
-                queue.dma_start(
+                queue[quad % 2].dma_start(
                     out=plane[32 * quad : 32 * quad + 4, :].bitcast(I32),
                     in_=rows[0, 4 * quad : 4 * quad + 4, :].bitcast(I32),
                 )
 
-        for plane in (tab_s, wc_s_raw, we_s_raw):
-            nc.vector.memset(plane[:].bitcast(I32), 0)
-        for n, lst in (("a", offs), ("c", offs2), ("e", offs3)):
-            nc.sync.dma_start(lists[n][:], lst)
-        load_scale_rows(nc.scalar, tab_s, tab_scales)
+        nc.vector.memset(tab_s[:, : T // 2].bitcast(I32), 0)
+        nc.gpsimd.memset(tab_s[:, T // 2 :].bitcast(I32), 0)
+        for plane in (wc_s_raw, we_s_raw):
+            nc.gpsimd.memset(plane[:].bitcast(I32), 0)
+        nc.sync.dma_start(lists["a"][:], offs)
+        load_scale_rows((nc.sync, nc.scalar), tab_s, tab_scales)
+        nc.sync.dma_start(lists["c"][:], offs2)
+        nc.sync.dma_start(lists["e"][:], offs3)
         wa_rows = wa.rearrange("(p j) r -> p j r", j=PACK)
         nc.sync.dma_start(out=wa_raw[0][:], in_=wa_rows[:, :, :512])
-        load_scale_rows(nc.sync, wc_s_raw, wc_scales)
-        nc.sync.dma_start(out=wc_raw[:], in_=wc_words[0].bitcast(I32))
         nc.sync.dma_start(out=wa_raw[1][:], in_=wa_rows[:, :, 512:])
+        load_scale_rows((nc.sync, nc.sync), wc_s_raw, wc_scales)
         nc.sync.dma_start(
             out=tab_w[:].bitcast(I32), in_=tab_words[0].rearrange("p t i -> p (t i)").bitcast(I32)
         )
-        load_scale_rows(nc.sync, we_s_raw, we_scales)
+        nc.sync.dma_start(out=wc_raw[:], in_=wc_words[0].bitcast(I32))
         nc.sync.dma_start(out=we_raw[:], in_=we_words[0].rearrange("p y i -> p (y i)").bitcast(I32))
-        nc.sync.dma_start(out=src_sb[:], in_=src.rearrange("(p t) -> p t", t=PACK))
+        load_scale_rows((nc.sync, nc.sync), we_s_raw, we_scales)
         wt_rows = wt.rearrange("(g k t i) n -> g i k t n", g=PASSES, t=PACK, i=4)
         for g in range(PASSES):
             for i in range(4):
-                nc.sync.dma_start(out=wt_raw[i:P:4, 2048 * g : 2048 * (g + 1)].rearrange("k (t n) -> k t n", t=PACK), in_=wt_rows[g, i])
+                nc.sync.dma_start(out=wt_raw[g][i:P:4, :].rearrange("k (t n) -> k t n", t=PACK), in_=wt_rows[g, i])
+        nc.sync.dma_start(out=src_sb[:], in_=src.rearrange("(p t) -> p t", t=PACK))
 
         v_s = {n: held("v_s_" + n, [P, S], U8) for n in "ace"}
-
-        def gather_scales(n):
+        for n in "ace":
             nc.vector.tensor_copy(v_s[n][:], tab_s[:].indirect(lists[n][:]))
 
-        gather_scales("a")
-        gather_scales("c")
-        gather_scales("e")
-
-        wa_bf = held("wa_bf", [P, PACK * H], BF16)
-        for g in range(PASSES):
-            nc.scalar.copy(
-                out=wa_bf[:, 2048 * g : 2048 * (g + 1)].rearrange("p (t k i j) -> p t k j i", t=PACK, i=4, j=PACK),
-                in_=wa_raw[g][:].rearrange("p j (k t i) -> p t k j i", t=PACK, i=4),
-            )
+        wa_bf = [held("wa_bf%d" % g, [P, PACK * N], BF16) for g in range(PASSES)]
         wa_w = held("wa_w", [P, H], U32)
         wa_s = held("wa_s", [P, H], U8)
+        for g in range(PASSES):
+            nc.scalar.copy(
+                out=wa_bf[g][:].rearrange("p (t k i j) -> p t k j i", t=PACK, i=4, j=PACK),
+                in_=wa_raw[g][:].rearrange("p j (k t i) -> p t k j i", t=PACK, i=4),
+            )
         for g in range(PASSES):
             nc.vector.quantize_mx(
                 out=wa_w[:, 512 * g : 512 * (g + 1)].bitcast(E4M3),
                 scales=wa_s[:, 512 * g : 512 * (g + 1)],
-                in_=wa_bf[:, 2048 * g : 2048 * (g + 1)],
+                in_=wa_bf[g][:],
             )
 
         v_w = {}
 
-        def gather_words(n, u):
+        def gather_words(n, u, halves=1):
             cols = HALF // 16
-            v_w[n, u] = ring.tile([P, HALF], U32, name="v_w_%s%d" % (n, u), tag="then_%s%d" % (n, u), align_bytes=64)
-            nc.vector.tensor_copy(v_w[n, u][:], tab_w[:].indirect(lists[n][:, cols * u : cols * (u + 1)]))
+            at = {"a0": 0, "c0": 2048, "a1": 4096, "e0": 6144, "c1": 10240}[n + str(u)]
+            words = placed.tile([P, halves * HALF], U32, name="v_w_%s%d" % (n, u), offset=at, align_bytes=64)
+            nc.vector.tensor_copy(words[:], tab_w[:].indirect(lists[n][:, cols * u : cols * (u + halves)]))
+            for half in range(halves):
+                v_w[n, u + half] = words[:, HALF * half : HALF * (half + 1)]
 
         def deal(name, raw):
             width = raw.shape[1]
@@ -125,13 +126,15 @@ def tile_list_electrode_kinetics_transport_kernel(
             )
             return dealt
 
-        wc_w = deal("wc_w", wc_raw[:])
         wc_s = deal("wc_s", wc_s_raw[:].bitcast(I32))
         gather_words("a", 0)
+        wc_w = deal("wc_w", wc_raw[:])
         gather_words("c", 0)
-        we_s = deal("we_s", we_s_raw[:].bitcast(I32))
+        gather_words("a", 1)
         we_w = deal("we_w", we_raw[:])
-        gather_words("e", 0)
+        we_s = deal("we_s", we_s_raw[:].bitcast(I32))
+        gather_words("c", 1)
+        gather_words("e", 0, 2)
 
         def weights(n, s):
             cols = slice(P * s, P * (s + 1))
@@ -145,7 +148,8 @@ def tile_list_electrode_kinetics_transport_kernel(
             return we_w[:, cols].bitcast(E4M3), we_s[:].bitcast(U8)[:, cols]
 
         def first_product(n, jc, g):
-            bank = psum.tile([P, PACK, JC], F32, name="bank_" + n)
+            tag = "e" if (jc, g) == (2, 0) else n
+            bank = psum.tile([P, PACK, JC], F32, name="bank_" + tag)
             u, j0 = divmod(jc * JC, HALF)
             for t in range(PACK):
                 codes, scales = weights(n, PACK * g + t)
@@ -157,35 +161,40 @@ def tile_list_electrode_kinetics_transport_kernel(
                 )
             return bank[:].rearrange("p t j -> p (t j)")
 
-        late, ex, diffs, h_bf, h_q, y_sb, y_bf = {}, {}, {}, {}, {}, {}, {}
-        group_of = {jc: (first, count) for first, count in STORE_GROUPS for jc in range(first, first + count)}
-        UNIT = JC * PACK
+        ex, diffs, h_bf, h_q, y_sb, y_bf = {}, {}, {}, {}, {}, {}
+        group_of = {jc: (first, count) for first, count in GROUPS for jc in range(first, first + count)}
 
-        def exponentials(unit):
-            jc, g = divmod(unit, PASSES)
-            if unit == PASSES * HOLD:
-                both = ring.tile([P, SLICES * N], F32, name="late", tag="then_exp")
-                late["a"], late["c"] = both[:, :2048], both[:, 2048:]
-            for n in "ac":
-                if g == 0 and jc >= HOLD:
-                    ex[n] = late[n][:, PASSES * UNIT * (jc % 2) : PASSES * UNIT * (jc % 2 + 1)]
-                elif g == 0:
-                    tag = {"a0": "then_a1", "c0": "then_c1", "a1": "then_e1"}.get(n + str(jc), "early_" + n + str(jc))
-                    ex[n] = ring.tile([P, PASSES * UNIT], F32, name="exp_" + n, tag=tag, align_bytes=64)[:]
-                nc.scalar.activation(
-                    out=ex[n][:, UNIT * g : UNIT * (g + 1)],
-                    in_=first_product(n, jc, g),
-                    func=ACT.Exp,
-                )
-            if g == 0:
+        after = {}
+
+        def staged(g):
+            if g not in after:
+                after[g] = ring.tile([P, (4 - g) * PASSES * UNIT], F32, name="after_wt", tag="stage%d" % g)
+            return after[g]
+
+        def exponentials(jc, g0=0, g1=PASSES):
+            if jc in HOLDS:
+                both = staged(HOLDS[jc])[:, : 2 * PASSES * UNIT]
+            else:
+                both = ring.tile([P, 2 * (g1 - g0) * UNIT], F32, name="exp", bufs=4)
+            ex[jc, g0] = both
+            for g in range(g0, g1):
+                for side, n in enumerate("ac"):
+                    at = UNIT * ((g1 - g0) * side + g - g0)
+                    nc.scalar.activation(out=both[:, at : at + UNIT], in_=first_product(n, jc, g), func=ACT.Exp)
+
+        def subtract(jc, g0, g1):
+            if jc == 3 and g0 == 0:
+                diffs[jc] = staged(1)[:, 2 * PASSES * UNIT :]
+            elif jc < 2 and g0 == 0:
+                diffs[jc] = ring.tile([P, PASSES * UNIT], F32, name="first_diff")
+            elif g0 == 0:
                 diffs[jc] = ring.tile([P, PASSES * UNIT], F32, name="diff", bufs=3)
-            if jc in SPLIT_SUB or g == PASSES - 1:
-                cols = slice(UNIT * g, UNIT * (g + 1)) if jc in SPLIT_SUB else slice(0, PASSES * UNIT)
-                eng = nc.gpsimd if unit in SUB_ON_GPSIMD else nc.vector
-                eng.tensor_tensor(out=diffs[jc][:, cols], in0=ex["a"][:, cols], in1=ex["c"][:, cols], op=ALU.subtract)
+            lo, hi = UNIT * g0, UNIT * g1
+            eng = nc.gpsimd if (jc, g0) in SUB_G else nc.vector
+            sides = ex[jc, 0][:, lo:hi], ex[jc, 0][:, PASSES * UNIT + lo : PASSES * UNIT + hi]
+            eng.tensor_tensor(out=diffs[jc][:, lo:hi], in0=sides[0], in1=sides[1], op=ALU.subtract)
 
-        def rates(unit):
-            jc, g = divmod(unit, PASSES)
+        def rates(jc, g):
             first, count = group_of[jc]
             if g == 0 and jc == first:
                 h_bf[first] = ring.tile([P, PASSES * count * UNIT], BF16, name="h_bf", bufs=2, align_bytes=64)
@@ -198,8 +207,8 @@ def tile_list_electrode_kinetics_transport_kernel(
             )
 
         def quantise_rates(first, count):
-            words = ring.tile([P, PASSES * count * JC], U32, name="h_w", bufs=2, align_bytes=64)
-            scales = ring.tile([P, PASSES * count * JC], U8, name="h_s", bufs=2, align_bytes=64)
+            words = held("h_w%d" % first, [P, PASSES * count * JC], U32)
+            scales = held("h_s%d" % first, [P, PASSES * count * JC], U8)
             nc.vector.quantize_mx(out=words[:].bitcast(E4M3), scales=scales[:], in_=h_bf[first][:])
             h_q[first] = (words, scales)
 
@@ -234,15 +243,19 @@ def tile_list_electrode_kinetics_transport_kernel(
             if g == PASSES - 1:
                 nc.sync.dma_start(out=out_rows[:, :, jc * JC :], in_=y_sb[jc][:])
 
-        wt_bf = held("wt_bf", [P, SLICES * N], BF16)
+        wt_bf = [held("wt_bf%d" % g, [P, PACK * N], BF16) for g in range(PASSES)]
         wt_w = held("wt_w", [P, PASSES * N], U32)
         wt_s = held("wt_s", [P, PASSES * N], U8)
 
-        def prepare_wt(g):
-            dst = wt_bf[:, 2048 * g : 2048 * (g + 1)].rearrange("p (t m j) -> p m j t", t=PACK, j=PACK)
-            source = wt_raw[:, 2048 * g : 2048 * (g + 1)].rearrange("p (j m t) -> p m j t", j=PACK, t=PACK)
+        def round_wt(g):
+            dst = wt_bf[g][:].rearrange("p (t m j) -> p m j t", t=PACK, j=PACK)
+            source = wt_raw[g][:].rearrange("p (j m t) -> p m j t", j=PACK, t=PACK)
             if WT_CAST[g] == "v":
                 nc.vector.tensor_copy(out=dst, in_=source)
+            elif WT_CAST[g] == "g":
+                dst = wt_bf[g][:].rearrange("p (t m j) -> p m t j", t=PACK, j=PACK)
+                source = wt_raw[g][:].rearrange("p (j m t) -> p m t j", j=PACK, t=PACK)
+                nc.gpsimd.tensor_scalar(out=dst, in0=source, scalar1=1.0, scalar2=0.0, op0=ALU.mult, op1=ALU.add)
             else:
                 nc.scalar.copy(out=dst, in_=source)
 
@@ -250,7 +263,7 @@ def tile_list_electrode_kinetics_transport_kernel(
             nc.vector.quantize_mx(
                 out=wt_w[:, N * g : N * (g + 1)].bitcast(E4M3),
                 scales=wt_s[:, N * g : N * (g + 1)],
-                in_=wt_bf[:, 2048 * g : 2048 * (g + 1)],
+                in_=wt_bf[g][:],
             )
 
         y_s = held("y_s", [P, S], U8)
@@ -282,41 +295,85 @@ def tile_list_electrode_kinetics_transport_kernel(
                         )
             nc.sync.dma_start(out=out_rows[:, :, first * JC : first * JC + width], in_=y_sb[first][:])
 
-        def round_y(first, count):
+        def round_y(index):
+            first, count = GROUPS[index]
             y_bf[first] = ring.tile([P, count * UNIT], BF16, name="y_bf", bufs=2, align_bytes=64)
             dst = y_bf[first][:].rearrange("p (c i t) -> p c t i", i=4, t=PACK)
             source = y_sb[first][:].rearrange("p t (c i) -> p c t i", i=4)
-            if YBF[first] == "v":
+            if YBF[index] == "v":
                 nc.vector.tensor_copy(out=dst, in_=source)
             else:
                 nc.scalar.copy(out=dst, in_=source)
 
-        def quantise_y(first, count):
+        def quantise_y(index):
+            first, count = GROUPS[index]
             cols = slice(first * JC, (first + count) * JC)
             y_w = held("y_w%d" % first, [P, count * JC], U32)
             nc.vector.quantize_mx(out=y_w[:].bitcast(E4M3), scales=y_s[:, cols], in_=y_bf[first][:])
             nc.sync.dma_start(out=out_words[:, cols], in_=y_w[:].bitcast(I32))
 
-        units = CHUNKS * PASSES
-        for step in range(units + 8):
-            if step < units:
-                exponentials(step)
-            if 0 <= step - 2 < units:
-                rates(step - 2)
-            if step in GATHER_STEPS:
-                gather_words("ace"[GATHER_STEPS.index(step)], 1)
-            if step == PASSES * HOLD - 1:
-                for g in range(PASSES):
-                    prepare_wt(g)
-            if step == PASSES * HOLD:
-                for g in range(PASSES):
-                    quantise_wt(g)
-            for lag, stage in (((2, quantise_rates), (3, transport), (4, round_y), (5, quantise_y))):
-                for first, count in STORE_GROUPS:
-                    if step == PASSES * (first + count) + lag and (first < CHUNKS - 1 or lag > 3):
-                        stage(first, count)
-            if step - units - 1 in range(PASSES):
-                last_pass(step - units - 1)
+        def chunk_rates(jc):
+            subtract(jc, 0, 2)
+            rates(jc, 0)
+            rates(jc, 1)
+
+        exponentials(0)
+        subtract(0, 0, 2)
+        exponentials(1)
+        round_wt(0)
+        exponentials(2)
+        rates(0, 0)
+        rates(0, 1)
+        subtract(1, 0, 2)
+        exponentials(3)
+        subtract(2, 0, 2)
+        rates(1, 0)
+        rates(1, 1)
+        quantise_wt(0)
+        quantise_rates(0, 2)
+        round_wt(1)
+        subtract(3, 0, 2)
+        rates(2, 0)
+        rates(2, 1)
+        quantise_wt(1)
+        exponentials(4)
+        rates(3, 0)
+        rates(3, 1)
+        transport(0, 2)
+        subtract(4, 0, 2)
+        quantise_rates(2, 2)
+        exponentials(5)
+        rates(4, 0)
+        rates(4, 1)
+        round_y(0)
+        transport(2, 2)
+        subtract(5, 0, 2)
+        exponentials(6)
+        quantise_y(0)
+        rates(5, 0)
+        rates(5, 1)
+        subtract(6, 0, 2)
+        quantise_rates(4, 2)
+        exponentials(7)
+        round_y(1)
+        rates(6, 0)
+        rates(6, 1)
+        transport(4, 2)
+        subtract(7, 0, 1)
+        quantise_rates(6, 1)
+        subtract(7, 1, 2)
+        quantise_y(1)
+        round_y(2)
+        rates(7, 0)
+        transport(6, 1)
+        rates(7, 1)
+        last_pass(0)
+        last_pass(1)
+        round_y(3)
+        quantise_y(2)
+        round_y(4)
+        quantise_y(3)
+        quantise_y(4)
 
         for quad in range(4):
             queue = nc.sync if quad % 2 == 0 else nc.scalar

@@ -26,9 +26,9 @@ PASSES = H // (P * PACK)
 UNIT = JC * PACK
 RUN = 2
 GROUPS = ((0, 2), (2, 2), (4, 2), (6, 1), (7, 1))
-YBF = "vsssv"
+YBF = "ssssv"
 HOLDS = {4: 1}
-SUB_G = ((0, 0),)
+SUB_G = ((0, 0), (0, 1))
 WT_CAST = "gs"
 
 
@@ -50,11 +50,11 @@ def tile_list_electrode_kinetics_transport_kernel(
         tab_w = held("tab_w", [P, T], U32)
         tab_s = held("tab_s", [P, T], U8)
         wc_s_raw = held("wc_s_raw", [P, H], U8)
-        we_s_raw = held("we_s_raw", [P, H], U8)
-        wc_raw = placed.tile([P, H // 2], I32, name="wc_raw", offset=3072, align_bytes=64)
-        we_raw = placed.tile([P, H], I32, name="we_raw", offset=8192, align_bytes=64)
+        we_s_raw = placed.tile([P, H], U8, name="we_s_raw", offset=4096, align_bytes=64)
+        wc_raw = placed.tile([P, H // 2], I32, name="wc_raw", offset=10752, align_bytes=64)
+        we_raw = placed.tile([P, H], I32, name="we_raw", offset=0, align_bytes=64)
         wa_raw = [held("wa_raw%d" % u, [P, PACK, H // 2], F32) for u in range(2)]
-        wt_raw = [ring.tile([P, PACK * N], F32, name="wt_raw%d" % g, tag="stage%d" % g) for g in range(PASSES)]
+        wt_raw = [ring.tile([P, PACK * N], F32, name="wt_raw%d" % g, tag="stage%d" % g, align_bytes=64) for g in range(PASSES)]
         src_sb = held("src_sb", [P, PACK], F32)
 
         def load_scale_rows(queue, plane, rows):
@@ -109,11 +109,9 @@ def tile_list_electrode_kinetics_transport_kernel(
 
         v_w = {}
 
-        def gather_words(n, u, halves=1):
+        def gather_words(n, u, words, halves=1):
             cols = HALF // 16
-            at = {"a0": 0, "c0": 2048, "a1": 4096, "e0": 6144, "c1": 10240}[n + str(u)]
-            words = placed.tile([P, halves * HALF], U32, name="v_w_%s%d" % (n, u), offset=at, align_bytes=64)
-            nc.vector.tensor_copy(words[:], tab_w[:].indirect(lists[n][:, cols * u : cols * (u + halves)]))
+            nc.vector.tensor_copy(words, tab_w[:].indirect(lists[n][:, cols * u : cols * (u + halves)]))
             for half in range(halves):
                 v_w[n, u + half] = words[:, HALF * half : HALF * (half + 1)]
 
@@ -127,14 +125,16 @@ def tile_list_electrode_kinetics_transport_kernel(
             return dealt
 
         wc_s = deal("wc_s", wc_s_raw[:].bitcast(I32))
-        gather_words("a", 0)
+        gather_words("a", 0, held("v_w_a0", [P, HALF], U32)[:])
         wc_w = deal("wc_w", wc_raw[:])
-        gather_words("c", 0)
-        gather_words("a", 1)
+        gather_words("c", 0, held("v_w_c0", [P, HALF], U32)[:])
         we_w = deal("we_w", we_raw[:])
         we_s = deal("we_s", we_s_raw[:].bitcast(I32))
-        gather_words("c", 1)
-        gather_words("e", 0, 2)
+        v_w_a1 = placed.tile([P, HALF], U32, name="v_w_a1", offset=10752, align_bytes=64)
+        gather_words("a", 1, v_w_a1[:])
+        v_w_late = placed.tile([P, 3 * HALF], U32, name="v_w_late", offset=4608, align_bytes=64)
+        gather_words("c", 1, v_w_late[:, :HALF])
+        gather_words("e", 0, v_w_late[:, HALF:], 2)
 
         def weights(n, s):
             cols = slice(P * s, P * (s + 1))
@@ -148,7 +148,7 @@ def tile_list_electrode_kinetics_transport_kernel(
             return we_w[:, cols].bitcast(E4M3), we_s[:].bitcast(U8)[:, cols]
 
         def first_product(n, jc, g):
-            tag = "e" if (jc, g) == (2, 0) else n
+            tag = "e" if n == "c" and PASSES * jc + g in (3, 4) else n
             bank = psum.tile([P, PACK, JC], F32, name="bank_" + tag)
             u, j0 = divmod(jc * JC, HALF)
             for t in range(PACK):
@@ -168,7 +168,7 @@ def tile_list_electrode_kinetics_transport_kernel(
 
         def staged(g):
             if g not in after:
-                after[g] = ring.tile([P, (4 - g) * PASSES * UNIT], F32, name="after_wt", tag="stage%d" % g)
+                after[g] = ring.tile([P, 4 * PASSES * UNIT], F32, name="after_wt", tag="stage%d" % g, align_bytes=64)
             return after[g]
 
         def exponentials(jc, g0=0, g1=PASSES):
@@ -177,16 +177,23 @@ def tile_list_electrode_kinetics_transport_kernel(
             else:
                 both = ring.tile([P, 2 * (g1 - g0) * UNIT], F32, name="exp", bufs=4)
             ex[jc, g0] = both
-            for g in range(g0, g1):
-                for side, n in enumerate("ac"):
+            order = [(g, side) for g in range(g0, g1) for side in range(2)]
+            for g, side in sorted(order, key=lambda pair: pair[1]) if jc == 0 else order:
+                if True:
+                    n = "ac"[side]
                     at = UNIT * ((g1 - g0) * side + g - g0)
                     nc.scalar.activation(out=both[:, at : at + UNIT], in_=first_product(n, jc, g), func=ACT.Exp)
 
+        halves = {}
+
         def subtract(jc, g0, g1):
             if jc == 3 and g0 == 0:
-                diffs[jc] = staged(1)[:, 2 * PASSES * UNIT :]
-            elif jc < 2 and g0 == 0:
-                diffs[jc] = ring.tile([P, PASSES * UNIT], F32, name="first_diff")
+                diffs[jc] = staged(1)[:, 2 * PASSES * UNIT : 3 * PASSES * UNIT]
+            elif jc == 0:
+                diffs[jc] = ring.tile([P, PASSES * UNIT], F32, name="early_diff", bufs=2)
+                halves[g0] = diffs[jc]
+            elif jc < 3:
+                diffs[jc] = ring.tile([P, PASSES * UNIT], F32, name="early_diff", bufs=2)
             elif g0 == 0:
                 diffs[jc] = ring.tile([P, PASSES * UNIT], F32, name="diff", bufs=3)
             lo, hi = UNIT * g0, UNIT * g1
@@ -196,12 +203,14 @@ def tile_list_electrode_kinetics_transport_kernel(
 
         def rates(jc, g):
             first, count = group_of[jc]
-            if g == 0 and jc == first:
+            if g == 0 and jc == 2:
+                h_bf[first] = staged(1)[:, 3 * PASSES * UNIT :].bitcast(BF16)
+            elif g == 0 and jc == first:
                 h_bf[first] = ring.tile([P, PASSES * count * UNIT], BF16, name="h_bf", bufs=2, align_bytes=64)
             at = UNIT * (g * count + jc - first)
             nc.vector.tensor_tensor(
                 out=h_bf[first][:, at : at + UNIT].rearrange("p (c i t) -> p c t i", i=RUN, t=PACK),
-                in0=diffs[jc][:, UNIT * g : UNIT * (g + 1)].rearrange("p (t c i) -> p c t i", i=RUN, t=PACK),
+                in0=(halves[g] if jc == 0 else diffs[jc])[:, UNIT * g : UNIT * (g + 1)].rearrange("p (t c i) -> p c t i", i=RUN, t=PACK),
                 in1=first_product("e", jc, g).rearrange("p (t c i) -> p c t i", i=RUN, t=PACK),
                 op=ALU.mult,
             )
@@ -255,7 +264,11 @@ def tile_list_electrode_kinetics_transport_kernel(
             elif WT_CAST[g] == "g":
                 dst = wt_bf[g][:].rearrange("p (t m j) -> p m t j", t=PACK, j=PACK)
                 source = wt_raw[g][:].rearrange("p (j m t) -> p m t j", j=PACK, t=PACK)
-                nc.gpsimd.tensor_scalar(out=dst, in0=source, scalar1=1.0, scalar2=0.0, op0=ALU.mult, op1=ALU.add)
+                for m in range(0, P, P // 2):
+                    nc.gpsimd.tensor_scalar(
+                        out=dst[:, m : m + P // 2], in0=source[:, m : m + P // 2],
+                        scalar1=1.0, scalar2=0.0, op0=ALU.mult, op1=ALU.add,
+                    )
             else:
                 nc.scalar.copy(out=dst, in_=source)
 
@@ -318,7 +331,8 @@ def tile_list_electrode_kinetics_transport_kernel(
             rates(jc, 1)
 
         exponentials(0)
-        subtract(0, 0, 2)
+        subtract(0, 0, 1)
+        subtract(0, 1, 2)
         exponentials(1)
         round_wt(0)
         exponentials(2)
@@ -332,29 +346,29 @@ def tile_list_electrode_kinetics_transport_kernel(
         quantise_wt(0)
         quantise_rates(0, 2)
         round_wt(1)
-        subtract(3, 0, 2)
         rates(2, 0)
         rates(2, 1)
         quantise_wt(1)
         exponentials(4)
+        subtract(3, 0, 2)
+        transport(0, 2)
+        exponentials(5)
+        subtract(4, 0, 2)
         rates(3, 0)
         rates(3, 1)
-        transport(0, 2)
-        subtract(4, 0, 2)
+        round_y(0)
         quantise_rates(2, 2)
-        exponentials(5)
         rates(4, 0)
         rates(4, 1)
-        round_y(0)
-        transport(2, 2)
-        subtract(5, 0, 2)
         exponentials(6)
+        subtract(5, 0, 2)
+        transport(2, 2)
         quantise_y(0)
         rates(5, 0)
         rates(5, 1)
+        exponentials(7)
         subtract(6, 0, 2)
         quantise_rates(4, 2)
-        exponentials(7)
         round_y(1)
         rates(6, 0)
         rates(6, 1)

@@ -26,9 +26,9 @@ PASSES = H // (P * PACK)
 UNIT = JC * PACK
 RUN = 2
 GROUPS = ((0, 2), (2, 2), (4, 2), (6, 1), (7, 1))
-YBF = "ssssv"
+YBF = "vsssv"
 HOLDS = {4: 1}
-SUB_G = ((0, 0), (0, 1))
+SUB_G = ((0, 0), (0, 1), (2, 1), (3, 1), (4, 1), (5, 1), (6, 1))
 WT_CAST = "gs"
 
 
@@ -192,14 +192,18 @@ def tile_list_electrode_kinetics_transport_kernel(
             elif jc == 0:
                 diffs[jc] = ring.tile([P, PASSES * UNIT], F32, name="early_diff", bufs=2)
                 halves[g0] = diffs[jc]
-            elif jc < 3:
+            elif jc == 1:
+                diffs[jc] = staged(0)[:, : PASSES * UNIT]
+            elif jc < 3 and g0 == 0:
                 diffs[jc] = ring.tile([P, PASSES * UNIT], F32, name="early_diff", bufs=2)
             elif g0 == 0:
                 diffs[jc] = ring.tile([P, PASSES * UNIT], F32, name="diff", bufs=3)
             lo, hi = UNIT * g0, UNIT * g1
             eng = nc.gpsimd if (jc, g0) in SUB_G else nc.vector
             sides = ex[jc, 0][:, lo:hi], ex[jc, 0][:, PASSES * UNIT + lo : PASSES * UNIT + hi]
-            eng.tensor_tensor(out=diffs[jc][:, lo:hi], in0=sides[0], in1=sides[1], op=ALU.subtract)
+            spent = jc > 0 and (jc, g0) in SUB_G
+            target = ex[1 if jc == 2 else jc, 0][:, :UNIT] if spent else diffs[jc][:, lo:hi]
+            eng.tensor_tensor(out=target, in0=sides[0], in1=sides[1], op=ALU.subtract)
 
         def rates(jc, g):
             first, count = group_of[jc]
@@ -208,9 +212,13 @@ def tile_list_electrode_kinetics_transport_kernel(
             elif g == 0 and jc == first:
                 h_bf[first] = ring.tile([P, PASSES * count * UNIT], BF16, name="h_bf", bufs=2, align_bytes=64)
             at = UNIT * (g * count + jc - first)
+            if jc > 0 and (jc, g) in SUB_G:
+                diff = ex[1 if jc == 2 else jc, 0][:, :UNIT]
+            else:
+                diff = (halves[g] if jc == 0 else diffs[jc])[:, UNIT * g : UNIT * (g + 1)]
             nc.vector.tensor_tensor(
                 out=h_bf[first][:, at : at + UNIT].rearrange("p (c i t) -> p c t i", i=RUN, t=PACK),
-                in0=(halves[g] if jc == 0 else diffs[jc])[:, UNIT * g : UNIT * (g + 1)].rearrange("p (t c i) -> p c t i", i=RUN, t=PACK),
+                in0=diff.rearrange("p (t c i) -> p c t i", i=RUN, t=PACK),
                 in1=first_product("e", jc, g).rearrange("p (t c i) -> p c t i", i=RUN, t=PACK),
                 op=ALU.mult,
             )
@@ -340,34 +348,39 @@ def tile_list_electrode_kinetics_transport_kernel(
         rates(0, 1)
         subtract(1, 0, 2)
         exponentials(3)
-        subtract(2, 0, 2)
+        subtract(2, 0, 1)
+        subtract(2, 1, 2)
         rates(1, 0)
         rates(1, 1)
         quantise_wt(0)
         quantise_rates(0, 2)
         round_wt(1)
+        subtract(3, 0, 1)
+        subtract(3, 1, 2)
         rates(2, 0)
         rates(2, 1)
         quantise_wt(1)
         exponentials(4)
-        subtract(3, 0, 2)
         transport(0, 2)
         exponentials(5)
-        subtract(4, 0, 2)
+        subtract(4, 0, 1)
+        subtract(4, 1, 2)
         rates(3, 0)
         rates(3, 1)
-        round_y(0)
         quantise_rates(2, 2)
+        round_y(0)
+        exponentials(6)
+        subtract(5, 0, 1)
+        subtract(5, 1, 2)
         rates(4, 0)
         rates(4, 1)
-        exponentials(6)
-        subtract(5, 0, 2)
         transport(2, 2)
         quantise_y(0)
+        exponentials(7)
+        subtract(6, 0, 1)
+        subtract(6, 1, 2)
         rates(5, 0)
         rates(5, 1)
-        exponentials(7)
-        subtract(6, 0, 2)
         quantise_rates(4, 2)
         round_y(1)
         rates(6, 0)

@@ -28,7 +28,7 @@ RUN = 2
 GROUPS = ((0, 2), (2, 2), (4, 2), (6, 1), (7, 1))
 YBF = "vsssv"
 HOLDS = {4: 1}
-SUB_G = ((0, 0), (0, 1), (2, 1), (3, 1), (4, 1), (5, 1), (6, 1))
+SUB_G = ((0, 0), (0, 1), (2, 1), (3, 1), (4, 1), (5, 1), (6, 1), (7, 1))
 WT_CAST = "gs"
 
 
@@ -187,13 +187,13 @@ def tile_list_electrode_kinetics_transport_kernel(
         halves = {}
 
         def subtract(jc, g0, g1):
-            if jc == 3 and g0 == 0:
-                diffs[jc] = staged(1)[:, 2 * PASSES * UNIT : 3 * PASSES * UNIT]
-            elif jc == 0:
+            if jc == 0:
                 diffs[jc] = ring.tile([P, PASSES * UNIT], F32, name="early_diff", bufs=2)
                 halves[g0] = diffs[jc]
             elif jc == 1:
                 diffs[jc] = staged(0)[:, : PASSES * UNIT]
+            elif jc == 3 and g0 == 0:
+                diffs[jc] = staged(0)[:, PASSES * UNIT : 2 * PASSES * UNIT]
             elif jc < 3 and g0 == 0:
                 diffs[jc] = ring.tile([P, PASSES * UNIT], F32, name="early_diff", bufs=2)
             elif g0 == 0:
@@ -206,12 +206,12 @@ def tile_list_electrode_kinetics_transport_kernel(
             eng.tensor_tensor(out=target, in0=sides[0], in1=sides[1], op=ALU.subtract)
 
         def rates(jc, g):
-            first, count = group_of[jc]
+            first = jc
             if g == 0 and jc == 2:
-                h_bf[first] = staged(1)[:, 3 * PASSES * UNIT :].bitcast(BF16)
-            elif g == 0 and jc == first:
-                h_bf[first] = ring.tile([P, PASSES * count * UNIT], BF16, name="h_bf", bufs=2, align_bytes=64)
-            at = UNIT * (g * count + jc - first)
+                h_bf[first] = staged(1)[:, 2 * PASSES * UNIT : 2 * PASSES * UNIT + UNIT].bitcast(BF16)
+            elif g == 0:
+                h_bf[first] = ring.tile([P, PASSES * UNIT], BF16, name="h_bf", bufs=3, align_bytes=64)
+            at = UNIT * g
             if jc > 0 and (jc, g) in SUB_G:
                 diff = ex[1 if jc == 2 else jc, 0][:, :UNIT]
             else:
@@ -292,19 +292,21 @@ def tile_list_electrode_kinetics_transport_kernel(
         out_words = out_1[0].rearrange("p m t -> p (m t)").bitcast(I32)
 
         def transport(first, count):
-            words, scales = h_q[first]
             width = count * JC
             y_sb[first] = held("y_sb%d" % first, [P, PACK, width], F32)
             for t in range(PACK):
                 at = (t * width) % 512
                 if at == 0:
                     bank = psum.tile([P, 512], F32, name="bank_y")
-                for g in range(PASSES):
+                for step in range(count * PASSES):
+                    c, g = divmod(step, PASSES)
+                    words, scales = h_q[first + c]
                     cols = slice(N * g + P * t, N * g + P * (t + 1))
                     nc.tensor.matmul_mx(
-                        out=bank[:, at : at + width], lhsT=wt_w[:, cols].bitcast(E4M3), lhsT_scale=wt_s[:, cols],
-                        rhs=words[:, width * g : width * (g + 1)].bitcast(E4M3),
-                        rhs_scale=scales[:, width * g : width * (g + 1)],
+                        out=bank[:, at + JC * c : at + JC * (c + 1)],
+                        lhsT=wt_w[:, cols].bitcast(E4M3), lhsT_scale=wt_s[:, cols],
+                        rhs=words[:, JC * g : JC * (g + 1)].bitcast(E4M3),
+                        rhs_scale=scales[:, JC * g : JC * (g + 1)],
                         start=(g == 0), stop=(g == PASSES - 1),
                     )
                 if at + width == 512:
@@ -318,7 +320,7 @@ def tile_list_electrode_kinetics_transport_kernel(
 
         def round_y(index):
             first, count = GROUPS[index]
-            y_bf[first] = ring.tile([P, count * UNIT], BF16, name="y_bf", bufs=2, align_bytes=64)
+            y_bf[first] = ring.tile([P, count * UNIT], BF16, name="y_bf", bufs=4, align_bytes=64)
             dst = y_bf[first][:].rearrange("p (c i t) -> p c t i", i=4, t=PACK)
             source = y_sb[first][:].rearrange("p t (c i) -> p c t i", i=4)
             if YBF[index] == "v":
@@ -346,17 +348,18 @@ def tile_list_electrode_kinetics_transport_kernel(
         exponentials(2)
         rates(0, 0)
         rates(0, 1)
-        subtract(1, 0, 2)
-        exponentials(3)
         subtract(2, 0, 1)
+        quantise_rates(0, 1)
+        subtract(1, 0, 2)
         subtract(2, 1, 2)
+        exponentials(3)
         rates(1, 0)
         rates(1, 1)
         quantise_wt(0)
-        quantise_rates(0, 2)
-        round_wt(1)
         subtract(3, 0, 1)
         subtract(3, 1, 2)
+        quantise_rates(1, 1)
+        round_wt(1)
         rates(2, 0)
         rates(2, 1)
         quantise_wt(1)
@@ -365,13 +368,14 @@ def tile_list_electrode_kinetics_transport_kernel(
         exponentials(5)
         subtract(4, 0, 1)
         subtract(4, 1, 2)
+        quantise_rates(2, 1)
         rates(3, 0)
         rates(3, 1)
-        quantise_rates(2, 2)
         round_y(0)
         exponentials(6)
         subtract(5, 0, 1)
         subtract(5, 1, 2)
+        quantise_rates(3, 1)
         rates(4, 0)
         rates(4, 1)
         transport(2, 2)
@@ -379,21 +383,22 @@ def tile_list_electrode_kinetics_transport_kernel(
         exponentials(7)
         subtract(6, 0, 1)
         subtract(6, 1, 2)
+        quantise_rates(4, 1)
         rates(5, 0)
         rates(5, 1)
-        quantise_rates(4, 2)
         round_y(1)
+        subtract(7, 0, 1)
+        subtract(7, 1, 2)
+        quantise_rates(5, 1)
         rates(6, 0)
         rates(6, 1)
         transport(4, 2)
-        subtract(7, 0, 1)
-        quantise_rates(6, 1)
-        subtract(7, 1, 2)
         quantise_y(1)
-        round_y(2)
         rates(7, 0)
-        transport(6, 1)
+        quantise_rates(6, 1)
         rates(7, 1)
+        round_y(2)
+        transport(6, 1)
         last_pass(0)
         last_pass(1)
         round_y(3)

@@ -18,18 +18,17 @@ ALU = mybir.AluOpType
 
 P = 128
 PACK = 4
+BANK = 512
 JC = 128
 CHUNKS = S // JC
 HALF = S // 2
-SLICES = H // P
 PASSES = H // (P * PACK)
 UNIT = JC * PACK
-RUN = 2
-GROUPS = ((0, 2), (2, 2), (4, 2), (6, 1), (7, 1))
-YBF = "vsssv"
-HOLDS = {4: 1}
-SUB_G = ((0, 0), (0, 1), (2, 1), (3, 1), (4, 1), (5, 1), (6, 1), (7, 1))
-WT_CAST = "gs"
+BATCHES = ((0, 2), (2, 2), (4, 2), (6, 1), (7, 1))
+LAST = len(BATCHES) - 1
+ROUNDED_ON_VECTOR = (0, LAST)
+BANK_ON_VECTOR = (1, 2)
+AT_WE, AT_WE_SCALES, AT_LATE_WORDS, AT_WC = 0, 4096, 4608, 10752
 
 
 def tile_list_electrode_kinetics_transport_kernel(
@@ -46,20 +45,26 @@ def tile_list_electrode_kinetics_transport_kernel(
         def held(name, shape, dtype):
             return keep.tile(shape, dtype, name=name, align_bytes=64)
 
+        def place(name, shape, dtype, offset):
+            return placed.tile(shape, dtype, name=name, offset=offset, align_bytes=64)
+
         lists = {n: held("list_" + n, [P, S // 16], U16) for n in "ace"}
         tab_w = held("tab_w", [P, T], U32)
         tab_s = held("tab_s", [P, T], U8)
         wc_s_raw = held("wc_s_raw", [P, H], U8)
-        we_s_raw = placed.tile([P, H], U8, name="we_s_raw", offset=4096, align_bytes=64)
-        wc_raw = placed.tile([P, H // 2], I32, name="wc_raw", offset=10752, align_bytes=64)
-        we_raw = placed.tile([P, H], I32, name="we_raw", offset=0, align_bytes=64)
-        wa_raw = [held("wa_raw%d" % u, [P, PACK, H // 2], F32) for u in range(2)]
-        wt_raw = [ring.tile([P, PACK * N], F32, name="wt_raw%d" % g, tag="stage%d" % g, align_bytes=64) for g in range(PASSES)]
+        we_s_raw = place("we_s_raw", [P, H], U8, AT_WE_SCALES)
+        wc_raw = place("wc_raw", [P, H // 2], I32, AT_WC)
+        we_raw = place("we_raw", [P, H], I32, AT_WE)
+        wa_raw = [held("wa_raw%d" % g, [P, PACK, N], F32) for g in range(PASSES)]
+        wt_raw = [
+            ring.tile([P, PACK * N], F32, name="wt_raw%d" % g, tag="stage%d" % g, align_bytes=64)
+            for g in range(PASSES)
+        ]
         src_sb = held("src_sb", [P, PACK], F32)
 
-        def load_scale_rows(queue, plane, rows):
+        def load_scale_rows(queues, plane, rows):
             for quad in range(4):
-                queue[quad % 2].dma_start(
+                queues[quad % len(queues)].dma_start(
                     out=plane[32 * quad : 32 * quad + 4, :].bitcast(I32),
                     in_=rows[0, 4 * quad : 4 * quad + 4, :].bitcast(I32),
                 )
@@ -73,20 +78,21 @@ def tile_list_electrode_kinetics_transport_kernel(
         nc.sync.dma_start(lists["c"][:], offs2)
         nc.sync.dma_start(lists["e"][:], offs3)
         wa_rows = wa.rearrange("(p j) r -> p j r", j=PACK)
-        nc.sync.dma_start(out=wa_raw[0][:], in_=wa_rows[:, :, :512])
-        nc.sync.dma_start(out=wa_raw[1][:], in_=wa_rows[:, :, 512:])
-        load_scale_rows((nc.sync, nc.sync), wc_s_raw, wc_scales)
-        nc.sync.dma_start(
-            out=tab_w[:].bitcast(I32), in_=tab_words[0].rearrange("p t i -> p (t i)").bitcast(I32)
-        )
+        for g in range(PASSES):
+            nc.sync.dma_start(out=wa_raw[g][:], in_=wa_rows[:, :, N * g : N * (g + 1)])
+        load_scale_rows((nc.sync,), wc_s_raw, wc_scales)
+        nc.sync.dma_start(out=tab_w[:].bitcast(I32), in_=tab_words[0].rearrange("p t i -> p (t i)").bitcast(I32))
         nc.sync.dma_start(out=wc_raw[:], in_=wc_words[0].bitcast(I32))
         nc.sync.dma_start(out=we_raw[:], in_=we_words[0].rearrange("p y i -> p (y i)").bitcast(I32))
-        load_scale_rows((nc.sync, nc.sync), we_s_raw, we_scales)
-        wt_rows = wt.rearrange("(g k t i) n -> g i k t n", g=PASSES, t=PACK, i=4)
+        load_scale_rows((nc.sync,), we_s_raw, we_scales)
+        wt_rows = wt.rearrange("(g q t i) n -> g i q t n", g=PASSES, t=PACK, i=4)
         for g in range(PASSES):
             for i in range(4):
-                nc.sync.dma_start(out=wt_raw[g][i:P:4, :].rearrange("k (t n) -> k t n", t=PACK), in_=wt_rows[g, i])
+                nc.sync.dma_start(out=wt_raw[g][i:P:4, :].rearrange("q (t n) -> q t n", t=PACK), in_=wt_rows[g, i])
         nc.sync.dma_start(out=src_sb[:], in_=src.rearrange("(p t) -> p t", t=PACK))
+
+        def quantise(words, scales, values):
+            nc.vector.quantize_mx(out=words.bitcast(E4M3), scales=scales, in_=values)
 
         v_s = {n: held("v_s_" + n, [P, S], U8) for n in "ace"}
         for n in "ace":
@@ -97,30 +103,25 @@ def tile_list_electrode_kinetics_transport_kernel(
         wa_s = held("wa_s", [P, H], U8)
         for g in range(PASSES):
             nc.scalar.copy(
-                out=wa_bf[g][:].rearrange("p (t k i j) -> p t k j i", t=PACK, i=4, j=PACK),
-                in_=wa_raw[g][:].rearrange("p j (k t i) -> p t k j i", t=PACK, i=4),
+                out=wa_bf[g][:].rearrange("p (t q i j) -> p t q j i", t=PACK, i=4, j=PACK),
+                in_=wa_raw[g][:].rearrange("p j (q t i) -> p t q j i", t=PACK, i=4),
             )
         for g in range(PASSES):
-            nc.vector.quantize_mx(
-                out=wa_w[:, 512 * g : 512 * (g + 1)].bitcast(E4M3),
-                scales=wa_s[:, 512 * g : 512 * (g + 1)],
-                in_=wa_bf[g][:],
-            )
+            quantise(wa_w[:, N * g : N * (g + 1)], wa_s[:, N * g : N * (g + 1)], wa_bf[g][:])
 
         v_w = {}
 
-        def gather_words(n, u, words, halves=1):
-            cols = HALF // 16
-            nc.vector.tensor_copy(words, tab_w[:].indirect(lists[n][:, cols * u : cols * (u + halves)]))
+        def gather_words(n, first, words):
+            halves, cols = words.shape[1] // HALF, HALF // 16
+            nc.vector.tensor_copy(words, tab_w[:].indirect(lists[n][:, cols * first : cols * (first + halves)]))
             for half in range(halves):
-                v_w[n, u + half] = words[:, HALF * half : HALF * (half + 1)]
+                v_w[n, first + half] = words[:, HALF * half : HALF * (half + 1)]
 
         def deal(name, raw):
-            width = raw.shape[1]
-            dealt = held(name, [P, width], I32)
+            dealt = held(name, [P, raw.shape[1]], I32)
             nc.vector.tensor_copy(
-                out=dealt[:].rearrange("p (g t k w) -> p g t k w", g=PASSES, t=PACK, k=32),
-                in_=raw.rearrange("p (g k t w) -> p g t k w", g=PASSES, t=PACK, k=32),
+                out=dealt[:].rearrange("p (g t q w) -> p g t q w", g=PASSES, t=PACK, q=32),
+                in_=raw.rearrange("p (g q t w) -> p g t q w", g=PASSES, t=PACK, q=32),
             )
             return dealt
 
@@ -130,11 +131,10 @@ def tile_list_electrode_kinetics_transport_kernel(
         gather_words("c", 0, held("v_w_c0", [P, HALF], U32)[:])
         we_w = deal("we_w", we_raw[:])
         we_s = deal("we_s", we_s_raw[:].bitcast(I32))
-        v_w_a1 = placed.tile([P, HALF], U32, name="v_w_a1", offset=10752, align_bytes=64)
-        gather_words("a", 1, v_w_a1[:])
-        v_w_late = placed.tile([P, 3 * HALF], U32, name="v_w_late", offset=4608, align_bytes=64)
-        gather_words("c", 1, v_w_late[:, :HALF])
-        gather_words("e", 0, v_w_late[:, HALF:], 2)
+        gather_words("a", 1, place("v_w_a1", [P, HALF], U32, AT_WC)[:])
+        late_words = place("late_words", [P, 3 * HALF], U32, AT_LATE_WORDS)
+        gather_words("c", 1, late_words[:, :HALF])
+        gather_words("e", 0, late_words[:, HALF:])
 
         def weights(n, s):
             cols = slice(P * s, P * (s + 1))
@@ -148,264 +148,210 @@ def tile_list_electrode_kinetics_transport_kernel(
             return we_w[:, cols].bitcast(E4M3), we_s[:].bitcast(U8)[:, cols]
 
         def first_product(n, jc, g):
-            tag = "e" if n == "c" and PASSES * jc + g in (3, 4) else n
+            tag = "e" if n == "c" and (jc, g) in ((1, 1), (2, 0)) else n
             bank = psum.tile([P, PACK, JC], F32, name="bank_" + tag)
-            u, j0 = divmod(jc * JC, HALF)
+            half, j0 = divmod(jc * JC, HALF)
             for t in range(PACK):
                 codes, scales = weights(n, PACK * g + t)
                 nc.tensor.matmul_mx(
                     out=bank[:, t, :], lhsT=codes, lhsT_scale=scales,
-                    rhs=v_w[n, u][:, j0 : j0 + JC].bitcast(E4M3),
+                    rhs=v_w[n, half][:, j0 : j0 + JC].bitcast(E4M3),
                     rhs_scale=v_s[n][:, jc * JC : (jc + 1) * JC],
                     start=True, stop=True,
                 )
             return bank[:].rearrange("p t j -> p (t j)")
 
-        ex, diffs, h_bf, h_q, y_sb, y_bf = {}, {}, {}, {}, {}, {}
-        group_of = {jc: (first, count) for first, count in GROUPS for jc in range(first, first + count)}
+        ex, diff, h_bf, h_q = {}, {}, {}, {}
 
-        after = {}
-
-        def staged(g):
-            if g not in after:
-                after[g] = ring.tile([P, 4 * PASSES * UNIT], F32, name="after_wt", tag="stage%d" % g, align_bytes=64)
-            return after[g]
-
-        def exponentials(jc, g0=0, g1=PASSES):
-            if jc in HOLDS:
-                both = staged(HOLDS[jc])[:, : 2 * PASSES * UNIT]
-            else:
-                both = ring.tile([P, 2 * (g1 - g0) * UNIT], F32, name="exp", bufs=4)
-            ex[jc, g0] = both
-            order = [(g, side) for g in range(g0, g1) for side in range(2)]
-            for g, side in sorted(order, key=lambda pair: pair[1]) if jc == 0 else order:
-                if True:
-                    n = "ac"[side]
-                    at = UNIT * ((g1 - g0) * side + g - g0)
-                    nc.scalar.activation(out=both[:, at : at + UNIT], in_=first_product(n, jc, g), func=ACT.Exp)
-
-        halves = {}
-
-        def subtract(jc, g0, g1):
+        def exponentials(jc, tile=None):
+            if tile is None:
+                tile = ring.tile([P, 2 * PASSES * UNIT], F32, name="exp", bufs=4)
+            ex[jc] = tile
+            order = [(g, side) for g in range(PASSES) for side in range(2)]
             if jc == 0:
-                diffs[jc] = ring.tile([P, PASSES * UNIT], F32, name="early_diff", bufs=2)
-                halves[g0] = diffs[jc]
-            elif jc == 1:
-                diffs[jc] = staged(0)[:, : PASSES * UNIT]
-            elif jc == 3 and g0 == 0:
-                diffs[jc] = staged(0)[:, PASSES * UNIT : 2 * PASSES * UNIT]
-            elif jc < 3 and g0 == 0:
-                diffs[jc] = ring.tile([P, PASSES * UNIT], F32, name="early_diff", bufs=2)
-            elif g0 == 0:
-                diffs[jc] = ring.tile([P, PASSES * UNIT], F32, name="diff", bufs=3)
-            lo, hi = UNIT * g0, UNIT * g1
-            eng = nc.gpsimd if (jc, g0) in SUB_G else nc.vector
-            sides = ex[jc, 0][:, lo:hi], ex[jc, 0][:, PASSES * UNIT + lo : PASSES * UNIT + hi]
-            spent = jc > 0 and (jc, g0) in SUB_G
-            target = ex[1 if jc == 2 else jc, 0][:, :UNIT] if spent else diffs[jc][:, lo:hi]
-            eng.tensor_tensor(out=target, in0=sides[0], in1=sides[1], op=ALU.subtract)
+                order = sorted(order, key=lambda pair: pair[1])
+            for g, side in order:
+                at = UNIT * (PASSES * side + g)
+                nc.scalar.activation(out=tile[:, at : at + UNIT], in_=first_product("ac"[side], jc, g), func=ACT.Exp)
 
-        def rates(jc, g):
-            first = jc
-            if g == 0 and jc == 2:
-                h_bf[first] = staged(1)[:, 2 * PASSES * UNIT : 2 * PASSES * UNIT + UNIT].bitcast(BF16)
-            elif g == 0:
-                h_bf[first] = ring.tile([P, PASSES * UNIT], BF16, name="h_bf", bufs=3, align_bytes=64)
-            at = UNIT * g
-            if jc > 0 and (jc, g) in SUB_G:
-                diff = ex[1 if jc == 2 else jc, 0][:, :UNIT]
-            else:
-                diff = (halves[g] if jc == 0 else diffs[jc])[:, UNIT * g : UNIT * (g + 1)]
+        def subtract(engine, jc, g, target):
+            lo, width = UNIT * g, target.shape[1]
+            engine.tensor_tensor(
+                out=target, in0=ex[jc][:, lo : lo + width],
+                in1=ex[jc][:, PASSES * UNIT + lo : PASSES * UNIT + lo + width], op=ALU.subtract,
+            )
+            for more in range(width // UNIT):
+                diff[jc, g + more] = target[:, UNIT * more : UNIT * (more + 1)]
+
+        def rates(jc, g, tile=None):
+            if g == 0:
+                if tile is None:
+                    tile = ring.tile([P, PASSES * UNIT], BF16, name="h_bf", bufs=3, align_bytes=64)
+                h_bf[jc] = tile
             nc.vector.tensor_tensor(
-                out=h_bf[first][:, at : at + UNIT].rearrange("p (c i t) -> p c t i", i=RUN, t=PACK),
-                in0=diff.rearrange("p (t c i) -> p c t i", i=RUN, t=PACK),
-                in1=first_product("e", jc, g).rearrange("p (t c i) -> p c t i", i=RUN, t=PACK),
+                out=h_bf[jc][:, UNIT * g : UNIT * (g + 1)].rearrange("p (c i t) -> p c t i", i=2, t=PACK),
+                in0=diff[jc, g].rearrange("p (t c i) -> p c t i", i=2, t=PACK),
+                in1=first_product("e", jc, g).rearrange("p (t c i) -> p c t i", i=2, t=PACK),
                 op=ALU.mult,
             )
 
-        def quantise_rates(first, count):
-            words = held("h_w%d" % first, [P, PASSES * count * JC], U32)
-            scales = held("h_s%d" % first, [P, PASSES * count * JC], U8)
-            nc.vector.quantize_mx(out=words[:].bitcast(E4M3), scales=scales[:], in_=h_bf[first][:])
-            h_q[first] = (words, scales)
-
-        last_banks = []
-
-        def last_pass(g):
-            jc = CHUNKS - 1
-            words = held("h_w_last%d" % g, [P, JC], U32)
-            scales = held("h_s_last%d" % g, [P, JC], U8)
-            nc.vector.quantize_mx(
-                out=words[:].bitcast(E4M3), scales=scales[:], in_=h_bf[jc][:, UNIT * g : UNIT * (g + 1)]
-            )
-            if g == PASSES - 1:
-                y_sb[jc] = held("y_sb%d" % jc, [P, PACK, JC], F32)
-            for t in range(PACK):
-                if g == 0:
-                    last_banks.append(psum.tile([P, PACK, JC], F32, name="bank_" + "ac"[t % 2]))
-                cols = slice(N * g + P * t, N * g + P * (t + 1))
-                nc.tensor.matmul_mx(
-                    out=last_banks[t][:, 0, :], lhsT=wt_w[:, cols].bitcast(E4M3), lhsT_scale=wt_s[:, cols],
-                    rhs=words[:].bitcast(E4M3), rhs_scale=scales[:], start=(g == 0), stop=(g == PASSES - 1),
-                )
-                if g == PASSES - 1 and t % 2 == 0:
-                    nc.scalar.activation(
-                        out=y_sb[jc][:, t, :], in_=last_banks[t][:, 0, :], func=ACT.Identity, bias=src_sb[:, t : t + 1]
-                    )
-                elif g == PASSES - 1:
-                    nc.vector.tensor_scalar(
-                        out=y_sb[jc][:, t, :], in0=last_banks[t][:, 0, :], scalar1=src_sb[:, t : t + 1], scalar2=None,
-                        op0=ALU.add,
-                    )
-            if g == PASSES - 1:
-                nc.sync.dma_start(out=out_rows[:, :, jc * JC :], in_=y_sb[jc][:])
+        def quantise_rates(jc):
+            words = held("h_w%d" % jc, [P, PASSES * JC], U32)
+            scales = held("h_s%d" % jc, [P, PASSES * JC], U8)
+            quantise(words[:], scales[:], h_bf[jc][:])
+            h_q[jc] = (words, scales)
 
         wt_bf = [held("wt_bf%d" % g, [P, PACK * N], BF16) for g in range(PASSES)]
         wt_w = held("wt_w", [P, PASSES * N], U32)
         wt_s = held("wt_s", [P, PASSES * N], U8)
 
-        def round_wt(g):
-            dst = wt_bf[g][:].rearrange("p (t m j) -> p m j t", t=PACK, j=PACK)
-            source = wt_raw[g][:].rearrange("p (j m t) -> p m j t", j=PACK, t=PACK)
-            if WT_CAST[g] == "v":
-                nc.vector.tensor_copy(out=dst, in_=source)
-            elif WT_CAST[g] == "g":
-                dst = wt_bf[g][:].rearrange("p (t m j) -> p m t j", t=PACK, j=PACK)
-                source = wt_raw[g][:].rearrange("p (j m t) -> p m t j", j=PACK, t=PACK)
-                for m in range(0, P, P // 2):
-                    nc.gpsimd.tensor_scalar(
-                        out=dst[:, m : m + P // 2], in0=source[:, m : m + P // 2],
-                        scalar1=1.0, scalar2=0.0, op0=ALU.mult, op1=ALU.add,
-                    )
-            else:
-                nc.scalar.copy(out=dst, in_=source)
+        def round_wt_on_gpsimd(g):
+            dst = wt_bf[g][:].rearrange("p (t m j) -> p m t j", t=PACK, j=PACK)
+            source = wt_raw[g][:].rearrange("p (j m t) -> p m t j", j=PACK, t=PACK)
+            for m in range(0, P, P // 2):
+                nc.gpsimd.tensor_scalar(
+                    out=dst[:, m : m + P // 2], in0=source[:, m : m + P // 2],
+                    scalar1=1.0, scalar2=0.0, op0=ALU.mult, op1=ALU.add,
+                )
 
-        def quantise_wt(g):
-            nc.vector.quantize_mx(
-                out=wt_w[:, N * g : N * (g + 1)].bitcast(E4M3),
-                scales=wt_s[:, N * g : N * (g + 1)],
-                in_=wt_bf[g][:],
+        def round_wt_on_scalar(g):
+            nc.scalar.copy(
+                out=wt_bf[g][:].rearrange("p (t m j) -> p m j t", t=PACK, j=PACK),
+                in_=wt_raw[g][:].rearrange("p (j m t) -> p m j t", j=PACK, t=PACK),
             )
 
+        def quantise_wt(g):
+            quantise(wt_w[:, N * g : N * (g + 1)], wt_s[:, N * g : N * (g + 1)], wt_bf[g][:])
+
+        y_sb, y_bf = {}, {}
         y_s = held("y_s", [P, S], U8)
         out_rows = out_0.rearrange("(p t) j -> p t j", t=PACK)
         out_words = out_1[0].rearrange("p m t -> p (m t)").bitcast(I32)
 
-        def transport(first, count):
-            width = count * JC
-            y_sb[first] = held("y_sb%d" % first, [P, PACK, width], F32)
-            for t in range(PACK):
-                at = (t * width) % 512
-                if at == 0:
-                    bank = psum.tile([P, 512], F32, name="bank_y")
-                for step in range(count * PASSES):
-                    c, g = divmod(step, PASSES)
-                    words, scales = h_q[first + c]
-                    cols = slice(N * g + P * t, N * g + P * (t + 1))
-                    nc.tensor.matmul_mx(
-                        out=bank[:, at + JC * c : at + JC * (c + 1)],
-                        lhsT=wt_w[:, cols].bitcast(E4M3), lhsT_scale=wt_s[:, cols],
-                        rhs=words[:, JC * g : JC * (g + 1)].bitcast(E4M3),
-                        rhs_scale=scales[:, JC * g : JC * (g + 1)],
-                        start=(g == 0), stop=(g == PASSES - 1),
-                    )
-                if at + width == 512:
-                    for done in range(t + 1 - 512 // width, t + 1):
-                        at = (done * width) % 512
-                        nc.scalar.activation(
-                            out=y_sb[first][:, done, :], in_=bank[:, at : at + width], func=ACT.Identity,
-                            bias=src_sb[:, done : done + 1],
-                        )
-            nc.sync.dma_start(out=out_rows[:, :, first * JC : first * JC + width], in_=y_sb[first][:])
+        def second_product(out, t, g, words, scales):
+            cols = slice(N * g + P * t, N * g + P * (t + 1))
+            nc.tensor.matmul_mx(
+                out=out, lhsT=wt_w[:, cols].bitcast(E4M3), lhsT_scale=wt_s[:, cols],
+                rhs=words.bitcast(E4M3), rhs_scale=scales, start=(g == 0), stop=(g == PASSES - 1),
+            )
 
-        def round_y(index):
-            first, count = GROUPS[index]
-            y_bf[first] = ring.tile([P, count * UNIT], BF16, name="y_bf", bufs=4, align_bytes=64)
-            dst = y_bf[first][:].rearrange("p (c i t) -> p c t i", i=4, t=PACK)
-            source = y_sb[first][:].rearrange("p t (c i) -> p c t i", i=4)
-            if YBF[index] == "v":
+        def add_src_on_scalar(b, t, sums):
+            nc.scalar.activation(out=y_sb[b][:, t, :], in_=sums, func=ACT.Identity, bias=src_sb[:, t : t + 1])
+
+        def add_src_on_vector(b, t, sums):
+            nc.vector.tensor_scalar(
+                out=y_sb[b][:, t, :], in0=sums, scalar1=src_sb[:, t : t + 1], scalar2=None, op0=ALU.add
+            )
+
+        def store_y(b):
+            first, count = BATCHES[b]
+            nc.sync.dma_start(out=out_rows[:, :, first * JC : (first + count) * JC], in_=y_sb[b][:])
+
+        def transport(b):
+            first, count = BATCHES[b]
+            width = count * JC
+            per_bank = BANK // width
+            y_sb[b] = held("y_sb%d" % b, [P, PACK, width], F32)
+            for t0 in range(0, PACK, per_bank):
+                bank = psum.tile([P, per_bank, width], F32, name="bank_y")
+                for t in range(t0, t0 + per_bank):
+                    for c in range(count):
+                        words, scales = h_q[first + c]
+                        for g in range(PASSES):
+                            cols = slice(JC * g, JC * (g + 1))
+                            second_product(bank[:, t - t0, JC * c : JC * (c + 1)], t, g, words[:, cols], scales[:, cols])
+                add_src = add_src_on_vector if (b, t0) == BANK_ON_VECTOR else add_src_on_scalar
+                for t in range(t0, t0 + per_bank):
+                    add_src(b, t, bank[:, t - t0, :])
+            store_y(b)
+
+        def last_transport():
+            jc = CHUNKS - 1
+            banks = []
+            for g in range(PASSES):
+                words = held("h_w_last%d" % g, [P, JC], U32)
+                scales = held("h_s_last%d" % g, [P, JC], U8)
+                quantise(words[:], scales[:], h_bf[jc][:, UNIT * g : UNIT * (g + 1)])
+                if g == PASSES - 1:
+                    y_sb[LAST] = held("y_sb%d" % LAST, [P, PACK, JC], F32)
+                for t in range(PACK):
+                    if g == 0:
+                        banks.append(psum.tile([P, JC], F32, name="bank_" + "ac"[t % 2]))
+                    second_product(banks[t][:], t, g, words[:], scales[:])
+                    if g == PASSES - 1:
+                        add_src = add_src_on_scalar if t % 2 == 0 else add_src_on_vector
+                        add_src(LAST, t, banks[t][:])
+            store_y(LAST)
+
+        def round_y(b):
+            y_bf[b] = held("y_bf%d" % b, [P, BATCHES[b][1] * UNIT], BF16)
+            dst = y_bf[b][:].rearrange("p (c i t) -> p c t i", i=4, t=PACK)
+            source = y_sb[b][:].rearrange("p t (c i) -> p c t i", i=4)
+            if b in ROUNDED_ON_VECTOR:
                 nc.vector.tensor_copy(out=dst, in_=source)
             else:
                 nc.scalar.copy(out=dst, in_=source)
 
-        def quantise_y(index):
-            first, count = GROUPS[index]
+        def quantise_y(b):
+            first, count = BATCHES[b]
             cols = slice(first * JC, (first + count) * JC)
-            y_w = held("y_w%d" % first, [P, count * JC], U32)
-            nc.vector.quantize_mx(out=y_w[:].bitcast(E4M3), scales=y_s[:, cols], in_=y_bf[first][:])
+            y_w = held("y_w%d" % b, [P, count * JC], U32)
+            quantise(y_w[:], y_s[:, cols], y_bf[b][:])
             nc.sync.dma_start(out=out_words[:, cols], in_=y_w[:].bitcast(I32))
 
-        def chunk_rates(jc):
-            subtract(jc, 0, 2)
-            rates(jc, 0)
-            rates(jc, 1)
+        def early_diff():
+            return ring.tile([P, UNIT], F32, name="early_diff", bufs=2)[:]
 
         exponentials(0)
-        subtract(0, 0, 1)
-        subtract(0, 1, 2)
+        for g in range(PASSES):
+            subtract(nc.gpsimd, 0, g, early_diff())
         exponentials(1)
-        round_wt(0)
+        round_wt_on_gpsimd(0)
         exponentials(2)
         rates(0, 0)
         rates(0, 1)
-        subtract(2, 0, 1)
-        quantise_rates(0, 1)
-        subtract(1, 0, 2)
-        subtract(2, 1, 2)
+        subtract(nc.vector, 2, 0, early_diff())
+        quantise_rates(0)
+        after_wt0 = ring.tile([P, 3 * UNIT], F32, name="after_wt0", tag="stage0", align_bytes=64)
+        subtract(nc.vector, 1, 0, after_wt0[:, : 2 * UNIT])
+        subtract(nc.gpsimd, 2, 1, ex[1][:, :UNIT])
         exponentials(3)
         rates(1, 0)
         rates(1, 1)
         quantise_wt(0)
-        subtract(3, 0, 1)
-        subtract(3, 1, 2)
-        quantise_rates(1, 1)
-        round_wt(1)
-        rates(2, 0)
-        rates(2, 1)
-        quantise_wt(1)
-        exponentials(4)
-        transport(0, 2)
-        exponentials(5)
-        subtract(4, 0, 1)
-        subtract(4, 1, 2)
-        quantise_rates(2, 1)
-        rates(3, 0)
-        rates(3, 1)
-        round_y(0)
-        exponentials(6)
-        subtract(5, 0, 1)
-        subtract(5, 1, 2)
-        quantise_rates(3, 1)
-        rates(4, 0)
-        rates(4, 1)
-        transport(2, 2)
-        quantise_y(0)
-        exponentials(7)
-        subtract(6, 0, 1)
-        subtract(6, 1, 2)
-        quantise_rates(4, 1)
-        rates(5, 0)
-        rates(5, 1)
-        round_y(1)
-        subtract(7, 0, 1)
-        subtract(7, 1, 2)
-        quantise_rates(5, 1)
-        rates(6, 0)
-        rates(6, 1)
-        transport(4, 2)
-        quantise_y(1)
-        rates(7, 0)
-        quantise_rates(6, 1)
-        rates(7, 1)
-        round_y(2)
-        transport(6, 1)
-        last_pass(0)
-        last_pass(1)
-        round_y(3)
-        quantise_y(2)
-        round_y(4)
-        quantise_y(3)
-        quantise_y(4)
+        round_wt_on_scalar(1)
+        after_wt1 = ring.tile([P, 5 * UNIT], F32, name="after_wt1", tag="stage1", align_bytes=64)
+
+        for jc in range(3, CHUNKS):
+            if jc == 3:
+                first_diff = after_wt0[:, 2 * UNIT :]
+            else:
+                first_diff = ring.tile([P, UNIT], F32, name="diff", bufs=3)[:]
+            subtract(nc.vector, jc, 0, first_diff)
+            subtract(nc.gpsimd, jc, 1, ex[jc][:, :UNIT])
+            quantise_rates(jc - 2)
+            rates(jc - 1, 0, after_wt1[:, 4 * UNIT :].bitcast(BF16) if jc == 3 else None)
+            rates(jc - 1, 1)
+            if jc == 3:
+                quantise_wt(1)
+                exponentials(4, after_wt1[:, : 4 * UNIT])
+            for lag, stage in ((3, transport), (5, quantise_y), (4, round_y)):
+                if jc >= lag and (jc - lag) % 2 == 0:
+                    stage((jc - lag) // 2)
+            if jc + 2 < CHUNKS:
+                exponentials(jc + 2)
+
+        rates(CHUNKS - 1, 0)
+        quantise_rates(CHUNKS - 2)
+        rates(CHUNKS - 1, 1)
+        round_y(LAST - 2)
+        transport(LAST - 1)
+        last_transport()
+        round_y(LAST - 1)
+        quantise_y(LAST - 2)
+        round_y(LAST)
+        quantise_y(LAST - 1)
+        quantise_y(LAST)
 
         for quad in range(4):
             queue = nc.sync if quad % 2 == 0 else nc.scalar

@@ -26,9 +26,21 @@ PASSES = H // (P * PACK)
 UNIT = JC * PACK
 BATCHES = ((0, 2), (2, 2), (4, 2), (6, 1), (7, 1))
 LAST = len(BATCHES) - 1
-ROUNDED_ON_VECTOR = (0, LAST)
-BANK_ON_VECTOR = (1, 2)
-AT_WE, AT_WE_SCALES, AT_LATE_WORDS, AT_WC = 0, 4096, 4608, 10752
+UNITS = CHUNKS * PASSES
+PAIRS = UNITS // 2
+TILE = 4 * UNIT
+AT_LATE = 0
+AT_WT0 = AT_LATE + S + 5 * TILE
+AT_WT1 = AT_WT0 + 4 * TILE
+AT_C = AT_WT1 + 4 * TILE
+AT_A = AT_C + UNITS * TILE
+
+
+def unit_of(u):
+    k, i = divmod(u, 2)
+    if k < PAIRS - 2:
+        return 2 * (k // 2) + i, k % 2
+    return k, i
 
 
 def tile_list_electrode_kinetics_transport_kernel(
@@ -38,9 +50,8 @@ def tile_list_electrode_kinetics_transport_kernel(
     nc = tc.nc
     with ExitStack() as ctx:
         keep = ctx.enter_context(tc.tile_pool(name="keep", bufs=1))
-        ring = ctx.enter_context(tc.tile_pool(name="ring", bufs=1))
         placed = ctx.enter_context(tc.tile_pool(name="placed", bufs=1))
-        psum = ctx.enter_context(tc.psum_pool(name="psum", bufs=2))
+        psum = ctx.enter_context(tc.psum_pool(name="psum", bufs=1))
 
         def held(name, shape, dtype):
             return keep.tile(shape, dtype, name=name, align_bytes=64)
@@ -48,18 +59,18 @@ def tile_list_electrode_kinetics_transport_kernel(
         def place(name, shape, dtype, offset):
             return placed.tile(shape, dtype, name=name, offset=offset, align_bytes=64)
 
+        banks = [psum.tile([P, BANK], F32, name="bank%d" % b) for b in range(8)]
+        exp_banks, e_banks, y_banks = banks[0:3], banks[3:6], banks[6:8]
+
         lists = {n: held("list_" + n, [P, S // 16], U16) for n in "ace"}
         tab_w = held("tab_w", [P, T], U32)
         tab_s = held("tab_s", [P, T], U8)
-        wc_s_raw = held("wc_s_raw", [P, H], U8)
-        we_s_raw = place("we_s_raw", [P, H], U8, AT_WE_SCALES)
-        wc_raw = place("wc_raw", [P, H // 2], I32, AT_WC)
-        we_raw = place("we_raw", [P, H], I32, AT_WE)
+        wc_s_raw = place("wc_s_raw", [P, H], U8, AT_LATE + S // 2)
+        we_s_raw = held("we_s_raw", [P, H], U8)
+        wc_raw = held("wc_raw", [P, H // 2], I32)
+        we_raw = held("we_raw", [P, H], I32)
         wa_raw = [held("wa_raw%d" % g, [P, PACK, N], F32) for g in range(PASSES)]
-        wt_raw = [
-            ring.tile([P, PACK * N], F32, name="wt_raw%d" % g, tag="stage%d" % g, align_bytes=64)
-            for g in range(PASSES)
-        ]
+        wt_raw = [place("wt_raw0", [P, PACK * N], F32, AT_WT0), place("wt_raw1", [P, PACK * N], F32, AT_WT1)]
         src_sb = held("src_sb", [P, PACK], F32)
 
         def load_scale_rows(queues, plane, rows):
@@ -73,43 +84,36 @@ def tile_list_electrode_kinetics_transport_kernel(
         nc.gpsimd.memset(tab_s[:, T // 2 :].bitcast(I32), 0)
         for plane in (wc_s_raw, we_s_raw):
             nc.gpsimd.memset(plane[:].bitcast(I32), 0)
-        nc.sync.dma_start(lists["a"][:], offs)
-        load_scale_rows((nc.sync, nc.scalar), tab_s, tab_scales)
         nc.sync.dma_start(lists["c"][:], offs2)
-        nc.sync.dma_start(lists["e"][:], offs3)
-        wa_rows = wa.rearrange("(p j) r -> p j r", j=PACK)
-        for g in range(PASSES):
-            nc.sync.dma_start(out=wa_raw[g][:], in_=wa_rows[:, :, N * g : N * (g + 1)])
-        load_scale_rows((nc.sync,), wc_s_raw, wc_scales)
-        nc.sync.dma_start(out=tab_w[:].bitcast(I32), in_=tab_words[0].rearrange("p t i -> p (t i)").bitcast(I32))
+        load_scale_rows((nc.sync, nc.scalar), tab_s, tab_scales)
         nc.sync.dma_start(out=wc_raw[:], in_=wc_words[0].bitcast(I32))
-        nc.sync.dma_start(out=we_raw[:], in_=we_words[0].rearrange("p y i -> p (y i)").bitcast(I32))
-        load_scale_rows((nc.sync,), we_s_raw, we_scales)
+        nc.sync.dma_start(lists["a"][:], offs)
+        nc.sync.dma_start(out=tab_w[:].bitcast(I32), in_=tab_words[0].rearrange("p t i -> p (t i)").bitcast(I32))
+        load_scale_rows((nc.sync,), wc_s_raw, wc_scales)
+        wa_rows = wa.rearrange("(p j) r -> p j r", j=PACK)
+        nc.sync.dma_start(out=wa_raw[0][:], in_=wa_rows[:, :, :N])
+        nc.sync.dma_start(lists["e"][:], offs3)
+        nc.sync.dma_start(out=wa_raw[1][:], in_=wa_rows[:, :, N:])
         wt_rows = wt.rearrange("(g q t i) n -> g i q t n", g=PASSES, t=PACK, i=4)
-        for g in range(PASSES):
+
+        def load_wt(g):
             for i in range(4):
                 nc.sync.dma_start(out=wt_raw[g][i:P:4, :].rearrange("q (t n) -> q t n", t=PACK), in_=wt_rows[g, i])
+
+        load_wt(0)
+        nc.sync.dma_start(out=we_raw[:], in_=we_words[0].rearrange("p y i -> p (y i)").bitcast(I32))
+        load_scale_rows((nc.sync,), we_s_raw, we_scales)
+        load_wt(1)
         nc.sync.dma_start(out=src_sb[:], in_=src.rearrange("(p t) -> p t", t=PACK))
 
         def quantise(words, scales, values):
             nc.vector.quantize_mx(out=words.bitcast(E4M3), scales=scales, in_=values)
 
-        v_s = {n: held("v_s_" + n, [P, S], U8) for n in "ace"}
-        for n in "ace":
-            nc.vector.tensor_copy(v_s[n][:], tab_s[:].indirect(lists[n][:]))
+        v_s, v_w = {}, {}
 
-        wa_bf = [held("wa_bf%d" % g, [P, PACK * N], BF16) for g in range(PASSES)]
-        wa_w = held("wa_w", [P, H], U32)
-        wa_s = held("wa_s", [P, H], U8)
-        for g in range(PASSES):
-            nc.scalar.copy(
-                out=wa_bf[g][:].rearrange("p (t q i j) -> p t q j i", t=PACK, i=4, j=PACK),
-                in_=wa_raw[g][:].rearrange("p j (q t i) -> p t q j i", t=PACK, i=4),
-            )
-        for g in range(PASSES):
-            quantise(wa_w[:, N * g : N * (g + 1)], wa_s[:, N * g : N * (g + 1)], wa_bf[g][:])
-
-        v_w = {}
+        def gather_scales(n, tile):
+            nc.vector.tensor_copy(tile[:], tab_s[:].indirect(lists[n][:]))
+            v_s[n] = tile
 
         def gather_words(n, first, words):
             halves, cols = words.shape[1] // HALF, HALF // 16
@@ -117,111 +121,129 @@ def tile_list_electrode_kinetics_transport_kernel(
             for half in range(halves):
                 v_w[n, first + half] = words[:, HALF * half : HALF * (half + 1)]
 
-        def deal(name, raw):
-            dealt = held(name, [P, raw.shape[1]], I32)
+        def deal(dealt, raw):
             nc.vector.tensor_copy(
                 out=dealt[:].rearrange("p (g t q w) -> p g t q w", g=PASSES, t=PACK, q=32),
                 in_=raw.rearrange("p (g q t w) -> p g t q w", g=PASSES, t=PACK, q=32),
             )
             return dealt
 
-        wc_s = deal("wc_s", wc_s_raw[:].bitcast(I32))
-        gather_words("a", 0, held("v_w_a0", [P, HALF], U32)[:])
-        wc_w = deal("wc_w", wc_raw[:])
+        wc_w = deal(held("wc_w", [P, H // 2], I32), wc_raw[:])
+        gather_scales("c", held("v_s_c", [P, S], U8))
+        gather_scales("a", held("v_s_a", [P, S], U8))
         gather_words("c", 0, held("v_w_c0", [P, HALF], U32)[:])
-        we_w = deal("we_w", we_raw[:])
-        we_s = deal("we_s", we_s_raw[:].bitcast(I32))
-        gather_words("a", 1, place("v_w_a1", [P, HALF], U32, AT_WC)[:])
-        late_words = place("late_words", [P, 3 * HALF], U32, AT_LATE_WORDS)
+        wc_s = deal(held("wc_s", [P, H // 4], I32), wc_s_raw[:].bitcast(I32))
+        late_words = place("late_words", [P, 5 * HALF], U32, AT_LATE + S)
         gather_words("c", 1, late_words[:, :HALF])
-        gather_words("e", 0, late_words[:, HALF:])
+        gather_words("a", 0, late_words[:, HALF : 3 * HALF])
+        gather_scales("e", place("v_s_e", [P, S], U8, AT_LATE))
+        gather_words("e", 0, late_words[:, 3 * HALF :])
 
-        def weights(n, s):
+        wa_q, we_q = {}, {}
+
+        def weights(n, g, t):
+            s = PACK * g + t
             cols = slice(P * s, P * (s + 1))
             if n == "a":
-                return wa_w[:, cols].bitcast(E4M3), wa_s[:, cols]
+                return wa_q[g][0][:, P * t : P * (t + 1)].bitcast(E4M3), wa_q[g][1][:, P * t : P * (t + 1)]
             if n == "c":
                 return (
                     wc_w[:].bitcast(U8)[:, 2 * P * s : 2 * P * (s + 1)].bitcast(E2M1),
                     wc_s[:].bitcast(U8)[:, cols],
                 )
-            return we_w[:, cols].bitcast(E4M3), we_s[:].bitcast(U8)[:, cols]
+            return we_q["w"][:, cols].bitcast(E4M3), we_q["s"][:].bitcast(U8)[:, cols]
 
-        def first_product(n, jc, g):
-            tag = "e" if n == "c" and (jc, g) in ((1, 1), (2, 0)) else n
-            bank = psum.tile([P, PACK, JC], F32, name="bank_" + tag)
+        def first_product(n, u, bank):
+            jc, g = unit_of(u)
             half, j0 = divmod(jc * JC, HALF)
             for t in range(PACK):
-                codes, scales = weights(n, PACK * g + t)
+                codes, scales = weights(n, g, t)
                 nc.tensor.matmul_mx(
-                    out=bank[:, t, :], lhsT=codes, lhsT_scale=scales,
+                    out=bank[:, JC * t : JC * (t + 1)], lhsT=codes, lhsT_scale=scales,
                     rhs=v_w[n, half][:, j0 : j0 + JC].bitcast(E4M3),
                     rhs_scale=v_s[n][:, jc * JC : (jc + 1) * JC],
                     start=True, stop=True,
                 )
-            return bank[:].rearrange("p t j -> p (t j)")
+            return bank[:]
 
         ex, diff, h_bf, h_q = {}, {}, {}, {}
 
-        def exponentials(jc, tile=None):
-            if tile is None:
-                tile = ring.tile([P, 2 * PASSES * UNIT], F32, name="exp", bufs=4)
-            ex[jc] = tile
-            order = [(g, side) for g in range(PASSES) for side in range(2)]
-            if jc == 0:
-                order = sorted(order, key=lambda pair: pair[1])
-            for g, side in order:
-                at = UNIT * (PASSES * side + g)
-                nc.scalar.activation(out=tile[:, at : at + UNIT], in_=first_product("ac"[side], jc, g), func=ACT.Exp)
+        def at_exp_a(u):
+            if u < 6:
+                return AT_A + TILE * u
+            if u < 10:
+                return AT_WT1 + TILE * (u - 6)
+            return at_exp_a(u - 8)
 
-        def subtract(engine, jc, g, target):
-            lo, width = UNIT * g, target.shape[1]
-            engine.tensor_tensor(
-                out=target, in0=ex[jc][:, lo : lo + width],
-                in1=ex[jc][:, PASSES * UNIT + lo : PASSES * UNIT + lo + width], op=ALU.subtract,
-            )
-            for more in range(width // UNIT):
-                diff[jc, g + more] = target[:, UNIT * more : UNIT * (more + 1)]
+        def exponential(n, u):
+            tile = place("exp_%s%d" % (n, u), [P, UNIT], F32, at_exp_a(u) if n == "a" else AT_C + TILE * u)
+            bank = exp_banks[len(ex) % len(exp_banks)]
+            nc.scalar.activation(out=tile[:], in_=first_product(n, u, bank), func=ACT.Exp)
+            ex[n, u] = tile
 
-        def rates(jc, g, tile=None):
-            if g == 0:
-                if tile is None:
-                    tile = ring.tile([P, PASSES * UNIT], BF16, name="h_bf", bufs=3, align_bytes=64)
-                h_bf[jc] = tile
+        def subtract(u):
+            engine = nc.gpsimd if u % 2 and u > 1 else nc.vector
+            if u > 1:
+                tile = place("diff%d" % u, [P, UNIT], F32, at_exp_a(u - 1))
+            else:
+                tile = held("diff%d" % u, [P, UNIT], F32)
+            engine.tensor_tensor(out=tile[:], in0=ex["a", u][:], in1=ex["c", u][:], op=ALU.subtract)
+            diff[u] = tile
+
+        def rates(u):
+            k, i = divmod(u, 2)
+            if i == 0:
+                if k < PAIRS - 1:
+                    h_bf[k] = place("h_bf%d" % k, [P, 2 * UNIT], BF16, AT_C + TILE * (u + 2))
+                else:
+                    h_bf[k] = held("h_bf%d" % k, [P, 2 * UNIT], BF16)
             nc.vector.tensor_tensor(
-                out=h_bf[jc][:, UNIT * g : UNIT * (g + 1)].rearrange("p (c i t) -> p c t i", i=2, t=PACK),
-                in0=diff[jc, g].rearrange("p (t c i) -> p c t i", i=2, t=PACK),
-                in1=first_product("e", jc, g).rearrange("p (t c i) -> p c t i", i=2, t=PACK),
+                out=h_bf[k][:, UNIT * i : UNIT * (i + 1)].rearrange("p (c i t) -> p c t i", i=2, t=PACK),
+                in0=diff[u][:].rearrange("p (t c i) -> p c t i", i=2, t=PACK),
+                in1=first_product("e", u, e_banks[u % len(e_banks)]).rearrange("p (t c i) -> p c t i", i=2, t=PACK),
                 op=ALU.mult,
             )
 
-        def quantise_rates(jc):
-            words = held("h_w%d" % jc, [P, PASSES * JC], U32)
-            scales = held("h_s%d" % jc, [P, PASSES * JC], U8)
-            quantise(words[:], scales[:], h_bf[jc][:])
-            h_q[jc] = (words, scales)
+        def quantise_rates(k):
+            words = held("h_w%d" % k, [P, 2 * JC], U32)
+            scales = held("h_s%d" % k, [P, 2 * JC], U8)
+            quantise(words[:], scales[:], h_bf[k][:])
+            h_q[k] = (words, scales)
 
-        wt_bf = [held("wt_bf%d" % g, [P, PACK * N], BF16) for g in range(PASSES)]
-        wt_w = held("wt_w", [P, PASSES * N], U32)
-        wt_s = held("wt_s", [P, PASSES * N], U8)
+        wa_bf = [held("wa_bf%d" % g, [P, PACK * N], BF16) for g in range(PASSES)]
+
+        def round_wa(g):
+            nc.gpsimd.tensor_scalar(
+                out=wa_bf[g][:].rearrange("p (t q i j) -> p q t i j", t=PACK, i=4, j=PACK),
+                in0=wa_raw[g][:].rearrange("p j (q t i) -> p q t i j", t=PACK, i=4),
+                scalar1=1.0, scalar2=0.0, op0=ALU.mult, op1=ALU.add,
+            )
+
+        def quantise_wa(g, words, scales):
+            quantise(words[:], scales[:], wa_bf[g][:])
+            wa_q[g] = (words, scales)
+
+        wt_bf = {}
+        wt_w = [held("wt_w%d" % g, [P, N], U32) for g in range(PASSES)]
+        wt_s = [held("wt_s%d" % g, [P, N], U8) for g in range(PASSES)]
 
         def round_wt_on_gpsimd(g):
-            dst = wt_bf[g][:].rearrange("p (t m j) -> p m t j", t=PACK, j=PACK)
-            source = wt_raw[g][:].rearrange("p (j m t) -> p m t j", j=PACK, t=PACK)
-            for m in range(0, P, P // 2):
-                nc.gpsimd.tensor_scalar(
-                    out=dst[:, m : m + P // 2], in0=source[:, m : m + P // 2],
-                    scalar1=1.0, scalar2=0.0, op0=ALU.mult, op1=ALU.add,
-                )
+            wt_bf[g] = held("wt_bf%d" % g, [P, PACK * N], BF16)
+            nc.gpsimd.tensor_scalar(
+                out=wt_bf[g][:].rearrange("p (t m j) -> p m t j", t=PACK, j=PACK),
+                in0=wt_raw[g][:].rearrange("p (j m t) -> p m t j", j=PACK, t=PACK),
+                scalar1=1.0, scalar2=0.0, op0=ALU.mult, op1=ALU.add,
+            )
 
         def round_wt_on_scalar(g):
+            wt_bf[g] = place("wt_bf%d" % g, [P, PACK * N], BF16, AT_C)
             nc.scalar.copy(
                 out=wt_bf[g][:].rearrange("p (t m j) -> p m j t", t=PACK, j=PACK),
                 in_=wt_raw[g][:].rearrange("p (j m t) -> p m j t", j=PACK, t=PACK),
             )
 
         def quantise_wt(g):
-            quantise(wt_w[:, N * g : N * (g + 1)], wt_s[:, N * g : N * (g + 1)], wt_bf[g][:])
+            quantise(wt_w[g][:], wt_s[g][:], wt_bf[g][:])
 
         y_sb, y_bf = {}, {}
         y_s = held("y_s", [P, S], U8)
@@ -229,9 +251,9 @@ def tile_list_electrode_kinetics_transport_kernel(
         out_words = out_1[0].rearrange("p m t -> p (m t)").bitcast(I32)
 
         def second_product(out, t, g, words, scales):
-            cols = slice(N * g + P * t, N * g + P * (t + 1))
+            cols = slice(P * t, P * (t + 1))
             nc.tensor.matmul_mx(
-                out=out, lhsT=wt_w[:, cols].bitcast(E4M3), lhsT_scale=wt_s[:, cols],
+                out=out, lhsT=wt_w[g][:, cols].bitcast(E4M3), lhsT_scale=wt_s[g][:, cols],
                 rhs=words.bitcast(E4M3), rhs_scale=scales, start=(g == 0), stop=(g == PASSES - 1),
             )
 
@@ -253,105 +275,121 @@ def tile_list_electrode_kinetics_transport_kernel(
             per_bank = BANK // width
             y_sb[b] = held("y_sb%d" % b, [P, PACK, width], F32)
             for t0 in range(0, PACK, per_bank):
-                bank = psum.tile([P, per_bank, width], F32, name="bank_y")
+                bank = y_banks[t0 // per_bank]
                 for t in range(t0, t0 + per_bank):
-                    for c in range(count):
-                        words, scales = h_q[first + c]
-                        for g in range(PASSES):
+                    for g in range(PASSES):
+                        if count == 2:
+                            words, scales = h_q[first + g]
+                            cols = slice(0, width)
+                        else:
+                            words, scales = h_q[first]
                             cols = slice(JC * g, JC * (g + 1))
-                            second_product(bank[:, t - t0, JC * c : JC * (c + 1)], t, g, words[:, cols], scales[:, cols])
-                add_src = add_src_on_vector if (b, t0) == BANK_ON_VECTOR else add_src_on_scalar
+                        second_product(bank[:, width * (t - t0) : width * (t - t0 + 1)], t, g, words[:, cols], scales[:, cols])
                 for t in range(t0, t0 + per_bank):
-                    add_src(b, t, bank[:, t - t0, :])
+                    add_src_on_scalar(b, t, bank[:, width * (t - t0) : width * (t - t0 + 1)])
             store_y(b)
 
         def last_transport():
-            jc = CHUNKS - 1
-            banks = []
+            k = PAIRS - 1
+            sums = exp_banks + y_banks[1:]
             for g in range(PASSES):
                 words = held("h_w_last%d" % g, [P, JC], U32)
                 scales = held("h_s_last%d" % g, [P, JC], U8)
-                quantise(words[:], scales[:], h_bf[jc][:, UNIT * g : UNIT * (g + 1)])
+                quantise(words[:], scales[:], h_bf[k][:, UNIT * g : UNIT * (g + 1)])
                 if g == PASSES - 1:
                     y_sb[LAST] = held("y_sb%d" % LAST, [P, PACK, JC], F32)
                 for t in range(PACK):
-                    if g == 0:
-                        banks.append(psum.tile([P, JC], F32, name="bank_" + "ac"[t % 2]))
-                    second_product(banks[t][:], t, g, words[:], scales[:])
+                    second_product(sums[t][:, :JC], t, g, words[:], scales[:])
                     if g == PASSES - 1:
                         add_src = add_src_on_scalar if t % 2 == 0 else add_src_on_vector
-                        add_src(LAST, t, banks[t][:])
+                        add_src(LAST, t, sums[t][:, :JC])
             store_y(LAST)
 
-        def round_y(b):
+        def round_y(b, engine):
             y_bf[b] = held("y_bf%d" % b, [P, BATCHES[b][1] * UNIT], BF16)
             dst = y_bf[b][:].rearrange("p (c i t) -> p c t i", i=4, t=PACK)
             source = y_sb[b][:].rearrange("p t (c i) -> p c t i", i=4)
-            if b in ROUNDED_ON_VECTOR:
+            if engine == "v":
                 nc.vector.tensor_copy(out=dst, in_=source)
-            else:
+            elif engine == "s":
                 nc.scalar.copy(out=dst, in_=source)
+            else:
+                nc.gpsimd.tensor_scalar(
+                    out=y_bf[b][:].rearrange("p (j t) -> p j t", t=PACK), in0=y_sb[b][:].rearrange("p t j -> p j t"),
+                    scalar1=1.0, scalar2=0.0, op0=ALU.mult, op1=ALU.add,
+                )
 
-        def quantise_y(b):
+        def quantise_y(b, at=None):
             first, count = BATCHES[b]
             cols = slice(first * JC, (first + count) * JC)
-            y_w = held("y_w%d" % b, [P, count * JC], U32)
+            if at is None:
+                y_w = held("y_w%d" % b, [P, count * JC], U32)
+            else:
+                y_w = place("y_w%d" % b, [P, count * JC], U32, at)
             quantise(y_w[:], y_s[:, cols], y_bf[b][:])
             nc.sync.dma_start(out=out_words[:, cols], in_=y_w[:].bitcast(I32))
 
-        def early_diff():
-            return ring.tile([P, UNIT], F32, name="early_diff", bufs=2)[:]
-
-        exponentials(0)
-        for g in range(PASSES):
-            subtract(nc.gpsimd, 0, g, early_diff())
-        exponentials(1)
+        for u in range(14):
+            exponential("c", u)
+        round_wa(0)
+        round_wa(1)
         round_wt_on_gpsimd(0)
-        exponentials(2)
-        rates(0, 0)
-        rates(0, 1)
-        subtract(nc.vector, 2, 0, early_diff())
-        quantise_rates(0)
-        after_wt0 = ring.tile([P, 3 * UNIT], F32, name="after_wt0", tag="stage0", align_bytes=64)
-        subtract(nc.vector, 1, 0, after_wt0[:, : 2 * UNIT])
-        subtract(nc.gpsimd, 2, 1, ex[1][:, :UNIT])
-        exponentials(3)
-        rates(1, 0)
-        rates(1, 1)
-        quantise_wt(0)
-        round_wt_on_scalar(1)
-        after_wt1 = ring.tile([P, 5 * UNIT], F32, name="after_wt1", tag="stage1", align_bytes=64)
+        quantise_wa(0, place("wa_w0", [P, N], U32, AT_WT0 + 4 * H), place("wa_s0", [P, N], U8, AT_WT0 + 7 * H))
+        quantise_wa(1, held("wa_w1", [P, N], U32), place("wa_s1", [P, N], U8, AT_WT0 + 7 * H + N))
+        we_q["w"] = deal(place("we_w", [P, H], I32, AT_WT0), we_raw[:])
+        we_q["s"] = deal(place("we_s", [P, H // 4], I32, AT_WT0 + 6 * H), we_s_raw[:].bitcast(I32))
+        for u in range(6):
+            exponential("a", u)
+        subtract(0)
+        subtract(1)
 
-        for jc in range(3, CHUNKS):
-            if jc == 3:
-                first_diff = after_wt0[:, 2 * UNIT :]
+        def step(k):
+            subtract(2 * k)
+            if k >= 2:
+                quantise_rates(k - 2)
             else:
-                first_diff = ring.tile([P, UNIT], F32, name="diff", bufs=3)[:]
-            subtract(nc.vector, jc, 0, first_diff)
-            subtract(nc.gpsimd, jc, 1, ex[jc][:, :UNIT])
-            quantise_rates(jc - 2)
-            rates(jc - 1, 0, after_wt1[:, 4 * UNIT :].bitcast(BF16) if jc == 3 else None)
-            rates(jc - 1, 1)
-            if jc == 3:
-                quantise_wt(1)
-                exponentials(4, after_wt1[:, : 4 * UNIT])
-            for lag, stage in ((3, transport), (5, quantise_y), (4, round_y)):
-                if jc >= lag and (jc - lag) % 2 == 0:
-                    stage((jc - lag) // 2)
-            if jc + 2 < CHUNKS:
-                exponentials(jc + 2)
+                quantise_wt(0)
+            subtract(2 * k + 1)
+            rates(2 * k - 2)
+            rates(2 * k - 1)
 
-        rates(CHUNKS - 1, 0)
-        quantise_rates(CHUNKS - 2)
-        rates(CHUNKS - 1, 1)
-        round_y(LAST - 2)
-        transport(LAST - 1)
+        step(1)
+        round_wt_on_scalar(1)
+        for u in range(6, 10):
+            exponential("a", u)
+        exponential("c", 14)
+        exponential("c", 15)
+        step(2)
+        exponential("a", 10)
+        quantise_wt(1)
+        step(3)
+        transport(0)
+        exponential("a", 11)
+        exponential("a", 12)
+        round_y(0, "s")
+        step(4)
+        exponential("a", 13)
+        step(5)
+        transport(1)
+        exponential("a", 14)
+        exponential("a", 15)
+        round_y(1, "s")
+        quantise_y(0, AT_C + TILE * 11)
+        step(6)
+        step(7)
+        transport(2)
+        round_y(2, "s")
+        rates(14)
+        quantise_rates(6)
+        rates(15)
+        transport(3)
         last_transport()
-        round_y(LAST - 1)
-        quantise_y(LAST - 2)
-        round_y(LAST)
-        quantise_y(LAST - 1)
+        round_y(3, "s")
+        quantise_y(1, AT_C + TILE * 15)
+        quantise_y(2)
+        round_y(LAST, "v")
         quantise_y(LAST)
+        quantise_y(3)
 
         for quad in range(4):
             queue = nc.sync if quad % 2 == 0 else nc.scalar

@@ -34,6 +34,7 @@ AT_WT0 = AT_LATE + S + 5 * TILE
 AT_WT1 = AT_WT0 + 4 * TILE
 AT_C = AT_WT1 + 4 * TILE
 AT_A = AT_C + UNITS * TILE
+AT_DIFF = AT_A + 6 * TILE
 
 
 def unit_of(u):
@@ -173,7 +174,10 @@ def tile_list_electrode_kinetics_transport_kernel(
                 return AT_A + TILE * u
             if u < 10:
                 return AT_WT1 + TILE * (u - 6)
-            return at_exp_a(u - 8)
+            return at_exp_a(u - 6 if u % 2 else u - 8)
+
+        def at_diff(u):
+            return AT_DIFF + 2 * TILE * (u // 2 % 2) + TILE // 2 + 64 * (u // 4)
 
         def exponential(n, u):
             tile = place("exp_%s%d" % (n, u), [P, UNIT], F32, at_exp_a(u) if n == "a" else AT_C + TILE * u)
@@ -183,7 +187,9 @@ def tile_list_electrode_kinetics_transport_kernel(
 
         def subtract(u):
             engine = nc.gpsimd if u % 2 and u > 1 else nc.vector
-            if u > 1:
+            if u % 2 == 0:
+                tile = place("diff%d" % u, [P, UNIT], F32, at_diff(u))
+            elif u > 1:
                 tile = place("diff%d" % u, [P, UNIT], F32, at_exp_a(u - 1))
             else:
                 tile = held("diff%d" % u, [P, UNIT], F32)
@@ -361,20 +367,20 @@ def tile_list_electrode_kinetics_transport_kernel(
         exponential("c", 15)
         step(2)
         exponential("a", 10)
+        exponential("a", 11)
         quantise_wt(1)
         step(3)
         transport(0)
-        exponential("a", 11)
         exponential("a", 12)
         round_y(0, "s")
-        step(4)
         exponential("a", 13)
-        step(5)
-        transport(1)
+        step(4)
         exponential("a", 14)
         exponential("a", 15)
+        step(5)
+        transport(1)
         round_y(1, "s")
-        quantise_y(0, AT_C + TILE * 11)
+        quantise_y(0, at_diff(8) + 64 - TILE // 2)
         step(6)
         step(7)
         transport(2)

@@ -30,11 +30,16 @@ UNITS = CHUNKS * PASSES
 PAIRS = UNITS // 2
 TILE = 4 * UNIT
 AT_LATE = 0
-AT_WT0 = AT_LATE + S + 5 * TILE
-AT_WT1 = AT_WT0 + 4 * TILE
-AT_C = AT_WT1 + 4 * TILE
+AT_C = AT_LATE + S + 3 * TILE
 AT_A = AT_C + UNITS * TILE
-AT_DIFF = AT_A + 6 * TILE
+AT_WA1 = AT_A + 6 * TILE
+AT_WA_BF = AT_WA1 + 4 * TILE
+AT_WE = AT_WA_BF + 2 * TILE
+AT_DIFF = AT_WE + 2 * TILE + 64 + TILE // 2
+AT_WT1 = AT_DIFF + TILE
+AT_A_LATE = AT_WT1 + 192
+AT_DIFF_ODD = AT_A_LATE + 4 * TILE
+AT_WT0 = AT_DIFF_ODD + TILE // 2
 
 
 def unit_of(u):
@@ -69,8 +74,10 @@ def tile_list_electrode_kinetics_transport_kernel(
         wc_s_raw = place("wc_s_raw", [P, H], U8, AT_LATE + S // 2)
         we_s_raw = held("we_s_raw", [P, H], U8)
         wc_raw = held("wc_raw", [P, H // 2], I32)
-        we_raw = held("we_raw", [P, H], I32)
-        wa_raw = [held("wa_raw%d" % g, [P, PACK, N], F32) for g in range(PASSES)]
+        we_raw = place("we_raw", [P, H], I32, AT_WE)
+        wa_cols = ((0, N // 2), (N // 2, N), (N, 2 * N))
+        wa_raw = [held("wa_raw%d" % lo, [P, PACK, hi - lo], F32) for lo, hi in wa_cols[:2]]
+        wa_raw.append(place("wa_raw_last", [P, PACK, N], F32, AT_WA1))
         wt_raw = [place("wt_raw0", [P, PACK * N], F32, AT_WT0), place("wt_raw1", [P, PACK * N], F32, AT_WT1)]
         src_sb = held("src_sb", [P, PACK], F32)
 
@@ -92,18 +99,19 @@ def tile_list_electrode_kinetics_transport_kernel(
         nc.sync.dma_start(out=tab_w[:].bitcast(I32), in_=tab_words[0].rearrange("p t i -> p (t i)").bitcast(I32))
         load_scale_rows((nc.sync,), wc_s_raw, wc_scales)
         wa_rows = wa.rearrange("(p j) r -> p j r", j=PACK)
-        nc.sync.dma_start(out=wa_raw[0][:], in_=wa_rows[:, :, :N])
-        nc.sync.dma_start(lists["e"][:], offs3)
-        nc.sync.dma_start(out=wa_raw[1][:], in_=wa_rows[:, :, N:])
+        for part, (lo, hi) in enumerate(wa_cols):
+            nc.sync.dma_start(out=wa_raw[part][:], in_=wa_rows[:, :, lo:hi])
+            if part == 1:
+                nc.sync.dma_start(lists["e"][:], offs3)
         wt_rows = wt.rearrange("(g q t i) n -> g i q t n", g=PASSES, t=PACK, i=4)
 
         def load_wt(g):
             for i in range(4):
                 nc.sync.dma_start(out=wt_raw[g][i:P:4, :].rearrange("q (t n) -> q t n", t=PACK), in_=wt_rows[g, i])
 
-        load_wt(0)
-        nc.sync.dma_start(out=we_raw[:], in_=we_words[0].rearrange("p y i -> p (y i)").bitcast(I32))
         load_scale_rows((nc.sync,), we_s_raw, we_scales)
+        nc.sync.dma_start(out=we_raw[:], in_=we_words[0].rearrange("p y i -> p (y i)").bitcast(I32))
+        load_wt(0)
         load_wt(1)
         nc.sync.dma_start(out=src_sb[:], in_=src.rearrange("(p t) -> p t", t=PACK))
 
@@ -134,11 +142,10 @@ def tile_list_electrode_kinetics_transport_kernel(
         gather_scales("a", held("v_s_a", [P, S], U8))
         gather_words("c", 0, held("v_w_c0", [P, HALF], U32)[:])
         wc_s = deal(held("wc_s", [P, H // 4], I32), wc_s_raw[:].bitcast(I32))
-        late_words = place("late_words", [P, 5 * HALF], U32, AT_LATE + S)
+        late_words = place("late_words", [P, 3 * HALF], U32, AT_LATE + S)
         gather_words("c", 1, late_words[:, :HALF])
         gather_words("a", 0, late_words[:, HALF : 3 * HALF])
         gather_scales("e", place("v_s_e", [P, S], U8, AT_LATE))
-        gather_words("e", 0, late_words[:, 3 * HALF :])
 
         wa_q, we_q = {}, {}
 
@@ -173,11 +180,11 @@ def tile_list_electrode_kinetics_transport_kernel(
             if u < 6:
                 return AT_A + TILE * u
             if u < 10:
-                return AT_WT1 + TILE * (u - 6)
+                return AT_A_LATE + TILE * (u - 6)
             return at_exp_a(u - 6 if u % 2 else u - 8)
 
         def at_diff(u):
-            return AT_DIFF + 2 * TILE * (u // 2 % 2) + TILE // 2 + 64 * (u // 4)
+            return (AT_DIFF_ODD if u // 2 % 2 else AT_DIFF) + 64 * (u // 4)
 
         def exponential(n, u):
             tile = place("exp_%s%d" % (n, u), [P, UNIT], F32, at_exp_a(u) if n == "a" else AT_C + TILE * u)
@@ -216,12 +223,14 @@ def tile_list_electrode_kinetics_transport_kernel(
             quantise(words[:], scales[:], h_bf[k][:])
             h_q[k] = (words, scales)
 
-        wa_bf = [held("wa_bf%d" % g, [P, PACK * N], BF16) for g in range(PASSES)]
+        wa_bf = [held("wa_bf0", [P, PACK * N], BF16), place("wa_bf1", [P, PACK * N], BF16, AT_WA_BF)]
 
-        def round_wa(g):
+        def round_wa(part):
+            lo, hi = wa_cols[part]
+            g, q0 = lo // N, lo % N // 16
             nc.gpsimd.tensor_scalar(
-                out=wa_bf[g][:].rearrange("p (t q i j) -> p q t i j", t=PACK, i=4, j=PACK),
-                in0=wa_raw[g][:].rearrange("p j (q t i) -> p q t i j", t=PACK, i=4),
+                out=wa_bf[g][:].rearrange("p (t q i j) -> p q t i j", t=PACK, i=4, j=PACK)[:, q0 : q0 + (hi - lo) // 16],
+                in0=wa_raw[part][:].rearrange("p j (q t i) -> p q t i j", t=PACK, i=4),
                 scalar1=1.0, scalar2=0.0, op0=ALU.mult, op1=ALU.add,
             )
 
@@ -234,7 +243,7 @@ def tile_list_electrode_kinetics_transport_kernel(
         wt_s = [held("wt_s%d" % g, [P, N], U8) for g in range(PASSES)]
 
         def round_wt_on_gpsimd(g):
-            wt_bf[g] = held("wt_bf%d" % g, [P, PACK * N], BF16)
+            wt_bf[g] = place("wt_bf%d" % g, [P, PACK * N], BF16, AT_WE + 64)
             nc.gpsimd.tensor_scalar(
                 out=wt_bf[g][:].rearrange("p (t m j) -> p m t j", t=PACK, j=PACK),
                 in0=wt_raw[g][:].rearrange("p (j m t) -> p m t j", j=PACK, t=PACK),
@@ -335,15 +344,16 @@ def tile_list_electrode_kinetics_transport_kernel(
             quantise(y_w[:], y_s[:, cols], y_bf[b][:])
             nc.sync.dma_start(out=out_words[:, cols], in_=y_w[:].bitcast(I32))
 
-        for u in range(14):
+        for u in range(12):
             exponential("c", u)
-        round_wa(0)
-        round_wa(1)
+        for part in range(len(wa_cols)):
+            round_wa(part)
+        quantise_wa(0, place("wa_w0", [P, N], U32, AT_WA1 + 4 * H), place("wa_s0", [P, N], U8, AT_WA1 + 7 * H))
+        quantise_wa(1, held("wa_w1", [P, N], U32), place("wa_s1", [P, N], U8, AT_WA1 + 7 * H + N))
+        we_q["s"] = deal(place("we_s", [P, H // 4], I32, AT_WA1 + 6 * H), we_s_raw[:].bitcast(I32))
+        we_q["w"] = deal(place("we_w", [P, H], I32, AT_WA1), we_raw[:])
+        gather_words("e", 0, place("v_w_e", [P, S], U32, AT_WA_BF + 64)[:])
         round_wt_on_gpsimd(0)
-        quantise_wa(0, place("wa_w0", [P, N], U32, AT_WT0 + 4 * H), place("wa_s0", [P, N], U8, AT_WT0 + 7 * H))
-        quantise_wa(1, held("wa_w1", [P, N], U32), place("wa_s1", [P, N], U8, AT_WT0 + 7 * H + N))
-        we_q["w"] = deal(place("we_w", [P, H], I32, AT_WT0), we_raw[:])
-        we_q["s"] = deal(place("we_s", [P, H // 4], I32, AT_WT0 + 6 * H), we_s_raw[:].bitcast(I32))
         for u in range(6):
             exponential("a", u)
         subtract(0)
@@ -363,8 +373,8 @@ def tile_list_electrode_kinetics_transport_kernel(
         round_wt_on_scalar(1)
         for u in range(6, 10):
             exponential("a", u)
-        exponential("c", 14)
-        exponential("c", 15)
+        for u in range(12, UNITS):
+            exponential("c", u)
         step(2)
         exponential("a", 10)
         exponential("a", 11)

@@ -30,16 +30,17 @@ UNITS = CHUNKS * PASSES
 PAIRS = UNITS // 2
 TILE = 4 * UNIT
 AT_LATE = 0
+PAIR = 2 * TILE
 AT_C = AT_LATE + S + 3 * TILE
-AT_A = AT_C + UNITS * TILE
-AT_WA1 = AT_A + 6 * TILE
-AT_WA_BF = AT_WA1 + 4 * TILE
-AT_WE = AT_WA_BF + 2 * TILE
-AT_DIFF = AT_WE + 2 * TILE + 64 + TILE // 2
-AT_WT1 = AT_DIFF + TILE
-AT_A_LATE = AT_WT1 + 192
-AT_DIFF_ODD = AT_A_LATE + 4 * TILE
-AT_WT0 = AT_DIFF_ODD + TILE // 2
+AT_A = AT_C + PAIRS * PAIR
+AT_WA1 = AT_A + 3 * PAIR
+AT_WA_BF = AT_WA1 + 2 * PAIR
+AT_WE = AT_WA_BF + PAIR
+AT_H0 = AT_WE + PAIR + 64
+AT_WT1 = AT_H0 + PAIR - 64
+AT_WT0 = AT_WT1 + 2 * PAIR + 64
+AT_EXP_A = (AT_A, AT_A + PAIR, AT_A + 2 * PAIR, AT_WT1 + 64, AT_WT1 + 64 + PAIR, AT_A, AT_A + 2 * PAIR, AT_WT0 + PAIR)
+AT_DIFF = (AT_WE + 64, AT_WT0, AT_EXP_A[1], AT_WE + 64, AT_EXP_A[3], AT_EXP_A[1], AT_EXP_A[5], AT_EXP_A[3] + 64)
 
 
 def unit_of(u):
@@ -91,7 +92,7 @@ def tile_list_electrode_kinetics_transport_kernel(
         nc.vector.memset(tab_s[:, : T // 2].bitcast(I32), 0)
         nc.gpsimd.memset(tab_s[:, T // 2 :].bitcast(I32), 0)
         for plane in (wc_s_raw, we_s_raw):
-            nc.gpsimd.memset(plane[:].bitcast(I32), 0)
+            nc.vector.memset(plane[:].bitcast(I32), 0)
         nc.sync.dma_start(lists["c"][:], offs2)
         load_scale_rows((nc.sync, nc.scalar), tab_s, tab_scales)
         nc.sync.dma_start(out=wc_raw[:], in_=wc_words[0].bitcast(I32))
@@ -176,52 +177,50 @@ def tile_list_electrode_kinetics_transport_kernel(
 
         ex, diff, h_bf, h_q = {}, {}, {}, {}
 
-        def at_exp_a(u):
-            if u < 6:
-                return AT_A + TILE * u
-            if u < 10:
-                return AT_A_LATE + TILE * (u - 6)
-            return at_exp_a(u - 6 if u % 2 else u - 8)
-
-        def at_diff(u):
-            return (AT_DIFF_ODD if u // 2 % 2 else AT_DIFF) + 64 * (u // 4)
+        done = []
 
         def exponential(n, u):
-            tile = place("exp_%s%d" % (n, u), [P, UNIT], F32, at_exp_a(u) if n == "a" else AT_C + TILE * u)
-            bank = exp_banks[len(ex) % len(exp_banks)]
-            nc.scalar.activation(out=tile[:], in_=first_product(n, u, bank), func=ACT.Exp)
-            ex[n, u] = tile
-
-        def subtract(u):
-            engine = nc.gpsimd if u % 2 and u > 1 else nc.vector
-            if u % 2 == 0:
-                tile = place("diff%d" % u, [P, UNIT], F32, at_diff(u))
-            elif u > 1:
-                tile = place("diff%d" % u, [P, UNIT], F32, at_exp_a(u - 1))
-            else:
-                tile = held("diff%d" % u, [P, UNIT], F32)
-            engine.tensor_tensor(out=tile[:], in0=ex["a", u][:], in1=ex["c", u][:], op=ALU.subtract)
-            diff[u] = tile
-
-        def rates(u):
             k, i = divmod(u, 2)
             if i == 0:
-                if k < PAIRS - 1:
-                    h_bf[k] = place("h_bf%d" % k, [P, 2 * UNIT], BF16, AT_C + TILE * (u + 2))
-                else:
-                    h_bf[k] = held("h_bf%d" % k, [P, 2 * UNIT], BF16)
+                ex[n, k] = place("exp_%s%d" % (n, k), [P, 2 * UNIT], F32, AT_EXP_A[k] if n == "a" else AT_C + PAIR * k)
+            if n == "a" and 3 <= u < 6:
+                bank = e_banks[u - 3]
+            else:
+                bank = exp_banks[len(done) % len(exp_banks)]
+            nc.scalar.activation(
+                out=ex[n, k][:, UNIT * i : UNIT * (i + 1)], in_=first_product(n, u, bank), func=ACT.Exp
+            )
+            done.append(u)
+
+        def subtract(engine, first, count, target):
+            k, at = first // 2, first % 2 * UNIT
+            cols = slice(at, at + count * UNIT)
+            engine.tensor_tensor(out=target, in0=ex["a", k][:, cols], in1=ex["c", k][:, cols], op=ALU.subtract)
+            for i in range(count):
+                diff[first + i] = target[:, UNIT * i : UNIT * (i + 1)]
+
+        def diff_tile(k):
+            return place("diff%d" % k, [P, 2 * UNIT], F32, AT_DIFF[k])
+
+        def rates(u):
+            m, i = divmod(u, 4)
+            if i == 0:
+                h_bf[m] = place("h_bf%d" % m, [P, 4 * UNIT], BF16, (AT_H0, AT_C + 3 * PAIR, AT_C + 5 * PAIR, AT_C + 6 * PAIR)[m])
             nc.vector.tensor_tensor(
-                out=h_bf[k][:, UNIT * i : UNIT * (i + 1)].rearrange("p (c i t) -> p c t i", i=2, t=PACK),
-                in0=diff[u][:].rearrange("p (t c i) -> p c t i", i=2, t=PACK),
+                out=h_bf[m][:, UNIT * i : UNIT * (i + 1)].rearrange("p (c i t) -> p c t i", i=2, t=PACK),
+                in0=diff[u].rearrange("p (t c i) -> p c t i", i=2, t=PACK),
                 in1=first_product("e", u, e_banks[u % len(e_banks)]).rearrange("p (t c i) -> p c t i", i=2, t=PACK),
                 op=ALU.mult,
             )
 
-        def quantise_rates(k):
-            words = held("h_w%d" % k, [P, 2 * JC], U32)
-            scales = held("h_s%d" % k, [P, 2 * JC], U8)
-            quantise(words[:], scales[:], h_bf[k][:])
-            h_q[k] = (words, scales)
+        def quantise_rates(first, count):
+            words = held("h_w%d" % first, [P, count * JC], U32)
+            scales = held("h_s%d" % first, [P, count * JC], U8)
+            at = first % 4 * UNIT
+            quantise(words[:], scales[:], h_bf[first // 4][:, at : at + count * UNIT])
+            for i in range(0, count, 2):
+                cols = slice(JC * i, JC * min(i + 2, count))
+                h_q[first + i] = (words[:, cols], scales[:, cols])
 
         wa_bf = [held("wa_bf0", [P, PACK * N], BF16), place("wa_bf1", [P, PACK * N], BF16, AT_WA_BF)]
 
@@ -242,12 +241,11 @@ def tile_list_electrode_kinetics_transport_kernel(
         wt_w = [held("wt_w%d" % g, [P, N], U32) for g in range(PASSES)]
         wt_s = [held("wt_s%d" % g, [P, N], U8) for g in range(PASSES)]
 
-        def round_wt_on_gpsimd(g):
-            wt_bf[g] = place("wt_bf%d" % g, [P, PACK * N], BF16, AT_WE + 64)
-            nc.gpsimd.tensor_scalar(
+        def round_wt_on_vector(g):
+            wt_bf[g] = held("wt_bf%d" % g, [P, PACK * N], BF16)
+            nc.vector.tensor_copy(
                 out=wt_bf[g][:].rearrange("p (t m j) -> p m t j", t=PACK, j=PACK),
-                in0=wt_raw[g][:].rearrange("p (j m t) -> p m t j", j=PACK, t=PACK),
-                scalar1=1.0, scalar2=0.0, op0=ALU.mult, op1=ALU.add,
+                in_=wt_raw[g][:].rearrange("p (j m t) -> p m t j", j=PACK, t=PACK),
             )
 
         def round_wt_on_scalar(g):
@@ -294,10 +292,10 @@ def tile_list_electrode_kinetics_transport_kernel(
                 for t in range(t0, t0 + per_bank):
                     for g in range(PASSES):
                         if count == 2:
-                            words, scales = h_q[first + g]
+                            words, scales = h_q[2 * (first + g)]
                             cols = slice(0, width)
                         else:
-                            words, scales = h_q[first]
+                            words, scales = h_q[2 * first]
                             cols = slice(JC * g, JC * (g + 1))
                         second_product(bank[:, width * (t - t0) : width * (t - t0 + 1)], t, g, words[:, cols], scales[:, cols])
                 for t in range(t0, t0 + per_bank):
@@ -305,16 +303,14 @@ def tile_list_electrode_kinetics_transport_kernel(
             store_y(b)
 
         def last_transport():
-            k = PAIRS - 1
             sums = exp_banks + y_banks[1:]
             for g in range(PASSES):
-                words = held("h_w_last%d" % g, [P, JC], U32)
-                scales = held("h_s_last%d" % g, [P, JC], U8)
-                quantise(words[:], scales[:], h_bf[k][:, UNIT * g : UNIT * (g + 1)])
+                quantise_rates(UNITS - PASSES + g, 1)
+                words, scales = h_q[UNITS - PASSES + g]
                 if g == PASSES - 1:
                     y_sb[LAST] = held("y_sb%d" % LAST, [P, PACK, JC], F32)
                 for t in range(PACK):
-                    second_product(sums[t][:, :JC], t, g, words[:], scales[:])
+                    second_product(sums[t][:, :JC], t, g, words, scales)
                     if g == PASSES - 1:
                         add_src = add_src_on_scalar if t % 2 == 0 else add_src_on_vector
                         add_src(LAST, t, sums[t][:, :JC])
@@ -344,7 +340,7 @@ def tile_list_electrode_kinetics_transport_kernel(
             quantise(y_w[:], y_s[:, cols], y_bf[b][:])
             nc.sync.dma_start(out=out_words[:, cols], in_=y_w[:].bitcast(I32))
 
-        for u in range(12):
+        for u in range(11):
             exponential("c", u)
         for part in range(len(wa_cols)):
             round_wa(part)
@@ -353,55 +349,62 @@ def tile_list_electrode_kinetics_transport_kernel(
         we_q["s"] = deal(place("we_s", [P, H // 4], I32, AT_WA1 + 6 * H), we_s_raw[:].bitcast(I32))
         we_q["w"] = deal(place("we_w", [P, H], I32, AT_WA1), we_raw[:])
         gather_words("e", 0, place("v_w_e", [P, S], U32, AT_WA_BF + 64)[:])
-        round_wt_on_gpsimd(0)
         for u in range(6):
             exponential("a", u)
-        subtract(0)
-        subtract(1)
-
-        def step(k):
-            subtract(2 * k)
-            if k >= 2:
-                quantise_rates(k - 2)
-            else:
-                quantise_wt(0)
-            subtract(2 * k + 1)
-            rates(2 * k - 2)
-            rates(2 * k - 1)
-
-        step(1)
+        first_diff = diff_tile(0)
+        for u in range(2):
+            subtract(nc.gpsimd, u, 1, first_diff[:, UNIT * u : UNIT * (u + 1)])
+        round_wt_on_vector(0)
+        subtract(nc.vector, 2, 2, diff_tile(1)[:])
+        quantise_wt(0)
+        subtract(nc.gpsimd, 4, 2, diff_tile(2)[:])
         round_wt_on_scalar(1)
+        for u in range(4):
+            rates(u)
         for u in range(6, 10):
             exponential("a", u)
-        for u in range(12, UNITS):
-            exponential("c", u)
-        step(2)
+        exponential("c", 11)
         exponential("a", 10)
         exponential("a", 11)
+        exponential("c", 12)
+        exponential("c", 13)
+
+        def step(m):
+            if m < 3:
+                subtract(nc.vector, 4 * m + 2, 2, diff_tile(2 * m + 1)[:])
+            else:
+                subtract(nc.vector, 4 * m + 2, 1, diff_tile(2 * m + 1)[:, :UNIT])
+            quantise_rates(4 * m - 4, 4)
+            if m < 3:
+                subtract(nc.gpsimd, 4 * m + 4, 2, diff_tile(2 * m + 2)[:])
+            else:
+                subtract(nc.gpsimd, 4 * m + 3, 1, ex["a", 2 * m + 1][:, :UNIT])
+            for u in range(4 * m, min(4 * m + 4, UNITS - 1)):
+                rates(u)
+
         quantise_wt(1)
-        step(3)
+        step(1)
         transport(0)
         exponential("a", 12)
-        round_y(0, "s")
         exponential("a", 13)
-        step(4)
+        round_y(0, "s")
+        exponential("c", 14)
+        exponential("c", 15)
         exponential("a", 14)
         exponential("a", 15)
-        step(5)
+        step(2)
         transport(1)
         round_y(1, "s")
-        quantise_y(0, at_diff(8) + 64 - TILE // 2)
-        step(6)
-        step(7)
+        quantise_y(0, AT_EXP_A[3] + 64 - TILE // 2)
+        step(3)
         transport(2)
         round_y(2, "s")
-        rates(14)
-        quantise_rates(6)
+        quantise_rates(12, 2)
         rates(15)
         transport(3)
         last_transport()
         round_y(3, "s")
-        quantise_y(1, AT_C + TILE * 15)
+        quantise_y(1, AT_EXP_A[5])
         quantise_y(2)
         round_y(LAST, "v")
         quantise_y(LAST)

@@ -40,7 +40,7 @@ AT_H0 = AT_WE + PAIR + 64
 AT_WT1 = AT_H0 + PAIR - 64
 AT_WT0 = AT_WT1 + 2 * PAIR + 64
 AT_EXP_A = (AT_A, AT_A + PAIR, AT_A + 2 * PAIR, AT_WT1 + 64, AT_WT1 + 64 + PAIR, AT_A, AT_A + 2 * PAIR, AT_WT0 + PAIR)
-AT_DIFF = (AT_WE + 64, AT_WT0, AT_EXP_A[1], AT_WE + 64, AT_EXP_A[3], AT_EXP_A[1], AT_EXP_A[5], AT_EXP_A[3] + 64)
+AT_DIFF = (AT_WE + 64, AT_WT0, AT_EXP_A[1], AT_C, AT_EXP_A[3], AT_C, AT_EXP_A[5], AT_WE + 64)
 
 
 def unit_of(u):
@@ -67,7 +67,7 @@ def tile_list_electrode_kinetics_transport_kernel(
             return placed.tile(shape, dtype, name=name, offset=offset, align_bytes=64)
 
         banks = [psum.tile([P, BANK], F32, name="bank%d" % b) for b in range(8)]
-        exp_banks, e_banks, y_banks = banks[0:3], banks[3:6], banks[6:8]
+        exp_banks, e_banks, y_banks = banks[0:2], banks[2:6], banks[6:8]
 
         lists = {n: held("list_" + n, [P, S // 16], U16) for n in "ace"}
         tab_w = held("tab_w", [P, T], U32)
@@ -183,8 +183,10 @@ def tile_list_electrode_kinetics_transport_kernel(
             k, i = divmod(u, 2)
             if i == 0:
                 ex[n, k] = place("exp_%s%d" % (n, k), [P, 2 * UNIT], F32, AT_EXP_A[k] if n == "a" else AT_C + PAIR * k)
-            if n == "a" and 3 <= u < 6:
-                bank = e_banks[u - 3]
+            if n == "a" and 2 <= u < 6:
+                bank = e_banks[u - 2]
+            elif len(done) < 11 and len(done) % 4 > 1:
+                bank = y_banks[len(done) % 2]
             else:
                 bank = exp_banks[len(done) % len(exp_banks)]
             nc.scalar.activation(
@@ -238,14 +240,14 @@ def tile_list_electrode_kinetics_transport_kernel(
             wa_q[g] = (words, scales)
 
         wt_bf = {}
-        wt_w = [held("wt_w%d" % g, [P, N], U32) for g in range(PASSES)]
+        wt_w = {}
         wt_s = [held("wt_s%d" % g, [P, N], U8) for g in range(PASSES)]
 
         def round_wt_on_vector(g):
             wt_bf[g] = held("wt_bf%d" % g, [P, PACK * N], BF16)
             nc.vector.tensor_copy(
-                out=wt_bf[g][:].rearrange("p (t m j) -> p m t j", t=PACK, j=PACK),
-                in_=wt_raw[g][:].rearrange("p (j m t) -> p m t j", j=PACK, t=PACK),
+                out=wt_bf[g][:].rearrange("p (t m j) -> p m j t", t=PACK, j=PACK),
+                in_=wt_raw[g][:].rearrange("p (j m t) -> p m j t", j=PACK, t=PACK),
             )
 
         def round_wt_on_scalar(g):
@@ -256,6 +258,7 @@ def tile_list_electrode_kinetics_transport_kernel(
             )
 
         def quantise_wt(g):
+            wt_w[g] = place("wt_w1", [P, N], U32, AT_DIFF[1]) if g else held("wt_w0", [P, N], U32)
             quantise(wt_w[g][:], wt_s[g][:], wt_bf[g][:])
 
         y_sb, y_bf = {}, {}
@@ -303,7 +306,7 @@ def tile_list_electrode_kinetics_transport_kernel(
             store_y(b)
 
         def last_transport():
-            sums = exp_banks + y_banks[1:]
+            sums = exp_banks + e_banks[:2]
             for g in range(PASSES):
                 quantise_rates(UNITS - PASSES + g, 1)
                 words, scales = h_q[UNITS - PASSES + g]
@@ -317,7 +320,10 @@ def tile_list_electrode_kinetics_transport_kernel(
             store_y(LAST)
 
         def round_y(b, engine):
-            y_bf[b] = held("y_bf%d" % b, [P, BATCHES[b][1] * UNIT], BF16)
+            if b:
+                y_bf[b] = held("y_bf%d" % b, [P, BATCHES[b][1] * UNIT], BF16)
+            else:
+                y_bf[b] = place("y_bf%d" % b, [P, BATCHES[b][1] * UNIT], BF16, AT_DIFF[7])
             dst = y_bf[b][:].rearrange("p (c i t) -> p c t i", i=4, t=PACK)
             source = y_sb[b][:].rearrange("p t (c i) -> p c t i", i=4)
             if engine == "v":
@@ -395,7 +401,7 @@ def tile_list_electrode_kinetics_transport_kernel(
         step(2)
         transport(1)
         round_y(1, "s")
-        quantise_y(0, AT_EXP_A[3] + 64 - TILE // 2)
+        quantise_y(0, AT_DIFF[5])
         step(3)
         transport(2)
         round_y(2, "s")

@@ -24,30 +24,58 @@ CHUNKS = S // JC
 HALF = S // 2
 PASSES = H // (P * PACK)
 UNIT = JC * PACK
+UNITS = CHUNKS * PASSES
+STEP = 4
 BATCHES = ((0, 2), (2, 2), (4, 2), (6, 1), (7, 1))
 LAST = len(BATCHES) - 1
-UNITS = CHUNKS * PASSES
-PAIRS = UNITS // 2
+EARLY_C = 11
+EARLY_A = 6
+WA_LOADS = ((0, N // 2), (N // 2, N), (N, 2 * N))
+
+EDGE = 64
 TILE = 4 * UNIT
-AT_LATE = 0
 PAIR = 2 * TILE
-AT_C = AT_LATE + S + 3 * TILE
-AT_A = AT_C + PAIRS * PAIR
-AT_WA1 = AT_A + 3 * PAIR
-AT_WA_BF = AT_WA1 + 2 * PAIR
-AT_WE = AT_WA_BF + PAIR
-AT_H0 = AT_WE + PAIR + 64
-AT_WT1 = AT_H0 + PAIR - 64
-AT_WT0 = AT_WT1 + 2 * PAIR + 64
-AT_EXP_A = (AT_A, AT_A + PAIR, AT_A + 2 * PAIR, AT_WT1 + 64, AT_WT1 + 64 + PAIR, AT_A, AT_A + 2 * PAIR, AT_WT0 + PAIR)
-AT_DIFF = (AT_WE + 64, AT_WT0, AT_EXP_A[1], AT_C, AT_EXP_A[3], AT_C, AT_EXP_A[5], AT_WE + 64)
+AT_WA_BF0 = 0
+AT_E_SCALES = AT_WA_BF0 + PAIR
+AT_WORDS = AT_E_SCALES + S
+AT_WC_SCALES = AT_E_SCALES - EDGE
+AT_TAB = AT_WORDS + 4 * TILE
+AT_WA1 = AT_TAB + 4 * T
+AT_WA_BF1 = AT_WA1 + 2 * PAIR
+AT_WE = AT_WA_BF1 + PAIR
+AT_E_WORDS = AT_WA_BF1 + EDGE
+AT_WT_BF0 = AT_WE + EDGE
+AT_A1 = AT_WT_BF0 + PAIR
+AT_H0 = AT_A1 + PAIR
+AT_A3 = AT_H0 + PAIR
+AT_WT1 = AT_A3 - EDGE
+AT_WT0 = AT_A3 + 2 * PAIR
+AT_C0 = AT_WT0 + 2 * PAIR
+AT_A5 = AT_C0 + 4 * PAIR
+AT_C4 = AT_A5 + PAIR
+AT_A14 = AT_C4 + 2 * PAIR
+AT_C6 = AT_A14 + TILE
+AT_C14 = AT_C6 + PAIR
+AT_A0 = AT_C14 + PAIR
+AT_A2 = AT_A0 + PAIR
+AT_A15 = AT_A2 + PAIR
+AT_EXP = {
+    "a": {0: AT_A0, 2: AT_A1, 4: AT_A2, 6: AT_A3, 8: AT_A3 + PAIR, 10: AT_A5, 12: AT_A2, 14: AT_A14, 15: AT_A15},
+    "c": {0: AT_C0, 2: AT_C0 + PAIR, 4: AT_C0 + 2 * PAIR, 6: AT_C0 + 3 * PAIR, 8: AT_C4, 10: AT_C4 + PAIR, 12: AT_C6,
+          14: AT_C14, 15: AT_C14 + TILE},
+}
+AT_H = (AT_H0, AT_EXP["c"][6], AT_EXP["c"][10], AT_C14 - TILE)
+AT_DIFF = {
+    0: AT_WT0, 2: AT_WT0 + PAIR, 4: AT_A1 - TILE, 6: AT_TAB, 8: AT_A3 - TILE, 10: AT_TAB, 12: AT_A5 - TILE, 14: AT_A0,
+    15: AT_A14 - TILE // 2,
+}
 
 
 def unit_of(u):
-    k, i = divmod(u, 2)
-    if k < PAIRS - 2:
-        return 2 * (k // 2) + i, k % 2
-    return k, i
+    pair, i = divmod(u, 2)
+    if pair < BATCHES[LAST - 1][0]:
+        return 2 * (pair // 2) + i, pair % 2
+    return pair, i
 
 
 def tile_list_electrode_kinetics_transport_kernel(
@@ -70,14 +98,13 @@ def tile_list_electrode_kinetics_transport_kernel(
         exp_banks, e_banks, y_banks = banks[0:2], banks[2:6], banks[6:8]
 
         lists = {n: held("list_" + n, [P, S // 16], U16) for n in "ace"}
-        tab_w = held("tab_w", [P, T], U32)
+        tab_w = place("tab_w", [P, T], U32, AT_TAB)
         tab_s = held("tab_s", [P, T], U8)
-        wc_s_raw = place("wc_s_raw", [P, H], U8, AT_LATE + S // 2)
-        we_s_raw = held("we_s_raw", [P, H], U8)
+        wc_s_raw = place("wc_s_raw", [P, H + 2 * EDGE], U8, AT_WC_SCALES)[:, :H]
+        we_s_raw = held("we_s_raw", [P, H], U8)[:]
         wc_raw = held("wc_raw", [P, H // 2], I32)
         we_raw = place("we_raw", [P, H], I32, AT_WE)
-        wa_cols = ((0, N // 2), (N // 2, N), (N, 2 * N))
-        wa_raw = [held("wa_raw%d" % lo, [P, PACK, hi - lo], F32) for lo, hi in wa_cols[:2]]
+        wa_raw = [held("wa_raw%d" % lo, [P, PACK, hi - lo], F32) for lo, hi in WA_LOADS[:-1]]
         wa_raw.append(place("wa_raw_last", [P, PACK, N], F32, AT_WA1))
         wt_raw = [place("wt_raw0", [P, PACK * N], F32, AT_WT0), place("wt_raw1", [P, PACK * N], F32, AT_WT1)]
         src_sb = held("src_sb", [P, PACK], F32)
@@ -92,7 +119,7 @@ def tile_list_electrode_kinetics_transport_kernel(
         nc.vector.memset(tab_s[:, : T // 2].bitcast(I32), 0)
         nc.gpsimd.memset(tab_s[:, T // 2 :].bitcast(I32), 0)
         for plane in (wc_s_raw, we_s_raw):
-            nc.vector.memset(plane[:].bitcast(I32), 0)
+            nc.vector.memset(plane.bitcast(I32), 0)
         nc.sync.dma_start(lists["c"][:], offs2)
         load_scale_rows((nc.sync, nc.scalar), tab_s, tab_scales)
         nc.sync.dma_start(out=wc_raw[:], in_=wc_words[0].bitcast(I32))
@@ -100,20 +127,16 @@ def tile_list_electrode_kinetics_transport_kernel(
         nc.sync.dma_start(out=tab_w[:].bitcast(I32), in_=tab_words[0].rearrange("p t i -> p (t i)").bitcast(I32))
         load_scale_rows((nc.sync,), wc_s_raw, wc_scales)
         wa_rows = wa.rearrange("(p j) r -> p j r", j=PACK)
-        for part, (lo, hi) in enumerate(wa_cols):
+        for part, (lo, hi) in enumerate(WA_LOADS):
             nc.sync.dma_start(out=wa_raw[part][:], in_=wa_rows[:, :, lo:hi])
-            if part == 1:
+            if hi == N:
                 nc.sync.dma_start(lists["e"][:], offs3)
-        wt_rows = wt.rearrange("(g q t i) n -> g i q t n", g=PASSES, t=PACK, i=4)
-
-        def load_wt(g):
-            for i in range(4):
-                nc.sync.dma_start(out=wt_raw[g][i:P:4, :].rearrange("q (t n) -> q t n", t=PACK), in_=wt_rows[g, i])
-
         load_scale_rows((nc.sync,), we_s_raw, we_scales)
         nc.sync.dma_start(out=we_raw[:], in_=we_words[0].rearrange("p y i -> p (y i)").bitcast(I32))
-        load_wt(0)
-        load_wt(1)
+        wt_rows = wt.rearrange("(g q t i) n -> g i q t n", g=PASSES, t=PACK, i=4)
+        for g in range(PASSES):
+            for i in range(4):
+                nc.sync.dma_start(out=wt_raw[g][i:P:4, :].rearrange("q (t n) -> q t n", t=PACK), in_=wt_rows[g, i])
         nc.sync.dma_start(out=src_sb[:], in_=src.rearrange("(p t) -> p t", t=PACK))
 
         def quantise(words, scales, values):
@@ -141,12 +164,12 @@ def tile_list_electrode_kinetics_transport_kernel(
         wc_w = deal(held("wc_w", [P, H // 2], I32), wc_raw[:])
         gather_scales("c", held("v_s_c", [P, S], U8))
         gather_scales("a", held("v_s_a", [P, S], U8))
-        gather_words("c", 0, held("v_w_c0", [P, HALF], U32)[:])
-        wc_s = deal(held("wc_s", [P, H // 4], I32), wc_s_raw[:].bitcast(I32))
-        late_words = place("late_words", [P, 3 * HALF], U32, AT_LATE + S)
-        gather_words("c", 1, late_words[:, :HALF])
-        gather_words("a", 0, late_words[:, HALF : 3 * HALF])
-        gather_scales("e", place("v_s_e", [P, S], U8, AT_LATE))
+        wc_s = deal(held("wc_s", [P, H // 4], I32), wc_s_raw.bitcast(I32))
+        v_w_ca = place("v_w_ca", [P, 2 * S], U32, AT_WORDS)
+        gather_words("c", 0, v_w_ca[:, :HALF])
+        gather_words("c", 1, v_w_ca[:, HALF:S])
+        gather_words("a", 0, v_w_ca[:, S:])
+        gather_scales("e", place("v_s_e", [P, S], U8, AT_E_SCALES))
 
         wa_q, we_q = {}, {}
 
@@ -177,60 +200,55 @@ def tile_list_electrode_kinetics_transport_kernel(
 
         ex, diff, h_bf, h_q = {}, {}, {}, {}
 
-        done = []
-
         def exponential(n, u):
-            k, i = divmod(u, 2)
-            if i == 0:
-                ex[n, k] = place("exp_%s%d" % (n, k), [P, 2 * UNIT], F32, AT_EXP_A[k] if n == "a" else AT_C + PAIR * k)
-            if n == "a" and 2 <= u < 6:
-                bank = e_banks[u - 2]
-            elif len(done) < 11 and len(done) % 4 > 1:
-                bank = y_banks[len(done) % 2]
+            count = len(ex)
+            if u in AT_EXP[n]:
+                width = UNIT if u >= UNITS - 2 else 2 * UNIT
+                ex[n, u] = place("exp_%s%d" % (n, u), [P, width], F32, AT_EXP[n][u])[:]
             else:
-                bank = exp_banks[len(done) % len(exp_banks)]
-            nc.scalar.activation(
-                out=ex[n, k][:, UNIT * i : UNIT * (i + 1)], in_=first_product(n, u, bank), func=ACT.Exp
-            )
-            done.append(u)
+                ex[n, u] = ex[n, u - 1][:, UNIT:]
+            if n == "a" and EARLY_A - STEP <= u < EARLY_A:
+                bank = e_banks[u - (EARLY_A - STEP)]
+            elif count < EARLY_C:
+                bank = (exp_banks + y_banks)[count % 4]
+            else:
+                bank = exp_banks[count % 2]
+            nc.scalar.activation(out=ex[n, u][:, :UNIT], in_=first_product(n, u, bank), func=ACT.Exp)
 
-        def subtract(engine, first, count, target):
-            k, at = first // 2, first % 2 * UNIT
-            cols = slice(at, at + count * UNIT)
-            engine.tensor_tensor(out=target, in0=ex["a", k][:, cols], in1=ex["c", k][:, cols], op=ALU.subtract)
-            for i in range(count):
+        def subtract(engine, first):
+            width = ex["a", first].shape[1]
+            target = place("diff%d" % first, [P, width], F32, AT_DIFF[first])
+            engine.tensor_tensor(out=target[:], in0=ex["a", first], in1=ex["c", first], op=ALU.subtract)
+            for i in range(width // UNIT):
                 diff[first + i] = target[:, UNIT * i : UNIT * (i + 1)]
 
-        def diff_tile(k):
-            return place("diff%d" % k, [P, 2 * UNIT], F32, AT_DIFF[k])
-
         def rates(u):
-            m, i = divmod(u, 4)
+            m, i = divmod(u, STEP)
             if i == 0:
-                h_bf[m] = place("h_bf%d" % m, [P, 4 * UNIT], BF16, (AT_H0, AT_C + 3 * PAIR, AT_C + 5 * PAIR, AT_C + 6 * PAIR)[m])
+                h_bf[m] = place("h_bf%d" % m, [P, STEP * UNIT], BF16, AT_H[m])
             nc.vector.tensor_tensor(
                 out=h_bf[m][:, UNIT * i : UNIT * (i + 1)].rearrange("p (c i t) -> p c t i", i=2, t=PACK),
                 in0=diff[u].rearrange("p (t c i) -> p c t i", i=2, t=PACK),
-                in1=first_product("e", u, e_banks[u % len(e_banks)]).rearrange("p (t c i) -> p c t i", i=2, t=PACK),
+                in1=first_product("e", u, e_banks[i]).rearrange("p (t c i) -> p c t i", i=2, t=PACK),
                 op=ALU.mult,
             )
 
         def quantise_rates(first, count):
             words = held("h_w%d" % first, [P, count * JC], U32)
             scales = held("h_s%d" % first, [P, count * JC], U8)
-            at = first % 4 * UNIT
-            quantise(words[:], scales[:], h_bf[first // 4][:, at : at + count * UNIT])
+            m, at = divmod(first, STEP)
+            quantise(words[:], scales[:], h_bf[m][:, UNIT * at : UNIT * (at + count)])
             for i in range(0, count, 2):
                 cols = slice(JC * i, JC * min(i + 2, count))
                 h_q[first + i] = (words[:, cols], scales[:, cols])
 
-        wa_bf = [held("wa_bf0", [P, PACK * N], BF16), place("wa_bf1", [P, PACK * N], BF16, AT_WA_BF)]
+        wa_bf = [place("wa_bf%d" % g, [P, PACK * N], BF16, at) for g, at in enumerate((AT_WA_BF0, AT_WA_BF1))]
 
         def round_wa(part):
-            lo, hi = wa_cols[part]
-            g, q0 = lo // N, lo % N // 16
+            lo, hi = WA_LOADS[part]
+            g, qs = lo // N, slice(lo % N // 16, lo % N // 16 + (hi - lo) // 16)
             nc.gpsimd.tensor_scalar(
-                out=wa_bf[g][:].rearrange("p (t q i j) -> p q t i j", t=PACK, i=4, j=PACK)[:, q0 : q0 + (hi - lo) // 16],
+                out=wa_bf[g][:].rearrange("p (t q i j) -> p q t i j", t=PACK, i=4, j=PACK)[:, qs],
                 in0=wa_raw[part][:].rearrange("p j (q t i) -> p q t i j", t=PACK, i=4),
                 scalar1=1.0, scalar2=0.0, op0=ALU.mult, op1=ALU.add,
             )
@@ -239,27 +257,27 @@ def tile_list_electrode_kinetics_transport_kernel(
             quantise(words[:], scales[:], wa_bf[g][:])
             wa_q[g] = (words, scales)
 
-        wt_bf = {}
-        wt_w = {}
+        wt_bf, wt_w = {}, {}
         wt_s = [held("wt_s%d" % g, [P, N], U8) for g in range(PASSES)]
 
-        def round_wt_on_vector(g):
-            wt_bf[g] = held("wt_bf%d" % g, [P, PACK * N], BF16)
-            nc.vector.tensor_copy(
-                out=wt_bf[g][:].rearrange("p (t m j) -> p m j t", t=PACK, j=PACK),
-                in_=wt_raw[g][:].rearrange("p (j m t) -> p m j t", j=PACK, t=PACK),
+        def round_wt_on_gpsimd(g):
+            wt_bf[g] = place("wt_bf%d" % g, [P, PACK * N], BF16, AT_WT_BF0)
+            nc.gpsimd.tensor_scalar(
+                out=wt_bf[g][:].rearrange("p (t m j) -> p m t j", t=PACK, j=PACK),
+                in0=wt_raw[g][:].rearrange("p (j m t) -> p m t j", j=PACK, t=PACK),
+                scalar1=1.0, scalar2=0.0, op0=ALU.mult, op1=ALU.add,
             )
 
         def round_wt_on_scalar(g):
-            wt_bf[g] = place("wt_bf%d" % g, [P, PACK * N], BF16, AT_C)
+            wt_bf[g] = place("wt_bf%d" % g, [P, PACK * N], BF16, AT_TAB)
             nc.scalar.copy(
                 out=wt_bf[g][:].rearrange("p (t m j) -> p m j t", t=PACK, j=PACK),
                 in_=wt_raw[g][:].rearrange("p (j m t) -> p m j t", j=PACK, t=PACK),
             )
 
-        def quantise_wt(g):
-            wt_w[g] = place("wt_w1", [P, N], U32, AT_DIFF[1]) if g else held("wt_w0", [P, N], U32)
-            quantise(wt_w[g][:], wt_s[g][:], wt_bf[g][:])
+        def quantise_wt(g, words):
+            wt_w[g] = words
+            quantise(words[:], wt_s[g][:], wt_bf[g][:])
 
         y_sb, y_bf = {}, {}
         y_s = held("y_s", [P, S], U8)
@@ -296,11 +314,9 @@ def tile_list_electrode_kinetics_transport_kernel(
                     for g in range(PASSES):
                         if count == 2:
                             words, scales = h_q[2 * (first + g)]
-                            cols = slice(0, width)
                         else:
-                            words, scales = h_q[2 * first]
-                            cols = slice(JC * g, JC * (g + 1))
-                        second_product(bank[:, width * (t - t0) : width * (t - t0 + 1)], t, g, words[:, cols], scales[:, cols])
+                            words, scales = (part[:, JC * g : JC * (g + 1)] for part in h_q[2 * first])
+                        second_product(bank[:, width * (t - t0) : width * (t - t0 + 1)], t, g, words, scales)
                 for t in range(t0, t0 + per_bank):
                     add_src_on_scalar(b, t, bank[:, width * (t - t0) : width * (t - t0 + 1)])
             store_y(b)
@@ -319,102 +335,82 @@ def tile_list_electrode_kinetics_transport_kernel(
                         add_src(LAST, t, sums[t][:, :JC])
             store_y(LAST)
 
-        def round_y(b, engine):
-            if b:
-                y_bf[b] = held("y_bf%d" % b, [P, BATCHES[b][1] * UNIT], BF16)
-            else:
-                y_bf[b] = place("y_bf%d" % b, [P, BATCHES[b][1] * UNIT], BF16, AT_DIFF[7])
-            dst = y_bf[b][:].rearrange("p (c i t) -> p c t i", i=4, t=PACK)
-            source = y_sb[b][:].rearrange("p t (c i) -> p c t i", i=4)
-            if engine == "v":
-                nc.vector.tensor_copy(out=dst, in_=source)
-            elif engine == "s":
-                nc.scalar.copy(out=dst, in_=source)
-            else:
-                nc.gpsimd.tensor_scalar(
-                    out=y_bf[b][:].rearrange("p (j t) -> p j t", t=PACK), in0=y_sb[b][:].rearrange("p t j -> p j t"),
-                    scalar1=1.0, scalar2=0.0, op0=ALU.mult, op1=ALU.add,
-                )
+        def round_y(b, copy, at=None):
+            name, shape = "y_bf%d" % b, [P, BATCHES[b][1] * UNIT]
+            y_bf[b] = held(name, shape, BF16) if at is None else place(name, shape, BF16, at)
+            copy(
+                out=y_bf[b][:].rearrange("p (c i t) -> p c t i", i=4, t=PACK),
+                in_=y_sb[b][:].rearrange("p t (c i) -> p c t i", i=4),
+            )
 
         def quantise_y(b, at=None):
             first, count = BATCHES[b]
             cols = slice(first * JC, (first + count) * JC)
-            if at is None:
-                y_w = held("y_w%d" % b, [P, count * JC], U32)
-            else:
-                y_w = place("y_w%d" % b, [P, count * JC], U32, at)
+            name, shape = "y_w%d" % b, [P, count * JC]
+            y_w = held(name, shape, U32) if at is None else place(name, shape, U32, at)
             quantise(y_w[:], y_s[:, cols], y_bf[b][:])
             nc.sync.dma_start(out=out_words[:, cols], in_=y_w[:].bitcast(I32))
 
-        for u in range(11):
-            exponential("c", u)
-        for part in range(len(wa_cols)):
+        def exponentials(n, first, end):
+            for u in range(first, end):
+                exponential(n, u)
+
+        def step(m):
+            first = STEP * m
+            subtract(nc.vector, first + 2)
+            quantise_rates(first - STEP, STEP)
+            subtract(nc.gpsimd, min(first + STEP, UNITS - 1))
+            for u in range(first, min(first + STEP, UNITS - 1)):
+                rates(u)
+
+        exponentials("c", 0, EARLY_C)
+        for part in range(len(WA_LOADS)):
             round_wa(part)
         quantise_wa(0, place("wa_w0", [P, N], U32, AT_WA1 + 4 * H), place("wa_s0", [P, N], U8, AT_WA1 + 7 * H))
         quantise_wa(1, held("wa_w1", [P, N], U32), place("wa_s1", [P, N], U8, AT_WA1 + 7 * H + N))
-        we_q["s"] = deal(place("we_s", [P, H // 4], I32, AT_WA1 + 6 * H), we_s_raw[:].bitcast(I32))
+        we_q["s"] = deal(place("we_s", [P, H // 4], I32, AT_WA1 + 6 * H), we_s_raw.bitcast(I32))
         we_q["w"] = deal(place("we_w", [P, H], I32, AT_WA1), we_raw[:])
-        gather_words("e", 0, place("v_w_e", [P, S], U32, AT_WA_BF + 64)[:])
-        for u in range(6):
-            exponential("a", u)
-        first_diff = diff_tile(0)
-        for u in range(2):
-            subtract(nc.gpsimd, u, 1, first_diff[:, UNIT * u : UNIT * (u + 1)])
-        round_wt_on_vector(0)
-        subtract(nc.vector, 2, 2, diff_tile(1)[:])
-        quantise_wt(0)
-        subtract(nc.gpsimd, 4, 2, diff_tile(2)[:])
+        gather_words("e", 0, place("v_w_e", [P, S], U32, AT_E_WORDS)[:])
+        exponentials("a", 0, EARLY_A)
+        round_wt_on_gpsimd(0)
+
+        subtract(nc.vector, 0)
+        subtract(nc.vector, 2)
+        quantise_wt(0, held("wt_w0", [P, N], U32))
+        subtract(nc.gpsimd, STEP)
         round_wt_on_scalar(1)
-        for u in range(4):
+        for u in range(STEP):
             rates(u)
-        for u in range(6, 10):
-            exponential("a", u)
-        exponential("c", 11)
-        exponential("a", 10)
-        exponential("a", 11)
-        exponential("c", 12)
-        exponential("c", 13)
 
-        def step(m):
-            if m < 3:
-                subtract(nc.vector, 4 * m + 2, 2, diff_tile(2 * m + 1)[:])
-            else:
-                subtract(nc.vector, 4 * m + 2, 1, diff_tile(2 * m + 1)[:, :UNIT])
-            quantise_rates(4 * m - 4, 4)
-            if m < 3:
-                subtract(nc.gpsimd, 4 * m + 4, 2, diff_tile(2 * m + 2)[:])
-            else:
-                subtract(nc.gpsimd, 4 * m + 3, 1, ex["a", 2 * m + 1][:, :UNIT])
-            for u in range(4 * m, min(4 * m + 4, UNITS - 1)):
-                rates(u)
-
-        quantise_wt(1)
+        exponentials("a", EARLY_A, 10)
+        exponentials("c", EARLY_C, 12)
+        exponentials("a", 10, 12)
+        exponentials("c", 12, 14)
+        quantise_wt(1, place("wt_w1", [P, N], U32, AT_DIFF[2]))
         step(1)
         transport(0)
-        exponential("a", 12)
-        exponential("a", 13)
-        round_y(0, "s")
-        exponential("c", 14)
-        exponential("c", 15)
-        exponential("a", 14)
-        exponential("a", 15)
+        exponentials("a", 12, 14)
+        round_y(0, nc.scalar.copy, AT_DIFF[14])
+        exponentials("c", 14, UNITS)
+        exponentials("a", 14, UNITS)
         step(2)
         transport(1)
-        round_y(1, "s")
-        quantise_y(0, AT_DIFF[5])
+        round_y(1, nc.scalar.copy)
+        quantise_y(0, AT_DIFF[10])
         step(3)
         transport(2)
-        round_y(2, "s")
-        quantise_rates(12, 2)
-        rates(15)
-        transport(3)
+        round_y(2, nc.scalar.copy)
+
+        quantise_rates(UNITS - STEP, 2)
+        rates(UNITS - 1)
+        transport(LAST - 1)
         last_transport()
-        round_y(3, "s")
-        quantise_y(1, AT_EXP_A[5])
+        round_y(LAST - 1, nc.scalar.copy)
+        quantise_y(1, AT_DIFF[12])
         quantise_y(2)
-        round_y(LAST, "v")
+        round_y(LAST, nc.vector.tensor_copy)
         quantise_y(LAST)
-        quantise_y(3)
+        quantise_y(LAST - 1)
 
         for quad in range(4):
             queue = nc.sync if quad % 2 == 0 else nc.scalar

@@ -44,31 +44,33 @@ AT_WA1 = AT_TAB + 4 * T
 AT_WA_BF1 = AT_WA1 + 2 * PAIR
 AT_WE = AT_WA_BF1 + PAIR
 AT_E_WORDS = AT_WA_BF1 + EDGE
-AT_WT_BF0 = AT_WE + EDGE
-AT_A1 = AT_WT_BF0 + PAIR
-AT_H0 = AT_A1 + PAIR
-AT_A3 = AT_H0 + PAIR
-AT_WT1 = AT_A3 - EDGE
-AT_WT0 = AT_A3 + 2 * PAIR
-AT_C0 = AT_WT0 + 2 * PAIR
-AT_A5 = AT_C0 + 4 * PAIR
-AT_C4 = AT_A5 + PAIR
-AT_A14 = AT_C4 + 2 * PAIR
+AT_D0 = AT_WE + EDGE
+AT_A1 = AT_D0 + PAIR
+AT_WT0 = AT_A1 + PAIR
+AT_WT1 = AT_WT0 + 2 * PAIR
+AT_A5 = AT_WT1 + PAIR
+AT_H1 = AT_WT1 + 2 * PAIR
+AT_C0 = AT_H1 + PAIR
+AT_C4 = AT_C0 + 4 * PAIR
+AT_Y0 = AT_C4 + 2 * PAIR
+AT_A14 = AT_Y0 + TILE
 AT_C6 = AT_A14 + TILE
 AT_C14 = AT_C6 + PAIR
-AT_A0 = AT_C14 + PAIR
-AT_A2 = AT_A0 + PAIR
+AT_A2 = AT_C14 + PAIR
 AT_A15 = AT_A2 + PAIR
+AT_A0 = AT_A15 + 2 * TILE
 AT_EXP = {
-    "a": {0: AT_A0, 2: AT_A1, 4: AT_A2, 6: AT_A3, 8: AT_A3 + PAIR, 10: AT_A5, 12: AT_A2, 14: AT_A14, 15: AT_A15},
+    "a": {0: AT_A0, 2: AT_A1, 4: AT_A2, 6: AT_WT0, 8: AT_WT1, 10: AT_A5, 12: AT_A2, 14: AT_A14, 15: AT_A15},
     "c": {0: AT_C0, 2: AT_C0 + PAIR, 4: AT_C0 + 2 * PAIR, 6: AT_C0 + 3 * PAIR, 8: AT_C4, 10: AT_C4 + PAIR, 12: AT_C6,
           14: AT_C14, 15: AT_C14 + TILE},
 }
-AT_H = (AT_H0, AT_EXP["c"][6], AT_EXP["c"][10], AT_C14 - TILE)
+AT_WT_BF = (AT_TAB, AT_TAB + PAIR)
+AT_H = (AT_TAB + 2 * PAIR, AT_H1, AT_EXP["c"][10], AT_C14 - TILE)
 AT_DIFF = {
-    0: AT_WT0, 2: AT_WT0 + PAIR, 4: AT_A1 - TILE, 6: AT_TAB, 8: AT_A3 - TILE, 10: AT_TAB, 12: AT_A5 - TILE, 14: AT_A0,
-    15: AT_A14 - TILE // 2,
+    0: AT_D0, 2: AT_A0, 4: AT_A1, 6: AT_A0 + EDGE, 8: AT_TAB + PAIR + TILE, 10: AT_A0 + EDGE, 12: AT_H1 - TILE,
+    14: AT_A0 + EDGE, 15: AT_Y0 - TILE // 2,
 }
+AT_WT_W = (AT_A0 + EDGE - TILE, AT_EXP["c"][6])
 
 
 def unit_of(u):
@@ -95,7 +97,7 @@ def tile_list_electrode_kinetics_transport_kernel(
             return placed.tile(shape, dtype, name=name, offset=offset, align_bytes=64)
 
         banks = [psum.tile([P, BANK], F32, name="bank%d" % b) for b in range(8)]
-        exp_banks, e_banks, y_banks = banks[0:2], banks[2:6], banks[6:8]
+        exp_banks, e_banks, y_bank = banks[0:3], banks[3:7], banks[7]
 
         lists = {n: held("list_" + n, [P, S // 16], U16) for n in "ace"}
         tab_w = place("tab_w", [P, T], U32, AT_TAB)
@@ -106,7 +108,7 @@ def tile_list_electrode_kinetics_transport_kernel(
         we_raw = place("we_raw", [P, H], I32, AT_WE)
         wa_raw = [held("wa_raw%d" % lo, [P, PACK, hi - lo], F32) for lo, hi in WA_LOADS[:-1]]
         wa_raw.append(place("wa_raw_last", [P, PACK, N], F32, AT_WA1))
-        wt_raw = [place("wt_raw0", [P, PACK * N], F32, AT_WT0), place("wt_raw1", [P, PACK * N], F32, AT_WT1)]
+        wt_raw = [place("wt_raw0", [P, PACK * N], F32, AT_WT0), place("wt_raw1", [P, PACK * N + EDGE // 4], F32, AT_WT1)]
         src_sb = held("src_sb", [P, PACK], F32)
 
         def load_scale_rows(queues, plane, rows):
@@ -136,7 +138,7 @@ def tile_list_electrode_kinetics_transport_kernel(
         wt_rows = wt.rearrange("(g q t i) n -> g i q t n", g=PASSES, t=PACK, i=4)
         for g in range(PASSES):
             for i in range(4):
-                nc.sync.dma_start(out=wt_raw[g][i:P:4, :].rearrange("q (t n) -> q t n", t=PACK), in_=wt_rows[g, i])
+                nc.sync.dma_start(out=wt_raw[g][i:P:4, : PACK * N].rearrange("q (t n) -> q t n", t=PACK), in_=wt_rows[g, i])
         nc.sync.dma_start(out=src_sb[:], in_=src.rearrange("(p t) -> p t", t=PACK))
 
         def quantise(words, scales, values):
@@ -200,8 +202,13 @@ def tile_list_electrode_kinetics_transport_kernel(
 
         ex, diff, h_bf, h_q = {}, {}, {}, {}
 
+        turns = []
+
+        def scalar_bank():
+            turns.append(len(turns))
+            return exp_banks[turns[-1] % len(exp_banks)]
+
         def exponential(n, u):
-            count = len(ex)
             if u in AT_EXP[n]:
                 width = UNIT if u >= UNITS - 2 else 2 * UNIT
                 ex[n, u] = place("exp_%s%d" % (n, u), [P, width], F32, AT_EXP[n][u])[:]
@@ -209,10 +216,10 @@ def tile_list_electrode_kinetics_transport_kernel(
                 ex[n, u] = ex[n, u - 1][:, UNIT:]
             if n == "a" and EARLY_A - STEP <= u < EARLY_A:
                 bank = e_banks[u - (EARLY_A - STEP)]
-            elif count < EARLY_C:
-                bank = (exp_banks + y_banks)[count % 4]
+            elif len(ex) <= EARLY_C:
+                bank = (exp_banks + [y_bank])[len(ex) % 4]
             else:
-                bank = exp_banks[count % 2]
+                bank = scalar_bank()
             nc.scalar.activation(out=ex[n, u][:, :UNIT], in_=first_product(n, u, bank), func=ACT.Exp)
 
         def subtract(engine, first):
@@ -260,24 +267,16 @@ def tile_list_electrode_kinetics_transport_kernel(
         wt_bf, wt_w = {}, {}
         wt_s = [held("wt_s%d" % g, [P, N], U8) for g in range(PASSES)]
 
-        def round_wt_on_gpsimd(g):
-            wt_bf[g] = place("wt_bf%d" % g, [P, PACK * N], BF16, AT_WT_BF0)
-            nc.gpsimd.tensor_scalar(
-                out=wt_bf[g][:].rearrange("p (t m j) -> p m t j", t=PACK, j=PACK),
-                in0=wt_raw[g][:].rearrange("p (j m t) -> p m t j", j=PACK, t=PACK),
-                scalar1=1.0, scalar2=0.0, op0=ALU.mult, op1=ALU.add,
-            )
-
         def round_wt_on_scalar(g):
-            wt_bf[g] = place("wt_bf%d" % g, [P, PACK * N], BF16, AT_TAB)
+            wt_bf[g] = place("wt_bf%d" % g, [P, PACK * N], BF16, AT_WT_BF[g])
             nc.scalar.copy(
                 out=wt_bf[g][:].rearrange("p (t m j) -> p m j t", t=PACK, j=PACK),
-                in_=wt_raw[g][:].rearrange("p (j m t) -> p m j t", j=PACK, t=PACK),
+                in_=wt_raw[g][:, : PACK * N].rearrange("p (j m t) -> p m j t", j=PACK, t=PACK),
             )
 
-        def quantise_wt(g, words):
-            wt_w[g] = words
-            quantise(words[:], wt_s[g][:], wt_bf[g][:])
+        def quantise_wt(g):
+            wt_w[g] = place("wt_w%d" % g, [P, N], U32, AT_WT_W[g])
+            quantise(wt_w[g][:], wt_s[g][:], wt_bf[g][:])
 
         y_sb, y_bf = {}, {}
         y_s = held("y_s", [P, S], U8)
@@ -303,30 +302,30 @@ def tile_list_electrode_kinetics_transport_kernel(
             first, count = BATCHES[b]
             nc.sync.dma_start(out=out_rows[:, :, first * JC : (first + count) * JC], in_=y_sb[b][:])
 
-        def transport(b):
+        def transport(b, half, add_src):
             first, count = BATCHES[b]
             width = count * JC
             per_bank = BANK // width
-            y_sb[b] = held("y_sb%d" % b, [P, PACK, width], F32)
-            for t0 in range(0, PACK, per_bank):
-                bank = y_banks[t0 // per_bank]
-                for t in range(t0, t0 + per_bank):
-                    for g in range(PASSES):
-                        if count == 2:
-                            words, scales = h_q[2 * (first + g)]
-                        else:
-                            words, scales = (part[:, JC * g : JC * (g + 1)] for part in h_q[2 * first])
-                        second_product(bank[:, width * (t - t0) : width * (t - t0 + 1)], t, g, words, scales)
-                for t in range(t0, t0 + per_bank):
-                    add_src_on_scalar(b, t, bank[:, width * (t - t0) : width * (t - t0 + 1)])
-            store_y(b)
+            if b not in y_sb:
+                y_sb[b] = held("y_sb%d" % b, [P, PACK, width], F32)
+            bank, t0 = (y_bank if half else scalar_bank()), half * per_bank
+            for t in range(t0, t0 + per_bank):
+                for g in range(PASSES):
+                    if count == 2:
+                        words, scales = h_q[2 * (first + g)]
+                    else:
+                        words, scales = (part[:, JC * g : JC * (g + 1)] for part in h_q[2 * first])
+                    second_product(bank[:, width * (t - t0) : width * (t - t0 + 1)], t, g, words, scales)
+            for t in range(t0, t0 + per_bank):
+                add_src(b, t, bank[:, width * (t - t0) : width * (t - t0 + 1)])
 
         def last_transport():
-            sums = exp_banks + e_banks[:2]
+            sums = [scalar_bank(), e_banks[0], scalar_bank(), e_banks[1]]
             for g in range(PASSES):
                 quantise_rates(UNITS - PASSES + g, 1)
                 words, scales = h_q[UNITS - PASSES + g]
                 if g == PASSES - 1:
+                    quantise_y(1, AT_DIFF[12])
                     y_sb[LAST] = held("y_sb%d" % LAST, [P, PACK, JC], F32)
                 for t in range(PACK):
                     second_product(sums[t][:, :JC], t, g, words, scales)
@@ -359,9 +358,14 @@ def tile_list_electrode_kinetics_transport_kernel(
             first = STEP * m
             subtract(nc.vector, first + 2)
             quantise_rates(first - STEP, STEP)
+            if m == 1:
+                quantise_wt(1)
+            if m == 3:
+                quantise_y(0)
             subtract(nc.gpsimd, min(first + STEP, UNITS - 1))
             for u in range(first, min(first + STEP, UNITS - 1)):
                 rates(u)
+            transport(m - 1, 1, add_src_on_vector)
 
         exponentials("c", 0, EARLY_C)
         for part in range(len(WA_LOADS)):
@@ -372,45 +376,47 @@ def tile_list_electrode_kinetics_transport_kernel(
         we_q["w"] = deal(place("we_w", [P, H], I32, AT_WA1), we_raw[:])
         gather_words("e", 0, place("v_w_e", [P, S], U32, AT_E_WORDS)[:])
         exponentials("a", 0, EARLY_A)
-        round_wt_on_gpsimd(0)
+        subtract(nc.gpsimd, 0)
 
-        subtract(nc.vector, 0)
         subtract(nc.vector, 2)
-        quantise_wt(0, held("wt_w0", [P, N], U32))
         subtract(nc.gpsimd, STEP)
-        round_wt_on_scalar(1)
+        round_wt_on_scalar(0)
         for u in range(STEP):
             rates(u)
 
-        exponentials("a", EARLY_A, 10)
-        exponentials("c", EARLY_C, 12)
-        exponentials("a", 10, 12)
-        exponentials("c", 12, 14)
-        quantise_wt(1, place("wt_w1", [P, N], U32, AT_DIFF[2]))
-        step(1)
-        transport(0)
+        exponentials("a", EARLY_A, 8)
+        round_wt_on_scalar(1)
+        exponentials("a", 8, 12)
+        exponentials("c", EARLY_C, 14)
         exponentials("a", 12, 14)
-        round_y(0, nc.scalar.copy, AT_DIFF[14])
-        exponentials("c", 14, UNITS)
-        exponentials("a", 14, UNITS)
+        quantise_wt(0)
+        step(1)
+        transport(0, 0, add_src_on_scalar)
+        store_y(0)
+        exponentials("c", 14, 15)
+        exponentials("a", 14, 15)
+        round_y(0, nc.scalar.copy, AT_Y0)
+        exponentials("c", 15, 16)
+        exponentials("a", 15, 16)
         step(2)
-        transport(1)
-        round_y(1, nc.scalar.copy)
-        quantise_y(0, AT_DIFF[10])
+        transport(1, 0, add_src_on_scalar)
+        store_y(1)
         step(3)
-        transport(2)
-        round_y(2, nc.scalar.copy)
+        transport(2, 0, add_src_on_scalar)
+        store_y(2)
+        round_y(1, nc.scalar.copy)
 
         quantise_rates(UNITS - STEP, 2)
         rates(UNITS - 1)
-        transport(LAST - 1)
+        transport(LAST - 1, 0, add_src_on_scalar)
+        store_y(LAST - 1)
         last_transport()
-        round_y(LAST - 1, nc.scalar.copy)
-        quantise_y(1, AT_DIFF[12])
-        quantise_y(2)
+        round_y(2, nc.scalar.copy)
         round_y(LAST, nc.vector.tensor_copy)
+        round_y(LAST - 1, nc.vector.tensor_copy)
         quantise_y(LAST)
         quantise_y(LAST - 1)
+        quantise_y(2)
 
         for quad in range(4):
             queue = nc.sync if quad % 2 == 0 else nc.scalar

@@ -112,10 +112,9 @@ def tile_list_electrode_kinetics_transport_kernel(
         src_sb = held("src_sb", [P, PACK], F32)
 
         def load_scale_rows(queues, plane, rows):
-            for quad in range(4):
-                queues[quad % len(queues)].dma_start(
-                    out=plane[32 * quad : 32 * quad + 4, :].bitcast(I32),
-                    in_=rows[0, 4 * quad : 4 * quad + 4, :].bitcast(I32),
+            for r in range(4):
+                queues[r % len(queues)].dma_start(
+                    out=plane[r:P:32, :].bitcast(I32), in_=rows[0, r:16:4, :].bitcast(I32)
                 )
 
         nc.vector.memset(tab_s[:, : T // 2].bitcast(I32), 0)
@@ -418,9 +417,6 @@ def tile_list_electrode_kinetics_transport_kernel(
         quantise_y(LAST - 1)
         quantise_y(2)
 
-        for quad in range(4):
-            queue = nc.sync if quad % 2 == 0 else nc.scalar
-            queue.dma_start(
-                out=out_2[0, 4 * quad : 4 * quad + 4, :].bitcast(I32),
-                in_=y_s[32 * quad : 32 * quad + 4, :].bitcast(I32),
-            )
+        for r in range(4):
+            queue = nc.sync if r % 2 == 0 else nc.scalar
+            queue.dma_start(out=out_2[0, r:16:4, :].bitcast(I32), in_=y_s[r:P:32, :].bitcast(I32))

@@ -28,7 +28,8 @@ UNITS = CHUNKS * PASSES
 STEP = 4
 BATCHES = ((0, 2), (2, 2), (4, 2), (6, 1), (7, 1))
 LAST = len(BATCHES) - 1
-EARLY_C = 11
+WE_PLANE = 4
+EARLY_C = 12
 EARLY_A = 6
 WA_LOADS = ((0, N // 2), (N // 2, N), (N, 2 * N))
 
@@ -102,7 +103,7 @@ def tile_list_electrode_kinetics_transport_kernel(
         lists = {n: held("list_" + n, [P, S // 16], U16) for n in "ace"}
         tab_w = place("tab_w", [P, T], U32, AT_TAB)
         tab_s = held("tab_s", [P, T], U8)
-        wc_s_raw = place("wc_s_raw", [P, H + 2 * EDGE], U8, AT_WC_SCALES)[:, :H]
+        wc_s_raw = place("wc_s_raw", [P, H + EDGE], U8, AT_WC_SCALES)[:, :H]
         we_s_raw = held("we_s_raw", [P, H], U8)[:]
         wc_raw = held("wc_raw", [P, H // 2], I32)
         we_raw = place("we_raw", [P, H], I32, AT_WE)
@@ -111,10 +112,10 @@ def tile_list_electrode_kinetics_transport_kernel(
         wt_raw = [place("wt_raw0", [P, PACK * N], F32, AT_WT0), place("wt_raw1", [P, PACK * N + EDGE // 4], F32, AT_WT1)]
         src_sb = held("src_sb", [P, PACK], F32)
 
-        def load_scale_rows(queues, plane, rows):
+        def load_scale_rows(queues, plane, rows, first=0):
             for r in range(4):
                 queues[r % len(queues)].dma_start(
-                    out=plane[r:P:32, :].bitcast(I32), in_=rows[0, r:16:4, :].bitcast(I32)
+                    out=plane[first + r : P : 32, :].bitcast(I32), in_=rows[0, r:16:4, :].bitcast(I32)
                 )
 
         nc.vector.memset(tab_s[:, : T // 2].bitcast(I32), 0)
@@ -132,7 +133,7 @@ def tile_list_electrode_kinetics_transport_kernel(
             nc.sync.dma_start(out=wa_raw[part][:], in_=wa_rows[:, :, lo:hi])
             if hi == N:
                 nc.sync.dma_start(lists["e"][:], offs3)
-        load_scale_rows((nc.sync,), we_s_raw, we_scales)
+        load_scale_rows((nc.sync,), we_s_raw, we_scales, WE_PLANE)
         nc.sync.dma_start(out=we_raw[:], in_=we_words[0].rearrange("p y i -> p (y i)").bitcast(I32))
         wt_rows = wt.rearrange("(g q t i) n -> g i q t n", g=PASSES, t=PACK, i=4)
         for g in range(PASSES):
@@ -150,10 +151,20 @@ def tile_list_electrode_kinetics_transport_kernel(
             v_s[n] = tile
 
         def gather_words(n, first, words):
-            halves, cols = words.shape[1] // HALF, HALF // 16
-            nc.vector.tensor_copy(words, tab_w[:].indirect(lists[n][:, cols * first : cols * (first + halves)]))
-            for half in range(halves):
-                v_w[n, first + half] = words[:, HALF * half : HALF * (half + 1)]
+            count, cols = words.shape[1] // JC, JC // 16
+            nc.vector.tensor_copy(words, tab_w[:].indirect(lists[n][:, cols * first : cols * (first + count)]))
+            for i in range(count):
+                v_w[n, first + i] = words[:, JC * i : JC * (i + 1)]
+
+        def deal_on_scalar(dealt, raw):
+            words = raw.shape[1] // PASSES
+            for g in range(PASSES):
+                cols = slice(words * g, words * (g + 1))
+                nc.scalar.copy(
+                    out=dealt[:, cols].rearrange("p (t q w) -> p t q w", t=PACK, q=32),
+                    in_=raw[:, cols].rearrange("p (q t w) -> p t q w", t=PACK, q=32),
+                )
+            return dealt
 
         def deal(dealt, raw):
             nc.vector.tensor_copy(
@@ -162,13 +173,13 @@ def tile_list_electrode_kinetics_transport_kernel(
             )
             return dealt
 
-        wc_w = deal(held("wc_w", [P, H // 2], I32), wc_raw[:])
+        wc_w = deal_on_scalar(held("wc_w", [P, H // 2], U32), wc_raw[:].bitcast(U32))
         gather_scales("c", held("v_s_c", [P, S], U8))
         gather_scales("a", held("v_s_a", [P, S], U8))
-        wc_s = deal(held("wc_s", [P, H // 4], I32), wc_s_raw.bitcast(I32))
+        wc_s = deal_on_scalar(held("wc_s", [P, H // 4], U32), wc_s_raw.bitcast(U32))
         v_w_ca = place("v_w_ca", [P, 2 * S], U32, AT_WORDS)
-        gather_words("c", 0, v_w_ca[:, :HALF])
-        gather_words("c", 1, v_w_ca[:, HALF:S])
+        gather_words("c", 0, v_w_ca[:, : 2 * JC])
+        gather_words("c", 2, v_w_ca[:, 2 * JC : S])
         gather_words("a", 0, v_w_ca[:, S:])
         gather_scales("e", place("v_s_e", [P, S], U8, AT_E_SCALES))
 
@@ -184,16 +195,15 @@ def tile_list_electrode_kinetics_transport_kernel(
                     wc_w[:].bitcast(U8)[:, 2 * P * s : 2 * P * (s + 1)].bitcast(E2M1),
                     wc_s[:].bitcast(U8)[:, cols],
                 )
-            return we_q["w"][:, cols].bitcast(E4M3), we_q["s"][:].bitcast(U8)[:, cols]
+            return we_q["w"][:, cols].bitcast(E4M3), we_q["s"][:].bitcast(U8)[WE_PLANE:, cols]
 
         def first_product(n, u, bank):
             jc, g = unit_of(u)
-            half, j0 = divmod(jc * JC, HALF)
             for t in range(PACK):
                 codes, scales = weights(n, g, t)
                 nc.tensor.matmul_mx(
                     out=bank[:, JC * t : JC * (t + 1)], lhsT=codes, lhsT_scale=scales,
-                    rhs=v_w[n, half][:, j0 : j0 + JC].bitcast(E4M3),
+                    rhs=v_w[n, jc].bitcast(E4M3),
                     rhs_scale=v_s[n][:, jc * JC : (jc + 1) * JC],
                     start=True, stop=True,
                 )
@@ -216,7 +226,7 @@ def tile_list_electrode_kinetics_transport_kernel(
             if n == "a" and EARLY_A - STEP <= u < EARLY_A:
                 bank = e_banks[u - (EARLY_A - STEP)]
             elif len(ex) <= EARLY_C:
-                bank = (exp_banks + [y_bank])[len(ex) % 4]
+                bank = (exp_banks + [y_bank])[(len(ex) - 1) % 4]
             else:
                 bank = scalar_bank()
             nc.scalar.activation(out=ex[n, u][:, :UNIT], in_=first_product(n, u, bank), func=ACT.Exp)
@@ -319,12 +329,15 @@ def tile_list_electrode_kinetics_transport_kernel(
                 add_src(b, t, bank[:, width * (t - t0) : width * (t - t0 + 1)])
 
         def last_transport():
-            sums = [scalar_bank(), e_banks[0], scalar_bank(), e_banks[1]]
+            sums = e_banks
             for g in range(PASSES):
-                quantise_rates(UNITS - PASSES + g, 1)
+                if g == PASSES - 1:
+                    quantise_y(0)
+                    quantise_rates(UNITS - 1, 1)
+                    quantise_y(1)
+                    store_words(0)
                 words, scales = h_q[UNITS - PASSES + g]
                 if g == PASSES - 1:
-                    quantise_y(1, AT_DIFF[12])
                     y_sb[LAST] = held("y_sb%d" % LAST, [P, PACK, JC], F32)
                 for t in range(PACK):
                     second_product(sums[t][:, :JC], t, g, words, scales)
@@ -341,13 +354,17 @@ def tile_list_electrode_kinetics_transport_kernel(
                 in_=y_sb[b][:].rearrange("p t (c i) -> p c t i", i=4),
             )
 
-        def quantise_y(b, at=None):
+        y_w = {}
+
+        def quantise_y(b):
             first, count = BATCHES[b]
-            cols = slice(first * JC, (first + count) * JC)
-            name, shape = "y_w%d" % b, [P, count * JC]
-            y_w = held(name, shape, U32) if at is None else place(name, shape, U32, at)
-            quantise(y_w[:], y_s[:, cols], y_bf[b][:])
-            nc.sync.dma_start(out=out_words[:, cols], in_=y_w[:].bitcast(I32))
+            half, at = divmod(first * JC, HALF)
+            if half not in y_w:
+                y_w[half] = place("y_w%d" % half, [P, HALF], U32, AT_DIFF[12] + TILE * half)
+            quantise(y_w[half][:, at : at + count * JC], y_s[:, first * JC : (first + count) * JC], y_bf[b][:])
+
+        def store_words(half):
+            nc.sync.dma_start(out=out_words[:, HALF * half : HALF * (half + 1)], in_=y_w[half][:].bitcast(I32))
 
         def exponentials(n, first, end):
             for u in range(first, end):
@@ -359,12 +376,11 @@ def tile_list_electrode_kinetics_transport_kernel(
             quantise_rates(first - STEP, STEP)
             if m == 1:
                 quantise_wt(1)
-            if m == 3:
-                quantise_y(0)
             subtract(nc.gpsimd, min(first + STEP, UNITS - 1))
             for u in range(first, min(first + STEP, UNITS - 1)):
                 rates(u)
-            transport(m - 1, 1, add_src_on_vector)
+            if m < 3:
+                transport(m - 1, 1, add_src_on_vector)
 
         exponentials("c", 0, EARLY_C)
         for part in range(len(WA_LOADS)):
@@ -394,18 +410,19 @@ def tile_list_electrode_kinetics_transport_kernel(
         store_y(0)
         exponentials("c", 14, 15)
         exponentials("a", 14, 15)
-        round_y(0, nc.scalar.copy, AT_Y0)
         exponentials("c", 15, 16)
         exponentials("a", 15, 16)
+        round_y(0, nc.scalar.copy)
         step(2)
         transport(1, 0, add_src_on_scalar)
         store_y(1)
         step(3)
         transport(2, 0, add_src_on_scalar)
+        transport(2, 1, add_src_on_scalar)
         store_y(2)
         round_y(1, nc.scalar.copy)
 
-        quantise_rates(UNITS - STEP, 2)
+        quantise_rates(UNITS - STEP, STEP - 1)
         rates(UNITS - 1)
         transport(LAST - 1, 0, add_src_on_scalar)
         store_y(LAST - 1)
@@ -413,9 +430,10 @@ def tile_list_electrode_kinetics_transport_kernel(
         round_y(2, nc.scalar.copy)
         round_y(LAST, nc.vector.tensor_copy)
         round_y(LAST - 1, nc.vector.tensor_copy)
+        quantise_y(2)
         quantise_y(LAST)
         quantise_y(LAST - 1)
-        quantise_y(2)
+        store_words(1)
 
         for r in range(4):
             queue = nc.sync if r % 2 == 0 else nc.scalar

@@ -29,6 +29,7 @@ STEP = 4
 BATCHES = ((0, 2), (2, 2), (4, 2), (6, 1), (7, 1))
 LAST = len(BATCHES) - 1
 WE_PLANE = 4
+WIDE_UNITS = 12
 EARLY_C = 12
 EARLY_A = 6
 WA_LOADS = ((0, N // 2), (N // 2, N), (N, 2 * N))
@@ -144,7 +145,7 @@ def tile_list_electrode_kinetics_transport_kernel(
         def quantise(words, scales, values):
             nc.vector.quantize_mx(out=words.bitcast(E4M3), scales=scales, in_=values)
 
-        v_s, v_w = {}, {}
+        v_s, v_w, v_w2 = {}, {}, {}
 
         def gather_scales(n, tile):
             nc.vector.tensor_copy(tile[:], tab_s[:].indirect(lists[n][:]))
@@ -155,6 +156,8 @@ def tile_list_electrode_kinetics_transport_kernel(
             nc.vector.tensor_copy(words, tab_w[:].indirect(lists[n][:, cols * first : cols * (first + count)]))
             for i in range(count):
                 v_w[n, first + i] = words[:, JC * i : JC * (i + 1)]
+                if i % 2 == 0:
+                    v_w2[n, first + i] = words[:, JC * i : JC * (i + 2)]
 
         def deal_on_scalar(dealt, raw):
             words = raw.shape[1] // PASSES
@@ -209,6 +212,16 @@ def tile_list_electrode_kinetics_transport_kernel(
                 )
             return bank[:]
 
+        def wide_product(n, u, bank):
+            jc, g = unit_of(u - u % 2)
+            for i in range(2):
+                codes, scales = weights(n, g, 2 * (u % 2) + i)
+                nc.tensor.matmul_mx(
+                    out=bank[:, 2 * JC * i : 2 * JC * (i + 1)], lhsT=codes, lhsT_scale=scales,
+                    rhs=v_w2[n, jc].bitcast(E4M3), rhs_scale=v_s[n][:, jc * JC : (jc + 2) * JC], start=True, stop=True,
+                )
+            return bank[:]
+
         ex, diff, h_bf, h_q = {}, {}, {}, {}
 
         turns = []
@@ -229,14 +242,18 @@ def tile_list_electrode_kinetics_transport_kernel(
                 bank = (exp_banks + [y_bank])[(len(ex) - 1) % 4]
             else:
                 bank = scalar_bank()
-            nc.scalar.activation(out=ex[n, u][:, :UNIT], in_=first_product(n, u, bank), func=ACT.Exp)
+            product = wide_product if u < WIDE_UNITS else first_product
+            nc.scalar.activation(out=ex[n, u][:, :UNIT], in_=product(n, u, bank), func=ACT.Exp)
 
         def subtract(engine, first):
             width = ex["a", first].shape[1]
             target = place("diff%d" % first, [P, width], F32, AT_DIFF[first])
             engine.tensor_tensor(out=target[:], in0=ex["a", first], in1=ex["c", first], op=ALU.subtract)
             for i in range(width // UNIT):
-                diff[first + i] = target[:, UNIT * i : UNIT * (i + 1)]
+                if first < WIDE_UNITS:
+                    diff[first + i] = target[:].rearrange("p (t j) -> p t j", t=PACK)[:, :, JC * i : JC * (i + 1)]
+                else:
+                    diff[first + i] = target[:, UNIT * i : UNIT * (i + 1)].rearrange("p (t j) -> p t j", t=PACK)
 
         def rates(u):
             m, i = divmod(u, STEP)
@@ -244,7 +261,7 @@ def tile_list_electrode_kinetics_transport_kernel(
                 h_bf[m] = place("h_bf%d" % m, [P, STEP * UNIT], BF16, AT_H[m])
             nc.vector.tensor_tensor(
                 out=h_bf[m][:, UNIT * i : UNIT * (i + 1)].rearrange("p (c i t) -> p c t i", i=2, t=PACK),
-                in0=diff[u].rearrange("p (t c i) -> p c t i", i=2, t=PACK),
+                in0=diff[u].rearrange("p t (c i) -> p c t i", i=2),
                 in1=first_product("e", u, e_banks[i]).rearrange("p (t c i) -> p c t i", i=2, t=PACK),
                 op=ALU.mult,
             )
@@ -302,6 +319,13 @@ def tile_list_electrode_kinetics_transport_kernel(
         def add_src_on_scalar(b, t, sums):
             nc.scalar.activation(out=y_sb[b][:, t, :], in_=sums, func=ACT.Identity, bias=src_sb[:, t : t + 1])
 
+        def add_src_to_bank(b, t0, count, bank):
+            width = y_sb[b].shape[2]
+            nc.vector.tensor_tensor(
+                out=y_sb[b][:, t0 : t0 + count, :], in0=bank[:].rearrange("p (t j) -> p t j", t=count),
+                in1=src_sb[:, t0 : t0 + count].unsqueeze(2).to_broadcast([P, count, width]), op=ALU.add,
+            )
+
         def add_src_on_vector(b, t, sums):
             nc.vector.tensor_scalar(
                 out=y_sb[b][:, t, :], in0=sums, scalar1=src_sb[:, t : t + 1], scalar2=None, op0=ALU.add
@@ -325,6 +349,9 @@ def tile_list_electrode_kinetics_transport_kernel(
                     else:
                         words, scales = (part[:, JC * g : JC * (g + 1)] for part in h_q[2 * first])
                     second_product(bank[:, width * (t - t0) : width * (t - t0 + 1)], t, g, words, scales)
+            if add_src is add_src_on_vector:
+                add_src_to_bank(b, t0, per_bank, bank)
+                return
             for t in range(t0, t0 + per_bank):
                 add_src(b, t, bank[:, width * (t - t0) : width * (t - t0 + 1)])
 
@@ -335,7 +362,7 @@ def tile_list_electrode_kinetics_transport_kernel(
                     quantise_y(0)
                     quantise_rates(UNITS - 1, 1)
                     quantise_y(1)
-                    store_words(0)
+                    store_words(0, HALF)
                 words, scales = h_q[UNITS - PASSES + g]
                 if g == PASSES - 1:
                     y_sb[LAST] = held("y_sb%d" % LAST, [P, PACK, JC], F32)
@@ -363,8 +390,9 @@ def tile_list_electrode_kinetics_transport_kernel(
                 y_w[half] = place("y_w%d" % half, [P, HALF], U32, AT_DIFF[12] + TILE * half)
             quantise(y_w[half][:, at : at + count * JC], y_s[:, first * JC : (first + count) * JC], y_bf[b][:])
 
-        def store_words(half):
-            nc.sync.dma_start(out=out_words[:, HALF * half : HALF * (half + 1)], in_=y_w[half][:].bitcast(I32))
+        def store_words(lo, hi):
+            half, at = divmod(lo, HALF)
+            nc.sync.dma_start(out=out_words[:, lo:hi], in_=y_w[half][:, at : at + hi - lo].bitcast(I32))
 
         def exponentials(n, first, end):
             for u in range(first, end):
@@ -428,12 +456,13 @@ def tile_list_electrode_kinetics_transport_kernel(
         store_y(LAST - 1)
         last_transport()
         round_y(2, nc.scalar.copy)
-        round_y(LAST, nc.vector.tensor_copy)
         round_y(LAST - 1, nc.vector.tensor_copy)
-        quantise_y(2)
-        quantise_y(LAST)
+        round_y(LAST, nc.vector.tensor_copy)
         quantise_y(LAST - 1)
-        store_words(1)
+        quantise_y(LAST)
+        store_words(S - 2 * JC, S)
+        quantise_y(2)
+        store_words(HALF, S - 2 * JC)
 
         for r in range(4):
             queue = nc.sync if r % 2 == 0 else nc.scalar

@@ -32,22 +32,21 @@ WE_PLANE = 4
 WIDE_UNITS = 12
 EARLY_C = 12
 EARLY_A = 6
-WA_LOADS = ((0, N // 2), (N // 2, N), (N, 2 * N))
+WA_LOADS = ((0, 128), (128, 352), (352, 656), (656, H))
 
 EDGE = 64
 TILE = 4 * UNIT
 PAIR = 2 * TILE
-AT_WA_BF0 = 0
-AT_E_SCALES = AT_WA_BF0 + PAIR
+AT_E_SCALES = EDGE
 AT_WORDS = AT_E_SCALES + S
 AT_WC_SCALES = AT_E_SCALES - EDGE
 AT_TAB = AT_WORDS + 4 * TILE
 AT_WA1 = AT_TAB + 4 * T
-AT_WA_BF1 = AT_WA1 + 2 * PAIR
-AT_WE = AT_WA_BF1 + PAIR
-AT_E_WORDS = AT_WA_BF1 + EDGE
+AT_WA_BF = AT_WA1 + 2 * PAIR
+AT_WE = AT_WA_BF + 2 * PAIR
+AT_E_WORDS = AT_WE - PAIR + EDGE
 AT_D0 = AT_WE + EDGE
-AT_A1 = AT_D0 + PAIR
+AT_A1 = AT_D0 + 2 * PAIR
 AT_WT0 = AT_A1 + PAIR
 AT_WT1 = AT_WT0 + 2 * PAIR
 AT_A5 = AT_WT1 + PAIR
@@ -69,10 +68,10 @@ AT_EXP = {
 AT_WT_BF = (AT_TAB, AT_TAB + PAIR)
 AT_H = (AT_TAB + 2 * PAIR, AT_H1, AT_EXP["c"][10], AT_C14 - TILE)
 AT_DIFF = {
-    0: AT_D0, 2: AT_A0, 4: AT_A1, 6: AT_A0 + EDGE, 8: AT_TAB + PAIR + TILE, 10: AT_A0 + EDGE, 12: AT_H1 - TILE,
-    14: AT_A0 + EDGE, 15: AT_Y0 - TILE // 2,
+    0: AT_D0, 4: AT_A1, 6: AT_D0 + PAIR, 8: AT_TAB + PAIR + TILE, 10: AT_D0 + PAIR, 12: AT_H1 - TILE,
+    14: AT_D0 + PAIR, 15: AT_Y0 - TILE // 2,
 }
-AT_WT_W = (AT_A0 + EDGE - TILE, AT_EXP["c"][6])
+AT_WT_W = (AT_D0, AT_EXP["c"][6])
 
 
 def unit_of(u):
@@ -109,7 +108,8 @@ def tile_list_electrode_kinetics_transport_kernel(
         wc_raw = held("wc_raw", [P, H // 2], I32)
         we_raw = place("we_raw", [P, H], I32, AT_WE)
         wa_raw = [held("wa_raw%d" % lo, [P, PACK, hi - lo], F32) for lo, hi in WA_LOADS[:-1]]
-        wa_raw.append(place("wa_raw_last", [P, PACK, N], F32, AT_WA1))
+        last = WA_LOADS[-1][1] - WA_LOADS[-1][0]
+        wa_raw.append(place("wa_raw_last", [P, PACK * N], F32, AT_WA1)[:, : PACK * last].rearrange("p (j r) -> p j r", j=PACK))
         wt_raw = [place("wt_raw0", [P, PACK * N], F32, AT_WT0), place("wt_raw1", [P, PACK * N + EDGE // 4], F32, AT_WT1)]
         src_sb = held("src_sb", [P, PACK], F32)
 
@@ -132,7 +132,7 @@ def tile_list_electrode_kinetics_transport_kernel(
         wa_rows = wa.rearrange("(p j) r -> p j r", j=PACK)
         for part, (lo, hi) in enumerate(WA_LOADS):
             nc.sync.dma_start(out=wa_raw[part][:], in_=wa_rows[:, :, lo:hi])
-            if hi == N:
+            if part == 1:
                 nc.sync.dma_start(lists["e"][:], offs3)
         load_scale_rows((nc.sync,), we_s_raw, we_scales, WE_PLANE)
         nc.sync.dma_start(out=we_raw[:], in_=we_words[0].rearrange("p y i -> p (y i)").bitcast(I32))
@@ -192,7 +192,8 @@ def tile_list_electrode_kinetics_transport_kernel(
             s = PACK * g + t
             cols = slice(P * s, P * (s + 1))
             if n == "a":
-                return wa_q[g][0][:, P * t : P * (t + 1)].bitcast(E4M3), wa_q[g][1][:, P * t : P * (t + 1)]
+                at = slice(P * (PASSES * (t % 2) + g), P * (PASSES * (t % 2) + g + 1))
+                return wa_q[t // 2][0][:, at].bitcast(E4M3), wa_q[t // 2][1][:, at]
             if n == "c":
                 return (
                     wc_w[:].bitcast(U8)[:, 2 * P * s : 2 * P * (s + 1)].bitcast(E2M1),
@@ -214,8 +215,11 @@ def tile_list_electrode_kinetics_transport_kernel(
 
         def wide_product(n, u, bank):
             jc, g = unit_of(u - u % 2)
+            half = u % 2
+            if u < STEP:
+                g, half = u % 2, u // 2
             for i in range(2):
-                codes, scales = weights(n, g, 2 * (u % 2) + i)
+                codes, scales = weights(n, g, 2 * half + i)
                 nc.tensor.matmul_mx(
                     out=bank[:, 2 * JC * i : 2 * JC * (i + 1)], lhsT=codes, lhsT_scale=scales,
                     rhs=v_w2[n, jc].bitcast(E4M3), rhs_scale=v_s[n][:, jc * JC : (jc + 2) * JC], start=True, stop=True,
@@ -247,6 +251,17 @@ def tile_list_electrode_kinetics_transport_kernel(
 
         def subtract(engine, first):
             width = ex["a", first].shape[1]
+            if first < STEP:
+                if first == 0:
+                    diff["step0"] = place("diff0", [P, PASSES, PACK, 2 * JC], F32, AT_DIFF[0])
+                    for u in range(STEP):
+                        diff[u] = diff["step0"][:, u // 2, :, JC * (u % 2) : JC * (u % 2 + 1)]
+                engine.tensor_tensor(
+                    out=diff["step0"][:, :, first : first + 2, :].rearrange("p g t j -> p g (t j)"),
+                    in0=ex["a", first].rearrange("p (g x) -> p g x", g=PASSES),
+                    in1=ex["c", first].rearrange("p (g x) -> p g x", g=PASSES), op=ALU.subtract,
+                )
+                return
             target = place("diff%d" % first, [P, width], F32, AT_DIFF[first])
             engine.tensor_tensor(out=target[:], in0=ex["a", first], in1=ex["c", first], op=ALU.subtract)
             for i in range(width // UNIT):
@@ -275,19 +290,19 @@ def tile_list_electrode_kinetics_transport_kernel(
                 cols = slice(JC * i, JC * min(i + 2, count))
                 h_q[first + i] = (words[:, cols], scales[:, cols])
 
-        wa_bf = [place("wa_bf%d" % g, [P, PACK * N], BF16, at) for g, at in enumerate((AT_WA_BF0, AT_WA_BF1))]
+        wa_bf = place("wa_bf", [P, PACK * H], BF16, AT_WA_BF)
 
         def round_wa(part):
             lo, hi = WA_LOADS[part]
-            g, qs = lo // N, slice(lo % N // 16, lo % N // 16 + (hi - lo) // 16)
+            qs = slice(lo // 16, hi // 16)
             nc.gpsimd.tensor_scalar(
-                out=wa_bf[g][:].rearrange("p (t q i j) -> p q t i j", t=PACK, i=4, j=PACK)[:, qs],
+                out=wa_bf[:].rearrange("p (t q i j) -> p q t i j", t=PACK, i=4, j=PACK)[:, qs],
                 in0=wa_raw[part][:].rearrange("p j (q t i) -> p q t i j", t=PACK, i=4),
                 scalar1=1.0, scalar2=0.0, op0=ALU.mult, op1=ALU.add,
             )
 
         def quantise_wa(g, words, scales):
-            quantise(words[:], scales[:], wa_bf[g][:])
+            quantise(words[:], scales[:], wa_bf[:, PACK * N * g : PACK * N * (g + 1)])
             wa_q[g] = (words, scales)
 
         wt_bf, wt_w = {}, {}

@@ -60,16 +60,17 @@ AT_C14 = AT_C6 + PAIR
 AT_A2 = AT_C14 + PAIR
 AT_A15 = AT_A2 + PAIR
 AT_A0 = AT_A15 + 2 * TILE
+AT_A1_HEAD = AT_A0 + PAIR
 AT_EXP = {
-    "a": {0: AT_A0, 2: AT_A1, 4: AT_A2, 6: AT_WT0, 8: AT_WT1, 10: AT_A5, 12: AT_A2, 14: AT_A14, 15: AT_A15},
+    "a": {0: AT_A0, 2: AT_A1_HEAD, 3: AT_A1, 4: AT_A2, 6: AT_WT0, 8: AT_WT1, 10: AT_A5, 12: AT_A2, 14: AT_A14, 15: AT_A15},
     "c": {0: AT_C0, 2: AT_C0 + PAIR, 4: AT_C0 + 2 * PAIR, 6: AT_C0 + 3 * PAIR, 8: AT_C4, 10: AT_C4 + PAIR, 12: AT_C6,
           14: AT_C14, 15: AT_C14 + TILE},
 }
 AT_WT_BF = (AT_TAB, AT_TAB + PAIR)
 AT_H = (AT_TAB + 2 * PAIR, AT_H1, AT_EXP["c"][10], AT_C14 - TILE)
 AT_DIFF = {
-    0: AT_D0, 4: AT_A1, 6: AT_D0 + PAIR, 8: AT_TAB + PAIR + TILE, 10: AT_D0 + PAIR, 12: AT_H1 - TILE,
-    14: AT_D0 + PAIR, 15: AT_Y0 - TILE // 2,
+    0: AT_D0, 4: AT_A1_HEAD, 6: AT_D0 + PAIR, 8: AT_TAB + PAIR + TILE, 10: AT_D0 + PAIR, 12: AT_A5,
+    14: AT_D0 + PAIR, 15: AT_A14,
 }
 AT_WT_W = (AT_D0, AT_EXP["c"][6])
 
@@ -236,7 +237,7 @@ def tile_list_electrode_kinetics_transport_kernel(
 
         def exponential(n, u):
             if u in AT_EXP[n]:
-                width = UNIT if u >= UNITS - 2 else 2 * UNIT
+                width = UNIT if u + 1 in AT_EXP[n] or u % 2 else 2 * UNIT
                 ex[n, u] = place("exp_%s%d" % (n, u), [P, width], F32, AT_EXP[n][u])[:]
             else:
                 ex[n, u] = ex[n, u - 1][:, UNIT:]
@@ -256,6 +257,13 @@ def tile_list_electrode_kinetics_transport_kernel(
                     diff["step0"] = place("diff0", [P, PASSES, PACK, 2 * JC], F32, AT_DIFF[0])
                     for u in range(STEP):
                         diff[u] = diff["step0"][:, u // 2, :, JC * (u % 2) : JC * (u % 2 + 1)]
+                if first == 2:
+                    for g in range(PASSES):
+                        engine.tensor_tensor(
+                            out=diff["step0"][:, g, 2:4, :].rearrange("p t j -> p (t j)"),
+                            in0=ex["a", 2 + g], in1=ex["c", 2 + g][:, :UNIT], op=ALU.subtract,
+                        )
+                    return
                 engine.tensor_tensor(
                     out=diff["step0"][:, :, first : first + 2, :].rearrange("p g t j -> p g (t j)"),
                     in0=ex["a", first].rearrange("p (g x) -> p g x", g=PASSES),

@@ -243,8 +243,6 @@ def tile_list_electrode_kinetics_transport_kernel(
                 ex[n, u] = ex[n, u - 1][:, UNIT:]
             if n == "a" and EARLY_A - STEP <= u < EARLY_A:
                 bank = e_banks[u - (EARLY_A - STEP)]
-            elif len(ex) <= EARLY_C:
-                bank = (exp_banks + [y_bank])[(len(ex) - 1) % 4]
             else:
                 bank = scalar_bank()
             product = wide_product if u < WIDE_UNITS else first_product
@@ -332,11 +330,11 @@ def tile_list_electrode_kinetics_transport_kernel(
         out_rows = out_0.rearrange("(p t) j -> p t j", t=PACK)
         out_words = out_1[0].rearrange("p m t -> p (m t)").bitcast(I32)
 
-        def second_product(out, t, g, words, scales):
+        def second_product(out, t, g, words, scales, start, stop):
             cols = slice(P * t, P * (t + 1))
             nc.tensor.matmul_mx(
                 out=out, lhsT=wt_w[g][:, cols].bitcast(E4M3), lhsT_scale=wt_s[g][:, cols],
-                rhs=words.bitcast(E4M3), rhs_scale=scales, start=(g == 0), stop=(g == PASSES - 1),
+                rhs=words.bitcast(E4M3), rhs_scale=scales, start=start, stop=stop,
             )
 
         def add_src_on_scalar(b, t, sums):
@@ -365,13 +363,16 @@ def tile_list_electrode_kinetics_transport_kernel(
             if b not in y_sb:
                 y_sb[b] = held("y_sb%d" % b, [P, PACK, width], F32)
             bank, t0 = (y_bank if half else scalar_bank()), half * per_bank
-            for t in range(t0, t0 + per_bank):
-                for g in range(PASSES):
+            for g in range(PASSES):
+                for t in range(t0, t0 + per_bank):
                     if count == 2:
                         words, scales = h_q[2 * (first + g)]
                     else:
                         words, scales = (part[:, JC * g : JC * (g + 1)] for part in h_q[2 * first])
-                    second_product(bank[:, width * (t - t0) : width * (t - t0 + 1)], t, g, words, scales)
+                    second_product(
+                        bank[:, width * (t - t0) : width * (t - t0 + 1)], t, g, words, scales,
+                        start=(g == 0 and t == t0), stop=(g == PASSES - 1 and t == t0 + per_bank - 1),
+                    )
             if add_src is add_src_on_vector:
                 add_src_to_bank(b, t0, per_bank, bank)
                 return
@@ -390,7 +391,7 @@ def tile_list_electrode_kinetics_transport_kernel(
                 if g == PASSES - 1:
                     y_sb[LAST] = held("y_sb%d" % LAST, [P, PACK, JC], F32)
                 for t in range(PACK):
-                    second_product(sums[t][:, :JC], t, g, words, scales)
+                    second_product(sums[t][:, :JC], t, g, words, scales, start=(g == 0), stop=(g == PASSES - 1))
                     if g == PASSES - 1:
                         add_src = add_src_on_scalar if t % 2 == 0 else add_src_on_vector
                         add_src(LAST, t, sums[t][:, :JC])
@@ -440,7 +441,9 @@ def tile_list_electrode_kinetics_transport_kernel(
         quantise_wa(1, held("wa_w1", [P, N], U32), place("wa_s1", [P, N], U8, AT_WA1 + 7 * H + N))
         we_q["s"] = deal(place("we_s", [P, H // 4], I32, AT_WA1 + 6 * H), we_s_raw.bitcast(I32))
         we_q["w"] = deal(place("we_w", [P, H], I32, AT_WA1), we_raw[:])
-        gather_words("e", 0, place("v_w_e", [P, S], U32, AT_E_WORDS)[:])
+        v_w_e = place("v_w_e", [P, S], U32, AT_E_WORDS)
+        gather_words("e", 0, v_w_e[:, : 2 * JC])
+        gather_words("e", 2, v_w_e[:, 2 * JC :])
         exponentials("a", 0, EARLY_A)
         subtract(nc.gpsimd, 0)
 

@@ -32,14 +32,15 @@ WE_PLANE = 4
 WIDE_UNITS = 12
 EARLY_C = 12
 EARLY_A = 6
-WA_LOADS = ((0, 128), (128, 352), (352, 656), (656, H))
+WA_LOADS = ((0, 128), (128, 320), (320, 640), (640, H))
 
 EDGE = 64
+ROW = 256
 TILE = 4 * UNIT
 PAIR = 2 * TILE
-AT_E_SCALES = EDGE
+AT_E_SCALES = 0
 AT_WORDS = AT_E_SCALES + S
-AT_WC_SCALES = AT_E_SCALES - EDGE
+AT_WC_SCALES = AT_E_SCALES
 AT_TAB = AT_WORDS + 4 * TILE
 AT_WA1 = AT_TAB + 4 * T
 AT_WA_BF = AT_WA1 + 2 * PAIR
@@ -47,7 +48,7 @@ AT_WE = AT_WA_BF + 2 * PAIR
 AT_E_WORDS = AT_WE - PAIR + EDGE
 AT_D0 = AT_WE + EDGE
 AT_A1 = AT_D0 + 2 * PAIR
-AT_WT0 = AT_A1 + PAIR
+AT_WT0 = AT_A1 + PAIR + ROW - EDGE
 AT_WT1 = AT_WT0 + 2 * PAIR
 AT_A5 = AT_WT1 + PAIR
 AT_H1 = AT_WT1 + 2 * PAIR
@@ -93,10 +94,10 @@ def tile_list_electrode_kinetics_transport_kernel(
         psum = ctx.enter_context(tc.psum_pool(name="psum", bufs=1))
 
         def held(name, shape, dtype):
-            return keep.tile(shape, dtype, name=name, align_bytes=64)
+            return keep.tile(shape, dtype, name=name, align_bytes=ROW)
 
         def place(name, shape, dtype, offset):
-            return placed.tile(shape, dtype, name=name, offset=offset, align_bytes=64)
+            return placed.tile(shape, dtype, name=name, offset=offset, align_bytes=EDGE if offset % ROW else ROW)
 
         banks = [psum.tile([P, BANK], F32, name="bank%d" % b) for b in range(8)]
         exp_banks, e_banks, y_bank = banks[0:3], banks[3:7], banks[7]
@@ -104,7 +105,7 @@ def tile_list_electrode_kinetics_transport_kernel(
         lists = {n: held("list_" + n, [P, S // 16], U16) for n in "ace"}
         tab_w = place("tab_w", [P, T], U32, AT_TAB)
         tab_s = held("tab_s", [P, T], U8)
-        wc_s_raw = place("wc_s_raw", [P, H + EDGE], U8, AT_WC_SCALES)[:, :H]
+        wc_s_raw = place("wc_s_raw", [P, H], U8, AT_WC_SCALES)[:]
         we_s_raw = held("we_s_raw", [P, H], U8)[:]
         wc_raw = held("wc_raw", [P, H // 2], I32)
         we_raw = place("we_raw", [P, H], I32, AT_WE)

@@ -34,7 +34,7 @@ EARLY_C = 12
 EARLY_A = 6
 WA_LOADS = ((0, 128), (128, 320), (320, 640), (640, H))
 
-EDGE = 64
+EDGE = 256
 ROW = 256
 TILE = 4 * UNIT
 PAIR = 2 * TILE
@@ -484,12 +484,12 @@ def tile_list_electrode_kinetics_transport_kernel(
         last_transport()
         round_y(2, nc.scalar.copy)
         round_y(LAST - 1, nc.vector.tensor_copy)
+        quantise_y(2)
+        store_words(HALF, S - 2 * JC)
         round_y(LAST, nc.vector.tensor_copy)
         quantise_y(LAST - 1)
         quantise_y(LAST)
         store_words(S - 2 * JC, S)
-        quantise_y(2)
-        store_words(HALF, S - 2 * JC)
 
         for r in range(4):
             queue = nc.sync if r % 2 == 0 else nc.scalar

@@ -389,14 +389,11 @@ def tile_list_electrode_kinetics_transport_kernel(
                     quantise_y(1)
                     store_words(0, HALF)
                 words, scales = h_q[UNITS - PASSES + g]
-                if g == PASSES - 1:
-                    y_sb[LAST] = held("y_sb%d" % LAST, [P, PACK, JC], F32)
                 for t in range(PACK):
                     second_product(sums[t][:, :JC], t, g, words, scales, start=(g == 0), stop=(g == PASSES - 1))
                     if g == PASSES - 1:
                         add_src = add_src_on_scalar if t % 2 == 0 else add_src_on_vector
                         add_src(LAST, t, sums[t][:, :JC])
-            store_y(LAST)
 
         def round_y(b, copy, at=None):
             name, shape = "y_bf%d" % b, [P, BATCHES[b][1] * UNIT]
@@ -479,9 +476,11 @@ def tile_list_electrode_kinetics_transport_kernel(
 
         quantise_rates(UNITS - STEP, STEP - 1)
         rates(UNITS - 1)
+        y_end = held("y_end", [P, PACK, 2 * JC], F32)
+        y_sb[LAST - 1], y_sb[LAST] = y_end[:, :, :JC], y_end[:, :, JC:]
         transport(LAST - 1, 0, add_src_on_scalar)
-        store_y(LAST - 1)
         last_transport()
+        nc.sync.dma_start(out=out_rows[:, :, S - 2 * JC :], in_=y_end[:])
         round_y(2, nc.scalar.copy)
         round_y(LAST - 1, nc.vector.tensor_copy)
         quantise_y(2)

from contextlib import ExitStack

import concourse.mybir as mybir

K, T, S, H, N = 512, 4096, 1024, 1024, 512
FLOPS = 2 * (3 * K * H * S + H * N * S)

F32 = mybir.dt.float32
BF16 = mybir.dt.bfloat16
I32 = mybir.dt.int32
U32 = mybir.dt.uint32
U16 = mybir.dt.uint16
U8 = mybir.dt.uint8
E4M3 = mybir.dt.float8_e4m3fn_x4
E2M1 = mybir.dt.float4_e2m1fn_x4
ACT = mybir.ActivationFunctionType
ALU = mybir.AluOpType

P = 128
PACK = 4
BANK = 512
JC = 128
CHUNKS = S // JC
HALF = S // 2
PASSES = H // (P * PACK)
UNIT = JC * PACK
UNITS = CHUNKS * PASSES
STEP = 4
BATCHES = ((0, 2), (2, 2), (4, 2), (6, 1), (7, 1))
LAST = len(BATCHES) - 1
WE_PLANE = 4
WIDE_UNITS = 12
EARLY_C = 12
EARLY_A = 6
WA_LOADS = ((0, 128), (128, 320), (320, 640), (640, H))

EDGE = 256
ROW = 256
TILE = 4 * UNIT
PAIR = 2 * TILE
AT_E_SCALES = 0
AT_WORDS = AT_E_SCALES + S
AT_WC_SCALES = AT_E_SCALES
AT_TAB = AT_WORDS + 4 * TILE
AT_WA1 = AT_TAB + 4 * T
AT_WA_BF = AT_WA1 + 2 * PAIR
AT_WE = AT_WA_BF + 2 * PAIR
AT_E_WORDS = AT_WE - PAIR + EDGE
AT_D0 = AT_WE + EDGE
AT_A1 = AT_D0 + 2 * PAIR
AT_WT0 = AT_A1 + PAIR + ROW - EDGE
AT_WT1 = AT_WT0 + 2 * PAIR
AT_A5 = AT_WT1 + PAIR
AT_H1 = AT_WT1 + 2 * PAIR
AT_C0 = AT_H1 + PAIR
AT_C4 = AT_C0 + 4 * PAIR
AT_Y0 = AT_C4 + 2 * PAIR
AT_A14 = AT_Y0 + TILE
AT_C6 = AT_A14 + TILE
AT_C14 = AT_C6 + PAIR
AT_A2 = AT_C14 + PAIR
AT_A15 = AT_A2 + PAIR
AT_A0 = AT_A15 + 2 * TILE
AT_A1_HEAD = AT_A0 + PAIR
AT_EXP = {
    "a": {0: AT_A0, 2: AT_A1_HEAD, 3: AT_A1, 4: AT_A2, 6: AT_WT0, 8: AT_WT1, 10: AT_A5, 12: AT_A2, 14: AT_A14, 15: AT_A15},
    "c": {0: AT_C0, 2: AT_C0 + PAIR, 4: AT_C0 + 2 * PAIR, 6: AT_C0 + 3 * PAIR, 8: AT_C4, 10: AT_C4 + PAIR, 12: AT_C6,
          14: AT_C14, 15: AT_C14 + TILE},
}
AT_WT_BF = (AT_TAB, AT_TAB + PAIR)
AT_H = (AT_TAB + 2 * PAIR, AT_H1, AT_EXP["c"][10], AT_C14 - TILE)
AT_DIFF = {
    0: AT_D0, 4: AT_A1_HEAD, 6: AT_D0 + PAIR, 8: AT_TAB + PAIR + TILE, 10: AT_D0 + PAIR, 12: AT_A5,
    14: AT_D0 + PAIR, 15: AT_A14,
}
AT_WT_W = (AT_D0, AT_EXP["c"][6])


def unit_of(u):
    pair, i = divmod(u, 2)
    if pair < BATCHES[LAST - 1][0]:
        return 2 * (pair // 2) + i, pair % 2
    return pair, i


def tile_list_electrode_kinetics_transport_kernel(
    tc, tab_words, tab_scales, offs, offs2, offs3, wa, wc_words, wc_scales, we_words, we_scales, wt, src,
    out_0, out_1, out_2,
):
    nc = tc.nc
    with ExitStack() as ctx:
        keep = ctx.enter_context(tc.tile_pool(name="keep", bufs=1))
        placed = ctx.enter_context(tc.tile_pool(name="placed", bufs=1))
        psum = ctx.enter_context(tc.psum_pool(name="psum", bufs=1))

        def held(name, shape, dtype):
            return keep.tile(shape, dtype, name=name, align_bytes=ROW)

        def place(name, shape, dtype, offset):
            return placed.tile(shape, dtype, name=name, offset=offset, align_bytes=EDGE if offset % ROW else ROW)

        banks = [psum.tile([P, BANK], F32, name="bank%d" % b) for b in range(8)]
        exp_banks, e_banks, y_bank = banks[0:3], banks[3:7], banks[7]

        lists = {n: held("list_" + n, [P, S // 16], U16) for n in "ace"}
        tab_w = place("tab_w", [P, T], U32, AT_TAB)
        tab_s = held("tab_s", [P, T], U8)
        wc_s_raw = place("wc_s_raw", [P, H], U8, AT_WC_SCALES)[:]
        we_s_raw = held("we_s_raw", [P, H], U8)[:]
        wc_raw = held("wc_raw", [P, H // 2], I32)
        we_raw = place("we_raw", [P, H], I32, AT_WE)
        wa_raw = [held("wa_raw%d" % lo, [P, PACK, hi - lo], F32) for lo, hi in WA_LOADS[:-1]]
        last = WA_LOADS[-1][1] - WA_LOADS[-1][0]
        wa_raw.append(place("wa_raw_last", [P, PACK * N], F32, AT_WA1)[:, : PACK * last].rearrange("p (j r) -> p j r", j=PACK))
        wt_raw = [place("wt_raw0", [P, PACK * N], F32, AT_WT0), place("wt_raw1", [P, PACK * N + EDGE // 4], F32, AT_WT1)]
        src_sb = held("src_sb", [P, PACK], F32)

        def load_scale_rows(queues, plane, rows, first=0):
            for r in range(4):
                queues[r % len(queues)].dma_start(
                    out=plane[first + r : P : 32, :].bitcast(I32), in_=rows[0, r:16:4, :].bitcast(I32)
                )

        nc.vector.memset(tab_s[:, : T // 2].bitcast(I32), 0)
        nc.gpsimd.memset(tab_s[:, T // 2 :].bitcast(I32), 0)
        for plane in (wc_s_raw, we_s_raw):
            nc.vector.memset(plane.bitcast(I32), 0)
        nc.sync.dma_start(lists["c"][:], offs2)
        load_scale_rows((nc.sync, nc.scalar), tab_s, tab_scales)
        nc.sync.dma_start(out=wc_raw[:], in_=wc_words[0].bitcast(I32))
        nc.sync.dma_start(lists["a"][:], offs)
        nc.sync.dma_start(out=tab_w[:].bitcast(I32), in_=tab_words[0].rearrange("p t i -> p (t i)").bitcast(I32))
        load_scale_rows((nc.sync,), wc_s_raw, wc_scales)
        wa_rows = wa.rearrange("(p j) r -> p j r", j=PACK)
        for part, (lo, hi) in enumerate(WA_LOADS):
            nc.sync.dma_start(out=wa_raw[part][:], in_=wa_rows[:, :, lo:hi])
            if part == 1:
                nc.sync.dma_start(lists["e"][:], offs3)
        load_scale_rows((nc.sync,), we_s_raw, we_scales, WE_PLANE)
        nc.sync.dma_start(out=we_raw[:], in_=we_words[0].rearrange("p y i -> p (y i)").bitcast(I32))
        wt_rows = wt.rearrange("(g q t i) n -> g i q t n", g=PASSES, t=PACK, i=4)
        for g in range(PASSES):
            for i in range(4):
                nc.sync.dma_start(out=wt_raw[g][i:P:4, : PACK * N].rearrange("q (t n) -> q t n", t=PACK), in_=wt_rows[g, i])
        nc.sync.dma_start(out=src_sb[:], in_=src.rearrange("(p t) -> p t", t=PACK))

        def quantise(words, scales, values):
            nc.vector.quantize_mx(out=words.bitcast(E4M3), scales=scales, in_=values)

        v_s, v_w, v_w2 = {}, {}, {}

        def gather_scales(n, tile):
            nc.vector.tensor_copy(tile[:], tab_s[:].indirect(lists[n][:]))
            v_s[n] = tile

        def gather_words(n, first, words):
            count, cols = words.shape[1] // JC, JC // 16
            nc.vector.tensor_copy(words, tab_w[:].indirect(lists[n][:, cols * first : cols * (first + count)]))
            for i in range(count):
                v_w[n, first + i] = words[:, JC * i : JC * (i + 1)]
                if i % 2 == 0:
                    v_w2[n, first + i] = words[:, JC * i : JC * (i + 2)]

        def deal_on_scalar(dealt, raw):
            words = raw.shape[1] // PASSES
            for g in range(PASSES):
                cols = slice(words * g, words * (g + 1))
                nc.scalar.copy(
                    out=dealt[:, cols].rearrange("p (t q w) -> p t q w", t=PACK, q=32),
                    in_=raw[:, cols].rearrange("p (q t w) -> p t q w", t=PACK, q=32),
                )
            return dealt

        def deal(dealt, raw):
            nc.vector.tensor_copy(
                out=dealt[:].rearrange("p (g t q w) -> p g t q w", g=PASSES, t=PACK, q=32),
                in_=raw.rearrange("p (g q t w) -> p g t q w", g=PASSES, t=PACK, q=32),
            )
            return dealt

        wc_w = deal_on_scalar(held("wc_w", [P, H // 2], U32), wc_raw[:].bitcast(U32))
        gather_scales("c", held("v_s_c", [P, S], U8))
        gather_scales("a", held("v_s_a", [P, S], U8))
        wc_s = deal_on_scalar(held("wc_s", [P, H // 4], U32), wc_s_raw.bitcast(U32))
        v_w_ca = place("v_w_ca", [P, 2 * S], U32, AT_WORDS)
        gather_words("c", 0, v_w_ca[:, : 2 * JC])
        gather_words("c", 2, v_w_ca[:, 2 * JC : S])
        gather_words("a", 0, v_w_ca[:, S:])
        gather_scales("e", place("v_s_e", [P, S], U8, AT_E_SCALES))

        wa_q, we_q = {}, {}

        def weights(n, g, t):
            s = PACK * g + t
            cols = slice(P * s, P * (s + 1))
            if n == "a":
                at = slice(P * (PASSES * (t % 2) + g), P * (PASSES * (t % 2) + g + 1))
                return wa_q[t // 2][0][:, at].bitcast(E4M3), wa_q[t // 2][1][:, at]
            if n == "c":
                return (
                    wc_w[:].bitcast(U8)[:, 2 * P * s : 2 * P * (s + 1)].bitcast(E2M1),
                    wc_s[:].bitcast(U8)[:, cols],
                )
            return we_q["w"][:, cols].bitcast(E4M3), we_q["s"][:].bitcast(U8)[WE_PLANE:, cols]

        def first_product(n, u, bank):
            jc, g = unit_of(u)
            for t in range(PACK):
                codes, scales = weights(n, g, t)
                nc.tensor.matmul_mx(
                    out=bank[:, JC * t : JC * (t + 1)], lhsT=codes, lhsT_scale=scales,
                    rhs=v_w[n, jc].bitcast(E4M3),
                    rhs_scale=v_s[n][:, jc * JC : (jc + 1) * JC],
                    start=True, stop=True,
                )
            return bank[:]

        def wide_product(n, u, bank):
            jc, g = unit_of(u - u % 2)
            half = u % 2
            if u < STEP:
                g, half = u % 2, u // 2
            for i in range(2):
                codes, scales = weights(n, g, 2 * half + i)
                nc.tensor.matmul_mx(
                    out=bank[:, 2 * JC * i : 2 * JC * (i + 1)], lhsT=codes, lhsT_scale=scales,
                    rhs=v_w2[n, jc].bitcast(E4M3), rhs_scale=v_s[n][:, jc * JC : (jc + 2) * JC], start=True, stop=True,
                )
            return bank[:]

        ex, diff, h_bf, h_q = {}, {}, {}, {}

        turns = []

        def scalar_bank():
            turns.append(len(turns))
            return exp_banks[turns[-1] % len(exp_banks)]

        def exponential(n, u):
            if u in AT_EXP[n]:
                width = UNIT if u + 1 in AT_EXP[n] or u % 2 else 2 * UNIT
                ex[n, u] = place("exp_%s%d" % (n, u), [P, width], F32, AT_EXP[n][u])[:]
            else:
                ex[n, u] = ex[n, u - 1][:, UNIT:]
            if n == "a" and EARLY_A - STEP <= u < EARLY_A:
                bank = e_banks[u - (EARLY_A - STEP)]
            else:
                bank = scalar_bank()
            product = wide_product if u < WIDE_UNITS else first_product
            nc.scalar.activation(out=ex[n, u][:, :UNIT], in_=product(n, u, bank), func=ACT.Exp)

        def subtract(engine, first):
            width = ex["a", first].shape[1]
            if first < STEP:
                if first == 0:
                    diff["step0"] = place("diff0", [P, PASSES, PACK, 2 * JC], F32, AT_DIFF[0])
                    for u in range(STEP):
                        diff[u] = diff["step0"][:, u // 2, :, JC * (u % 2) : JC * (u % 2 + 1)]
                if first == 2:
                    for g in range(PASSES):
                        engine.tensor_tensor(
                            out=diff["step0"][:, g, 2:4, :].rearrange("p t j -> p (t j)"),
                            in0=ex["a", 2 + g], in1=ex["c", 2 + g][:, :UNIT], op=ALU.subtract,
                        )
                    return
                engine.tensor_tensor(
                    out=diff["step0"][:, :, first : first + 2, :].rearrange("p g t j -> p g (t j)"),
                    in0=ex["a", first].rearrange("p (g x) -> p g x", g=PASSES),
                    in1=ex["c", first].rearrange("p (g x) -> p g x", g=PASSES), op=ALU.subtract,
                )
                return
            target = place("diff%d" % first, [P, width], F32, AT_DIFF[first])
            engine.tensor_tensor(out=target[:], in0=ex["a", first], in1=ex["c", first], op=ALU.subtract)
            for i in range(width // UNIT):
                if first < WIDE_UNITS:
                    diff[first + i] = target[:].rearrange("p (t j) -> p t j", t=PACK)[:, :, JC * i : JC * (i + 1)]
                else:
                    diff[first + i] = target[:, UNIT * i : UNIT * (i + 1)].rearrange("p (t j) -> p t j", t=PACK)

        def rates(u):
            m, i = divmod(u, STEP)
            if i == 0:
                h_bf[m] = place("h_bf%d" % m, [P, STEP * UNIT], BF16, AT_H[m])
            nc.vector.tensor_tensor(
                out=h_bf[m][:, UNIT * i : UNIT * (i + 1)].rearrange("p (c i t) -> p c t i", i=2, t=PACK),
                in0=diff[u].rearrange("p t (c i) -> p c t i", i=2),
                in1=first_product("e", u, e_banks[i]).rearrange("p (t c i) -> p c t i", i=2, t=PACK),
                op=ALU.mult,
            )

        def quantise_rates(first, count):
            words = held("h_w%d" % first, [P, count * JC], U32)
            scales = held("h_s%d" % first, [P, count * JC], U8)
            m, at = divmod(first, STEP)
            quantise(words[:], scales[:], h_bf[m][:, UNIT * at : UNIT * (at + count)])
            for i in range(0, count, 2):
                cols = slice(JC * i, JC * min(i + 2, count))
                h_q[first + i] = (words[:, cols], scales[:, cols])

        wa_bf = place("wa_bf", [P, PACK * H], BF16, AT_WA_BF)

        def round_wa(part):
            lo, hi = WA_LOADS[part]
            qs = slice(lo // 16, hi // 16)
            nc.gpsimd.tensor_scalar(
                out=wa_bf[:].rearrange("p (t q i j) -> p q t i j", t=PACK, i=4, j=PACK)[:, qs],
                in0=wa_raw[part][:].rearrange("p j (q t i) -> p q t i j", t=PACK, i=4),
                scalar1=1.0, scalar2=0.0, op0=ALU.mult, op1=ALU.add,
            )

        def quantise_wa(g, words, scales):
            quantise(words[:], scales[:], wa_bf[:, PACK * N * g : PACK * N * (g + 1)])
            wa_q[g] = (words, scales)

        wt_bf, wt_w = {}, {}
        wt_s = [held("wt_s%d" % g, [P, N], U8) for g in range(PASSES)]

        def round_wt_on_scalar(g):
            wt_bf[g] = place("wt_bf%d" % g, [P, PACK * N], BF16, AT_WT_BF[g])
            nc.scalar.copy(
                out=wt_bf[g][:].rearrange("p (t m j) -> p m j t", t=PACK, j=PACK),
                in_=wt_raw[g][:, : PACK * N].rearrange("p (j m t) -> p m j t", j=PACK, t=PACK),
            )

        def quantise_wt(g):
            wt_w[g] = place("wt_w%d" % g, [P, N], U32, AT_WT_W[g])
            quantise(wt_w[g][:], wt_s[g][:], wt_bf[g][:])

        y_sb, y_bf = {}, {}
        y_s = held("y_s", [P, S], U8)
        out_rows = out_0.rearrange("(p t) j -> p t j", t=PACK)
        out_words = out_1[0].rearrange("p m t -> p (m t)").bitcast(I32)

        def second_product(out, t, g, words, scales, start, stop):
            cols = slice(P * t, P * (t + 1))
            nc.tensor.matmul_mx(
                out=out, lhsT=wt_w[g][:, cols].bitcast(E4M3), lhsT_scale=wt_s[g][:, cols],
                rhs=words.bitcast(E4M3), rhs_scale=scales, start=start, stop=stop,
            )

        def add_src_on_scalar(b, t, sums):
            nc.scalar.activation(out=y_sb[b][:, t, :], in_=sums, func=ACT.Identity, bias=src_sb[:, t : t + 1])

        def add_src_to_bank(b, t0, count, bank):
            width = y_sb[b].shape[2]
            nc.vector.tensor_tensor(
                out=y_sb[b][:, t0 : t0 + count, :], in0=bank[:].rearrange("p (t j) -> p t j", t=count),
                in1=src_sb[:, t0 : t0 + count].unsqueeze(2).to_broadcast([P, count, width]), op=ALU.add,
            )

        def add_src_on_vector(b, t, sums):
            nc.vector.tensor_scalar(
                out=y_sb[b][:, t, :], in0=sums, scalar1=src_sb[:, t : t + 1], scalar2=None, op0=ALU.add
            )

        def store_y(b):
            first, count = BATCHES[b]
            nc.sync.dma_start(out=out_rows[:, :, first * JC : (first + count) * JC], in_=y_sb[b][:])

        def transport(b, half, add_src):
            first, count = BATCHES[b]
            width = count * JC
            per_bank = BANK // width
            if b not in y_sb:
                y_sb[b] = held("y_sb%d" % b, [P, PACK, width], F32)
            bank, t0 = (y_bank if half else scalar_bank()), half * per_bank
            for g in range(PASSES):
                for t in range(t0, t0 + per_bank):
                    if count == 2:
                        words, scales = h_q[2 * (first + g)]
                    else:
                        words, scales = (part[:, JC * g : JC * (g + 1)] for part in h_q[2 * first])
                    second_product(
                        bank[:, width * (t - t0) : width * (t - t0 + 1)], t, g, words, scales,
                        start=(g == 0 and t == t0), stop=(g == PASSES - 1 and t == t0 + per_bank - 1),
                    )
            if add_src is add_src_on_vector:
                add_src_to_bank(b, t0, per_bank, bank)
                return
            for t in range(t0, t0 + per_bank):
                add_src(b, t, bank[:, width * (t - t0) : width * (t - t0 + 1)])

        def last_transport():
            sums = e_banks
            for g in range(PASSES):
                if g == PASSES - 1:
                    quantise_y(0)
                    quantise_rates(UNITS - 1, 1)
                    quantise_y(1)
                    store_words(0, HALF)
                words, scales = h_q[UNITS - PASSES + g]
                for t in range(PACK):
                    second_product(sums[t][:, :JC], t, g, words, scales, start=(g == 0), stop=(g == PASSES - 1))
                    if g == PASSES - 1:
                        add_src = add_src_on_scalar if t % 2 == 0 else add_src_on_vector
                        add_src(LAST, t, sums[t][:, :JC])

        def round_y(b, copy, at=None):
            name, shape = "y_bf%d" % b, [P, BATCHES[b][1] * UNIT]
            y_bf[b] = held(name, shape, BF16) if at is None else place(name, shape, BF16, at)
            copy(
                out=y_bf[b][:].rearrange("p (c i t) -> p c t i", i=4, t=PACK),
                in_=y_sb[b][:].rearrange("p t (c i) -> p c t i", i=4),
            )

        y_w = {}

        def quantise_y(b):
            first, count = BATCHES[b]
            half, at = divmod(first * JC, HALF)
            if half not in y_w:
                y_w[half] = place("y_w%d" % half, [P, HALF], U32, AT_DIFF[12] + TILE * half)
            quantise(y_w[half][:, at : at + count * JC], y_s[:, first * JC : (first + count) * JC], y_bf[b][:])

        def store_words(lo, hi):
            half, at = divmod(lo, HALF)
            nc.sync.dma_start(out=out_words[:, lo:hi], in_=y_w[half][:, at : at + hi - lo].bitcast(I32))

        def exponentials(n, first, end):
            for u in range(first, end):
                exponential(n, u)

        def step(m):
            first = STEP * m
            subtract(nc.vector, first + 2)
            quantise_rates(first - STEP, STEP)
            if m == 1:
                quantise_wt(1)
            subtract(nc.gpsimd, min(first + STEP, UNITS - 1))
            for u in range(first, min(first + STEP, UNITS - 1)):
                rates(u)
            if m < 3:
                transport(m - 1, 1, add_src_on_vector)

        exponentials("c", 0, EARLY_C)
        for part in range(len(WA_LOADS)):
            round_wa(part)
        quantise_wa(0, place("wa_w0", [P, N], U32, AT_WA1 + 4 * H), place("wa_s0", [P, N], U8, AT_WA1 + 7 * H))
        quantise_wa(1, held("wa_w1", [P, N], U32), place("wa_s1", [P, N], U8, AT_WA1 + 7 * H + N))
        we_q["s"] = deal(place("we_s", [P, H // 4], I32, AT_WA1 + 6 * H), we_s_raw.bitcast(I32))
        we_q["w"] = deal(place("we_w", [P, H], I32, AT_WA1), we_raw[:])
        v_w_e = place("v_w_e", [P, S], U32, AT_E_WORDS)
        gather_words("e", 0, v_w_e[:, : 2 * JC])
        gather_words("e", 2, v_w_e[:, 2 * JC :])
        exponentials("a", 0, EARLY_A)
        subtract(nc.gpsimd, 0)

        subtract(nc.vector, 2)
        subtract(nc.gpsimd, STEP)
        round_wt_on_scalar(0)
        for u in range(STEP):
            rates(u)

        exponentials("a", EARLY_A, 8)
        round_wt_on_scalar(1)
        exponentials("a", 8, 12)
        exponentials("c", EARLY_C, 14)
        exponentials("a", 12, 14)
        quantise_wt(0)
        step(1)
        transport(0, 0, add_src_on_scalar)
        store_y(0)
        exponentials("c", 14, 15)
        exponentials("a", 14, 15)
        exponentials("c", 15, 16)
        exponentials("a", 15, 16)
        round_y(0, nc.scalar.copy)
        step(2)
        transport(1, 0, add_src_on_scalar)
        store_y(1)
        step(3)
        transport(2, 0, add_src_on_scalar)
        transport(2, 1, add_src_on_scalar)
        store_y(2)
        round_y(1, nc.scalar.copy)

        quantise_rates(UNITS - STEP, STEP - 1)
        rates(UNITS - 1)
        y_end = held("y_end", [P, PACK, 2 * JC], F32)
        y_sb[LAST - 1], y_sb[LAST] = y_end[:, :, :JC], y_end[:, :, JC:]
        transport(LAST - 1, 0, add_src_on_scalar)
        last_transport()
        nc.sync.dma_start(out=out_rows[:, :, S - 2 * JC :], in_=y_end[:])
        round_y(2, nc.scalar.copy)
        round_y(LAST - 1, nc.vector.tensor_copy)
        quantise_y(2)
        store_words(HALF, S - 2 * JC)
        round_y(LAST, nc.vector.tensor_copy)
        quantise_y(LAST - 1)
        quantise_y(LAST)
        store_words(S - 2 * JC, S)

        for r in range(4):
            queue = nc.sync if r % 2 == 0 else nc.scalar
            queue.dma_start(out=out_2[0, r:16:4, :].bitcast(I32), in_=y_s[r:P:32, :].bitcast(I32))
